import numpy as np
import ml_dtypes


def mxq(x, axis, fmt="e4m3"):
    dtype, down = {"e4m3": (ml_dtypes.float8_e4m3fn, 7), "e5m2": (ml_dtypes.float8_e5m2, 14)}[fmt]
    v = np.moveaxis(np.asarray(x, np.float32).astype(ml_dtypes.bfloat16).astype(np.float64), axis, -1)
    blocks = v.reshape(v.shape[:-1] + (-1, 32))
    amax = np.abs(blocks).max(-1, keepdims=True)
    byte = np.maximum(np.where(amax > 0, np.frexp(amax)[1] - 1 + 127, 0) - down, 1)
    scale = np.exp2(byte - 127.0)
    codes = (blocks / scale).astype(np.float32).astype(dtype).astype(np.float64)
    return np.moveaxis((codes * scale).reshape(v.shape), -1, axis)


WIDE = False


def mx_kscale(k):
    if not WIDE:
        return np.ones(k)
    levels = np.array([10, -10, 5, -5, 0])
    if k % 512:
        return np.exp2(np.random.permutation(np.resize(levels, k // 32))).repeat(32)
    a = np.empty((k // 512, 16))
    for p in range(k // 512):
        a[p, :8] = np.random.permutation(np.resize(levels, 8))
        for g in range(8):
            far = levels[np.abs(levels - a[p, g]) >= 10]
            a[p, g + 8] = far[np.random.randint(len(far))]
    return np.exp2(a.ravel()).repeat(32)


def f64(x):
    return np.asarray(x).astype(np.float64)


def striped(idx):
    return np.tile(idx.reshape(-1, 16).T, (8, 1)).astype(np.uint16)


def unstriped(offs):
    return offs[:16].T.reshape(-1).astype(np.int64)


E2M1 = np.array([0.0, 0.5, 1.0, 1.5, 2.0, 3.0, 4.0, 6.0, -0.0, -0.5, -1.0, -1.5, -2.0, -3.0, -4.0, -6.0])


def pack_weight(w, fmt):
    k, n = w.shape
    w = f64(np.asarray(w, np.float32).astype(ml_dtypes.bfloat16)).reshape(k // 32, 32, n)
    amax = np.abs(w).max(1)
    if fmt == "e4m3":
        byte = np.frexp(amax)[1] - 1 + 127 - 7
    else:
        mant, ex = np.frexp(amax / 6.0)
        byte = np.where(mant > 0.5, ex, ex - 1) + 127
    byte = np.clip(np.where(amax > 0, byte, 1), 1, 254)
    scaled = (w * np.exp2(127.0 - byte)[:, None, :]).reshape(k, n).astype(np.float32)
    by_word = np.ascontiguousarray(scaled.reshape(k // 512, 128, 4, n).transpose(0, 1, 3, 2))
    if fmt == "e4m3":
        words = by_word.astype(ml_dtypes.float8_e4m3fn).view(np.uint8)
    else:
        c = by_word.astype(ml_dtypes.float4_e2m1fn).view(np.uint8) & 0xF
        words = (c[..., 0::2] | (c[..., 1::2] << 4)).reshape(k // 512, 128, 2 * n)
    return np.ascontiguousarray(words), np.ascontiguousarray(byte.astype(np.uint8).reshape(k // 512, 16, n))


def unpack_weight(words, scales, fmt):
    g, _, n = scales.shape
    words = np.ascontiguousarray(words).reshape(g, 128, n, -1)
    if fmt == "e4m3":
        vals = words.view(ml_dtypes.float8_e4m3fn).astype(np.float64)
    else:
        nib = np.empty((g, 128, n, 4), np.uint8)
        nib[..., 0::2] = words & 0xF
        nib[..., 1::2] = words >> 4
        vals = E2M1[nib]
    vals = vals * np.repeat(np.exp2(scales.astype(np.float64) - 127.0), 8, axis=1)[..., None]
    return vals.transpose(0, 1, 3, 2).reshape(g * 512, n)


def gelu(v):
    return 0.5 * v * (1.0 + np.tanh(np.sqrt(2.0 / np.pi) * (v + 0.044715 * v**3)))


K, H, N, T, S, T2, P = 1024, 512, 512, 4096, 1024, 2048, 1024

def setup_inputs():
    n = np.random.standard_normal
    s = mx_kscale(K)[:, None]
    u = mx_kscale(H)[:, None]
    tab_words, tab_scales = pack_weight(n((K, T)) * s, "e4m3")
    w1_words, w1_scales = pack_weight(n((K, H)) / np.sqrt(K) / s * u.T, "e2m1")
    w3_words, w3_scales = pack_weight(n((H, N)) / np.sqrt(H) / u, "e4m3")
    return {
        "tab_words": tab_words, "tab_scales": tab_scales,
        "offs": striped(np.random.permutation(T)[:S]),
        "w1_words": w1_words, "w1_scales": w1_scales,
        "w2": (n((K, H)) / np.sqrt(K) / s).astype(np.float32),
        "wgs": np.exp(0.3 * n((128, S))).astype(np.float32),
        "page0": (n((H, T2)) * u).astype(np.float32),
        "offs2": striped(np.random.permutation(T2)[:S]),
        "offs3": striped(np.random.permutation(T2)[:P]),
        "offs4": striped(np.random.permutation(T2)[:P]),
        "w3_words": w3_words, "w3_scales": w3_scales,
        "w4": (n((H, N)) / np.sqrt(H) / u).astype(np.float32),
        "gain": np.exp(0.3 * n(N)).astype(np.float32),
    }

def reference(tab_words, tab_scales, offs, w1_words, w1_scales, w2, wgs, page0,
              offs2, offs3, offs4, w3_words, w3_scales, w4, gain):
    v = unpack_weight(tab_words, tab_scales, "e4m3")[:, unstriped(offs)]
    w1 = unpack_weight(w1_words, w1_scales, "e2m1")
    a = w1.T @ v
    b = mxq(f64(w2), 0, "e4m3").T @ v
    h = a * b
    page = f64(page0).copy()
    page[:, unstriped(offs2)] = np.tile(f64(wgs), (H // 128, 1)) * h
    x1 = page[:, unstriped(offs3)]
    x2 = page[:, unstriped(offs4)]
    d = mxq(x2 - x1, 0, "e4m3")
    w3 = unpack_weight(w3_words, w3_scales, "e4m3")
    y = w3.T @ d
    skip = mxq(f64(w4), 0, "e4m3").T @ d
    act = 0.5 * y * (1.0 + np.tanh(0.7978845608 * (y + 0.044715 * y ** 3)))
    return f64(gain)[:, None] * act + skip

@@ -1,0 +1,307 @@
+from contextlib import ExitStack
+
+import concourse.mybir as mybir
+from concourse.masks import make_identity
+
+K, H, N, T, S, T2, M = 1024, 512, 512, 4096, 1024, 2048, 1024
+FLOPS = 2 * 2 * K * H * S + 2 * 2 * H * N * M
+
+F32 = mybir.dt.float32
+BF16 = mybir.dt.bfloat16
+I32 = mybir.dt.int32
+U32 = mybir.dt.uint32
+U16 = mybir.dt.uint16
+U8 = mybir.dt.uint8
+FP8X4 = mybir.dt.float8_e4m3fn_x4
+FP4X4 = mybir.dt.float4_e2m1fn_x4
+MULT = mybir.AluOpType.mult
+ADD = mybir.AluOpType.add
+GELU = mybir.ActivationFunctionType.Gelu_apprx_tanh
+
+P = 128
+HALF = 512
+TILES = 4
+
+
+def tile_list_regression_bisect_features_kernel(
+    tc, tab_words, tab_scales, offs, w1_words, w1_scales, w2, wgs, page0,
+    offs2, offs3, offs4, w3_words, w3_scales, w4, gain, out,
+):
+    nc = tc.nc
+    with ExitStack() as ctx:
+        keep = ctx.enter_context(tc.tile_pool(name="keep", bufs=1))
+        ring = ctx.enter_context(tc.tile_pool(name="ring", bufs=2))
+        psum = ctx.enter_context(tc.psum_pool(name="psum", bufs=1))
+
+        def sb(name, shape, dtype):
+            return keep.tile(shape, dtype, name=name, align_bytes=64)
+
+        banks = [psum.tile([P, HALF], F32, name="bank%d" % i) for i in range(8)]
+
+        idx1 = keep.tile([P, S // 16], U16, name="idx1")
+        idx2 = keep.tile([P, S // 16], U16, name="idx2")
+        idx3 = keep.tile([P, M // 16], U16, name="idx3")
+        idx4 = keep.tile([P, M // 16], U16, name="idx4")
+        tab_w = [sb("tab_w%d" % a, [P, T], U32) for a in range(2)]
+        tab_s = sb("tab_s", [P, 2 * T], U8)
+        v_w = [sb("v_w%d" % a, [P, S], U32) for a in range(2)]
+        v_s = [sb("v_s%d" % a, [P, S], U8) for a in range(2)]
+        w1_w = sb("w1_w", [P, 2 * 2 * H], U8)
+        w1_s = sb("w1_s", [P, 2 * H], U8)
+        w3_w = sb("w3_w", [P, N], U32)
+        w3_s = sb("w3_s", [P, N], U8)
+        w2_first = [sb("w2_first%d" % a, [P, 4, P], F32) for a in range(2)]
+        w2_rest = [sb("w2_rest%d" % a, [P, 4, 3 * P], F32) for a in range(2)]
+        w2_w = [sb("w2_w%d" % t, [P, 2 * P], U32) for t in range(TILES)]
+        w2_s = [sb("w2_s%d" % t, [P, 2 * P], U8) for t in range(TILES)]
+        w4_raw = sb("w4_raw", [P, 4, N], F32)
+        w4_bf = sb("w4_bf", [P, 4 * N], BF16)
+        w4_w = sb("w4_w", [P, N], U32)
+        w4_s = sb("w4_s", [P, N], U8)
+        wgs_sb = [sb("wgs_sb%d" % h, [P, HALF], F32) for h in range(2)]
+        gain_sb = sb("gain_sb", [P, TILES], F32)
+        page = [sb("page%d" % t, [P, T2], F32) for t in range(TILES)]
+        ident = sb("ident", [P, P], F32)
+
+        nc.vector.memset(tab_s[:, 0 : 5 * 1024].bitcast(I32), 0)
+        nc.gpsimd.memset(tab_s[:, 5 * 1024 : 2 * T].bitcast(I32), 0)
+        nc.vector.memset(w1_s[:].bitcast(I32), 0)
+        nc.vector.memset(w3_s[:].bitcast(I32), 0)
+        make_identity(nc, ident[:])
+
+        nc.sync.dma_start(idx1[:], offs)
+        for q in range(4):
+            nc.sync.dma_start(
+                tab_s[32 * q : 32 * q + 4, :].bitcast(I32).rearrange("r (a c) -> r a c", a=2),
+                tab_scales[:, 4 * q : 4 * q + 4, :].bitcast(I32).rearrange("a r c -> r a c"),
+            )
+        nc.sync.dma_start(tab_w[0][:].bitcast(I32), tab_words[0].rearrange("p t i -> p (t i)").bitcast(I32))
+        w2_rows = w2.rearrange("(a p j) c -> a p j c", a=2, j=4)
+        for a in range(2):
+            nc.sync.dma_start(w2_first[a][:], w2_rows[a, :, :, 0:P])
+        nc.sync.dma_start(
+            w1_w[:].bitcast(I32).rearrange("p (a c) -> p a c", a=2),
+            w1_words.bitcast(I32).rearrange("a p c -> p a c"),
+        )
+        for q in range(4):
+            nc.sync.dma_start(
+                w1_s[32 * q : 32 * q + 4, :].bitcast(I32).rearrange("r (a c) -> r a c", a=2),
+                w1_scales[:, 4 * q : 4 * q + 4, :].bitcast(I32).rearrange("a r c -> r a c"),
+            )
+        nc.sync.dma_start(tab_w[1][:].bitcast(I32), tab_words[1].rearrange("p t i -> p (t i)").bitcast(I32))
+        nc.sync.dma_start(wgs_sb[0][:], wgs[:, 0:HALF])
+        nc.sync.dma_start(idx2[:], offs2)
+        nc.sync.dma_start(page[0][:], page0[0:P, :])
+        nc.sync.dma_start(wgs_sb[1][:], wgs[:, HALF:S])
+        for a in range(2):
+            nc.sync.dma_start(w2_rest[a][:], w2_rows[a, :, :, P:H])
+        nc.sync.dma_start(idx3[:], offs3)
+        nc.sync.dma_start(idx4[:], offs4)
+        for t in range(1, TILES - 1):
+            nc.sync.dma_start(page[t][:], page0[P * t : P * (t + 1), :])
+        nc.sync.dma_start(w4_raw[:], w4.rearrange("(p j) n -> p j n", j=4))
+        nc.sync.dma_start(w3_w[:].bitcast(I32), w3_words[0].rearrange("p n i -> p (n i)").bitcast(I32))
+        for q in range(4):
+            nc.sync.dma_start(
+                w3_s[32 * q : 32 * q + 4, :].bitcast(I32),
+                w3_scales[0, 4 * q : 4 * q + 4, :].bitcast(I32),
+            )
+        with nc.allow_non_contiguous_dma(reason="one gain value to each partition"):
+            nc.sync.dma_start(gain_sb[:], gain.rearrange("(c p) -> p c", p=P))
+        nc.sync.dma_start(page[TILES - 1][:], page0[P * (TILES - 1) : P * TILES, :])
+
+        def interleave(dst, src):
+            nc.scalar.copy(
+                dst.rearrange("p (c i j) -> p c j i", i=4, j=4),
+                src.rearrange("p j (c i) -> p c j i", i=4),
+            )
+
+        def quantise_w2(t, stage):
+            for a in range(2):
+                src = w2_first[a][:] if t == 0 else w2_rest[a][:, :, P * (t - 1) : P * t]
+                interleave(stage[:, HALF * a : HALF * (a + 1)], src)
+            nc.vector.quantize_mx(out=w2_w[t][:].bitcast(FP8X4), scales=w2_s[t][:], in_=stage)
+
+        for a in range(2):
+            nc.vector.tensor_copy(v_s[a][:], tab_s[:, T * a : T * (a + 1)].indirect(idx1[:]))
+        nc.vector.tensor_copy(v_w[0][:], tab_w[0][:].indirect(idx1[:]))
+        stage0 = sb("stage0", [P, 2 * HALF], BF16)
+        quantise_w2(0, stage0[:])
+        for h in range(2):
+            nc.vector.tensor_copy(v_w[1][:, HALF * h : HALF * (h + 1)], tab_w[1][:].indirect(idx1[:, 32 * h : 32 * (h + 1)]))
+
+        def first_products(t):
+            a_sb = ring.tile([P, S], F32, name="a_sb")
+            bw_sb = ring.tile([P, S], F32, name="bw_sb")
+            for h in range(2):
+                cols = slice(HALF * h, HALF * (h + 1))
+                a_bank, b_bank = banks[2 * h], banks[2 * h + 1]
+                for a in range(2):
+                    nc.tensor.matmul_mx(
+                        out=b_bank[:],
+                        lhsT=w2_w[t][:, P * a : P * (a + 1)].bitcast(FP8X4),
+                        lhsT_scale=w2_s[t][:, P * a : P * (a + 1)],
+                        rhs=v_w[a][:, cols].bitcast(FP8X4),
+                        rhs_scale=v_s[a][:, cols],
+                        start=(a == 0), stop=(a == 1),
+                    )
+                for a in range(2):
+                    c0 = H * a + P * t
+                    nc.tensor.matmul_mx(
+                        out=a_bank[:],
+                        lhsT=w1_w[:, 2 * c0 : 2 * (c0 + P)].bitcast(FP4X4),
+                        lhsT_scale=w1_s[:, c0 : c0 + P],
+                        rhs=v_w[a][:, cols].bitcast(FP8X4),
+                        rhs_scale=v_s[a][:, cols],
+                        start=(a == 0), stop=(a == 1),
+                    )
+                nc.scalar.copy(a_sb[:, cols], a_bank[:])
+                nc.vector.tensor_tensor(bw_sb[:, cols], b_bank[:], wgs_sb[h][:], MULT)
+            return a_sb, bw_sb
+
+        def gather_negated(dst, t, m0):
+            nc.vector.tensor_scalar(dst, page[t][:].indirect(idx3[:, m0 // 16 : (m0 + HALF) // 16]), -1.0, 0.0, MULT, ADD)
+
+        def turn(bank, parts, width, d_rows, t):
+            blocks = width // P
+            for i, part in enumerate(parts):
+                for b in range(blocks):
+                    nc.tensor.matmul(
+                        bank[:, P * b : P * (b + 1)], part[:, P * b : P * (b + 1)], ident[:],
+                        start=(i == 0 and b == 0), stop=(i == len(parts) - 1 and b == blocks - 1), is_transpose=True,
+                    )
+            nc.scalar.copy(
+                d_rows[:].rearrange("p b (u t j e) -> p t b u j e", u=2, t=TILES, e=2)[:, t],
+                bank[:, 0:width].rearrange("p (b j u e) -> p b u j e", j=32, u=2, e=2),
+            )
+
+        def turn_back(bank, d_rows, b0, blocks, dst):
+            for b in range(blocks):
+                words = d_rows[:, b0 + b, :].bitcast(F32)
+                for u in range(2):
+                    c0 = P * (2 * b + u)
+                    nc.tensor.transpose(bank[:, c0 : c0 + P], words[:, P * u : P * (u + 1)], ident[:])
+            nc.scalar.copy(
+                dst.rearrange("p (b m u) -> p b m u", u=2, m=P),
+                bank[:, 0 : 2 * P * blocks].rearrange("p (b u m) -> p b m u", u=2, m=P),
+            )
+
+        d_rows_a = sb("d_rows_a", [P, 4, H], BF16)
+        d_rows_b = sb("d_rows_b", [P, 2, H], BF16)
+        d_rows_c = sb("d_rows_c", [P, 1, H], BF16)
+        d_rows_d = sb("d_rows_d", [P, 1, H], BF16)
+        shared0 = sb("shared0", [P, 2 * HALF], F32)
+
+        a_sb, bw_sb = first_products(0)
+        for h in range(2):
+            cols = slice(HALF * h, HALF * (h + 1))
+            nc.vector.tensor_tensor(page[0][:].indirect(idx2[:, 32 * h : 32 * (h + 1)]), a_sb[:, cols], bw_sb[:, cols], MULT)
+        quantise_w2(1, shared0[:, 256:768].bitcast(BF16))
+        for t in range(TILES):
+            if t == 0:
+                x1, x2 = shared0[:, 0:HALF], shared0[:, HALF : 2 * HALF]
+            else:
+                nc.vector.tensor_tensor(page[t][:].indirect(idx2[:]), a_sb[:], bw_sb[:], MULT)
+                x12 = ring.tile([P, 2 * HALF], F32, name="x12")
+                x1, x2 = x12[:, 0:HALF], x12[:, HALF : 2 * HALF]
+            last_a, last_bw = a_sb, bw_sb
+            if 0 < t < TILES - 1:
+                a_sb, bw_sb = first_products(t + 1)
+            gather_negated(x1, t, 0)
+            nc.vector.tensor_copy(x2, page[t][:].indirect(idx4[:, 0:32]))
+            if t == 0:
+                a_sb, bw_sb = first_products(t + 1)
+            if t + 2 < TILES:
+                stage = ring.tile([P, 2 * HALF], BF16, name="stage", align_bytes=64)
+                quantise_w2(t + 2, stage[:])
+            turn(banks[4 + t % 2], [x1, x2], HALF, d_rows_a, t)
+            if t == 2:
+                interleave(w4_bf[:], w4_raw[:])
+                nc.vector.quantize_mx(out=w4_w[:].bitcast(FP8X4), scales=w4_s[:], in_=w4_bf[:])
+
+        arena = sb("arena", [P, 2 * HALF], F32)
+        d_w = sb("d_w", [P, M], U32)
+        d_s = sb("d_s", [P, M], U8)
+        for h in range(2):
+            turn_back(banks[6 + h], d_rows_a, 2 * h, 2, arena[:, HALF * h : HALF * (h + 1)])
+
+        x1_late = [last_a[:, 0:HALF], last_a[:, HALF:S], last_bw[:, 0:HALF], last_bw[:, HALF:S]]
+        for t in range(TILES):
+            gather_negated(x1_late[t], t, HALF)
+
+        def quantise_d(m0, width, src):
+            nc.vector.quantize_mx(out=d_w[:, m0 : m0 + width].bitcast(FP8X4), scales=d_s[:, m0 : m0 + width], in_=src.bitcast(BF16))
+
+        def second_product(dst, w_w, w_s, c, m0, width):
+            nc.tensor.matmul_mx(
+                out=dst,
+                lhsT=w_w[:, P * c : P * (c + 1)].bitcast(FP8X4),
+                lhsT_scale=w_s[:, P * c : P * (c + 1)],
+                rhs=d_w[:, m0 : m0 + width].bitcast(FP8X4),
+                rhs_scale=d_s[:, m0 : m0 + width],
+                start=True, stop=True,
+            )
+
+        out_tiles = out.rearrange("(c p) m -> p c m", p=P)
+
+        quantise_d(0, HALF, arena[:])
+        act_a = [sb("act_a%d" % c, [P, HALF], F32) for c in range(TILES)]
+        out_a = [sb("out_a%d" % c, [P, HALF], F32)[:] for c in range(2)] + [x1_late[1], x1_late[2]]
+        for c in range(TILES):
+            second_product(banks[6 + c % 2][:], w3_w, w3_s, c, 0, HALF)
+            second_product(banks[c][:], w4_w, w4_s, c, 0, HALF)
+            nc.scalar.activation(act_a[c][:], banks[6 + c % 2][:], GELU)
+
+        def finish_a(c):
+            nc.vector.scalar_tensor_tensor(out_a[c], act_a[c][:], gain_sb[:, c : c + 1], banks[c][:], MULT, ADD)
+            nc.sync.dma_start(out_tiles[:, c, 0:HALF], out_a[c])
+
+        def products(c0, count, m0, width, y_bank, skip_bank, act):
+            for i in range(count):
+                second_product(y_bank[:, width * i : width * (i + 1)], w3_w, w3_s, c0 + i, m0, width)
+            for i in range(count):
+                second_product(skip_bank[:, width * i : width * (i + 1)], w4_w, w4_s, c0 + i, m0, width)
+            nc.scalar.activation(act[:], y_bank[:], GELU)
+
+        def finish(c0, count, m0, width, skip_bank, act, res):
+            for i in range(count):
+                cols = slice(width * i, width * (i + 1))
+                nc.vector.scalar_tensor_tensor(res[:, cols], act[:, cols], gain_sb[:, c0 + i : c0 + i + 1], skip_bank[:, cols], MULT, ADD)
+            nc.sync.dma_start(out_tiles[:, c0 : c0 + count, m0 : m0 + width], res[:].rearrange("p (i m) -> p i m", m=width))
+
+        d_in_b = sb("d_in_b", [P, HALF], F32)
+        d_in_c = sb("d_in_c", [P, 256], F32)
+        d_in_d = sb("d_in_d", [P, 256], F32)
+        act_late = [sb("act_late%d" % i, [P, HALF], F32) for i in range(4)]
+        out_late = [sb("out_late%d" % i, [P, HALF], F32) for i in range(4)]
+
+        for t in range(TILES):
+            x2 = arena[:, 256 * t : 256 * (t + 1)]
+            nc.vector.tensor_copy(x2, page[t][:].indirect(idx4[:, 32:48]))
+            turn(banks[4 + t % 2], [x1_late[t][:, 0:256], x2], 256, d_rows_b, t)
+        turn_back(banks[6], d_rows_b, 0, 2, d_in_b[:])
+        finish_a(0)
+        for t in range(TILES):
+            diff = act_a[0][:, P * t : P * (t + 1)]
+            nc.vector.tensor_tensor(diff, page[t][:].indirect(idx4[:, 48:56]), x1_late[t][:, 256:384], ADD)
+            turn(banks[4 + t % 2], [diff], P, d_rows_c, t)
+        turn_back(banks[7], d_rows_c, 0, 1, d_in_c[:])
+        finish_a(1)
+        quantise_d(HALF, 256, d_in_b[:])
+        products(0, 2, HALF, 256, banks[0], banks[1], act_late[0])
+        for t in range(TILES):
+            diff = d_in_b[:, P * t : P * (t + 1)]
+            nc.vector.tensor_tensor(diff, page[t][:].indirect(idx4[:, 56:64]), x1_late[t][:, 384:512], ADD)
+            turn(banks[4 + t % 2], [diff], P, d_rows_d, t)
+        turn_back(banks[7], d_rows_d, 0, 1, d_in_d[:])
+        quantise_d(768, P, d_in_c[:])
+        finish_a(2)
+        finish_a(3)
+        quantise_d(896, P, d_in_d[:])
+        products(2, 2, HALF, 256, banks[6], banks[2], act_late[1])
+        products(0, 4, 768, P, banks[4], banks[3], act_late[2])
+        products(0, 4, 896, P, banks[5], banks[7], act_late[3])
+        finish(0, 2, HALF, 256, banks[1], act_late[0], out_late[0])
+        finish(2, 2, HALF, 256, banks[2], act_late[1], out_late[1])
+        finish(0, 4, 768, P, banks[3], act_late[2], out_late[2])
+        finish(0, 4, 896, P, banks[7], act_late[3], out_late[3])

@@ -46,59 +46,62 @@ def tile_list_regression_bisect_features_kernel(
         tab_s = sb("tab_s", [P, 2 * T], U8)
         v_w = [sb("v_w%d" % a, [P, S], U32) for a in range(2)]
         v_s = [sb("v_s%d" % a, [P, S], U8) for a in range(2)]
-        w1_w = sb("w1_w", [P, 2 * 2 * H], U8)
+        w1_first = sb("w1_first", [P, 2 * 2 * P], U8)
+        w1_rest = sb("w1_rest", [P, 2 * 6 * P], U8)
         w1_s = sb("w1_s", [P, 2 * H], U8)
         w3_w = sb("w3_w", [P, N], U32)
         w3_s = sb("w3_s", [P, N], U8)
         w2_first = [sb("w2_first%d" % a, [P, 4, P], F32) for a in range(2)]
-        w2_rest = [sb("w2_rest%d" % a, [P, 4, 3 * P], F32) for a in range(2)]
+        w2_second = [sb("w2_second%d" % a, [P, 4, P], F32) for a in range(2)]
+        w2_rest = [sb("w2_rest%d" % a, [P, 4, 2 * P], F32) for a in range(2)]
         w2_w = [sb("w2_w%d" % t, [P, 2 * P], U32) for t in range(TILES)]
         w2_s = [sb("w2_s%d" % t, [P, 2 * P], U8) for t in range(TILES)]
         w4_raw = sb("w4_raw", [P, 4, N], F32)
         w4_bf = sb("w4_bf", [P, 4 * N], BF16)
         w4_w = sb("w4_w", [P, N], U32)
         w4_s = sb("w4_s", [P, N], U8)
-        wgs_sb = [sb("wgs_sb%d" % h, [P, HALF], F32) for h in range(2)]
+        wgs_sb = sb("wgs_sb", [P, S], F32)
         gain_sb = sb("gain_sb", [P, TILES], F32)
         page = [sb("page%d" % t, [P, T2], F32) for t in range(TILES)]
         ident = sb("ident", [P, P], F32)
 
-        nc.vector.memset(tab_s[:, 0 : 5 * 1024].bitcast(I32), 0)
-        nc.gpsimd.memset(tab_s[:, 5 * 1024 : 2 * T].bitcast(I32), 0)
+        nc.vector.memset(tab_s[:, 0 : 4352].bitcast(I32), 0)
+        nc.gpsimd.memset(tab_s[:, 4352 : 2 * T].bitcast(I32), 0)
         nc.vector.memset(w1_s[:].bitcast(I32), 0)
         nc.vector.memset(w3_s[:].bitcast(I32), 0)
         make_identity(nc, ident[:])
 
-        nc.sync.dma_start(idx1[:], offs)
+        for idx, src in ((idx1, offs), (idx2, offs2), (idx3, offs3), (idx4, offs4)):
+            nc.sync.dma_start(idx[:], src)
         for q in range(4):
             nc.sync.dma_start(
                 tab_s[32 * q : 32 * q + 4, :].bitcast(I32).rearrange("r (a c) -> r a c", a=2),
                 tab_scales[:, 4 * q : 4 * q + 4, :].bitcast(I32).rearrange("a r c -> r a c"),
             )
-        nc.sync.dma_start(tab_w[0][:].bitcast(I32), tab_words[0].rearrange("p t i -> p (t i)").bitcast(I32))
         w2_rows = w2.rearrange("(a p j) c -> a p j c", a=2, j=4)
+        w1_rows = w1_words.bitcast(I32).rearrange("a p c -> p a c")
+        tab_rows = [tab_words[a].rearrange("p t i -> p (t i)").bitcast(I32) for a in range(2)]
+        nc.sync.dma_start(tab_w[0][:, 0 : T // 2].bitcast(I32), tab_rows[0][:, 0 : T // 2])
         for a in range(2):
             nc.sync.dma_start(w2_first[a][:], w2_rows[a, :, :, 0:P])
-        nc.sync.dma_start(
-            w1_w[:].bitcast(I32).rearrange("p (a c) -> p a c", a=2),
-            w1_words.bitcast(I32).rearrange("a p c -> p a c"),
-        )
+        nc.sync.dma_start(tab_w[0][:, T // 2 : T].bitcast(I32), tab_rows[0][:, T // 2 : T])
+        nc.sync.dma_start(w1_first[:].bitcast(I32).rearrange("p (a c) -> p a c", a=2), w1_rows[:, :, 0 : P // 2])
         for q in range(4):
             nc.sync.dma_start(
                 w1_s[32 * q : 32 * q + 4, :].bitcast(I32).rearrange("r (a c) -> r a c", a=2),
                 w1_scales[:, 4 * q : 4 * q + 4, :].bitcast(I32).rearrange("a r c -> r a c"),
             )
-        nc.sync.dma_start(tab_w[1][:].bitcast(I32), tab_words[1].rearrange("p t i -> p (t i)").bitcast(I32))
-        nc.sync.dma_start(wgs_sb[0][:], wgs[:, 0:HALF])
-        nc.sync.dma_start(idx2[:], offs2)
+        nc.sync.dma_start(tab_w[1][:].bitcast(I32), tab_rows[1])
+        nc.sync.dma_start(wgs_sb[:, 0:HALF], wgs[:, 0:HALF])
         nc.sync.dma_start(page[0][:], page0[0:P, :])
-        nc.sync.dma_start(wgs_sb[1][:], wgs[:, HALF:S])
+        nc.sync.dma_start(wgs_sb[:, HALF:S], wgs[:, HALF:S])
         for a in range(2):
-            nc.sync.dma_start(w2_rest[a][:], w2_rows[a, :, :, P:H])
-        nc.sync.dma_start(idx3[:], offs3)
-        nc.sync.dma_start(idx4[:], offs4)
-        for t in range(1, TILES - 1):
-            nc.sync.dma_start(page[t][:], page0[P * t : P * (t + 1), :])
+            nc.sync.dma_start(w2_second[a][:], w2_rows[a, :, :, P : 2 * P])
+        nc.sync.dma_start(w1_rest[:].bitcast(I32).rearrange("p (a c) -> p a c", a=2), w1_rows[:, :, P // 2 : 2 * P])
+        for a in range(2):
+            nc.sync.dma_start(w2_rest[a][:], w2_rows[a, :, :, 2 * P : H])
+        nc.sync.dma_start(page[1][:], page0[P : 2 * P, :])
+        nc.sync.dma_start(page[2][:], page0[2 * P : 3 * P, :])
         nc.sync.dma_start(w4_raw[:], w4.rearrange("(p j) n -> p j n", j=4))
         nc.sync.dma_start(w3_w[:].bitcast(I32), w3_words[0].rearrange("p n i -> p (n i)").bitcast(I32))
         for q in range(4):
@@ -112,51 +115,60 @@ def tile_list_regression_bisect_features_kernel(
 
         def interleave(dst, src):
             nc.scalar.copy(
-                dst.rearrange("p (c i j) -> p c j i", i=4, j=4),
-                src.rearrange("p j (c i) -> p c j i", i=4),
+                dst.rearrange("p (c j) -> p c j", j=4),
+                src.rearrange("p j c -> p c j"),
             )
 
         def quantise_w2(t, stage):
             for a in range(2):
-                src = w2_first[a][:] if t == 0 else w2_rest[a][:, :, P * (t - 1) : P * t]
+                src = [w2_first[a][:], w2_second[a][:], w2_rest[a][:, :, 0:P], w2_rest[a][:, :, P : 2 * P]][t]
                 interleave(stage[:, HALF * a : HALF * (a + 1)], src)
             nc.vector.quantize_mx(out=w2_w[t][:].bitcast(FP8X4), scales=w2_s[t][:], in_=stage)
 
+        stage0 = sb("stage0", [P, 2 * HALF], BF16)
+        quantise_w2(0, stage0[:])
         for a in range(2):
             nc.vector.tensor_copy(v_s[a][:], tab_s[:, T * a : T * (a + 1)].indirect(idx1[:]))
         nc.vector.tensor_copy(v_w[0][:], tab_w[0][:].indirect(idx1[:]))
-        stage0 = sb("stage0", [P, 2 * HALF], BF16)
-        quantise_w2(0, stage0[:])
         for h in range(2):
             nc.vector.tensor_copy(v_w[1][:, HALF * h : HALF * (h + 1)], tab_w[1][:].indirect(idx1[:, 32 * h : 32 * (h + 1)]))
 
+        def first_pass(t, h, a):
+            cols = slice(HALF * h, HALF * (h + 1))
+            nc.tensor.matmul_mx(
+                out=banks[2 * h + 1][:],
+                lhsT=w2_w[t][:, P * a : P * (a + 1)].bitcast(FP8X4),
+                lhsT_scale=w2_s[t][:, P * a : P * (a + 1)],
+                rhs=v_w[a][:, cols].bitcast(FP8X4),
+                rhs_scale=v_s[a][:, cols],
+                start=(a == 0), stop=(a == 1),
+            )
+            c0 = H * a + P * t
+            if t == 0:
+                w1_codes = w1_first[:, 2 * P * a : 2 * P * (a + 1)]
+            else:
+                w1_codes = w1_rest[:, 2 * P * (3 * a + t - 1) : 2 * P * (3 * a + t)]
+            nc.tensor.matmul_mx(
+                out=banks[2 * h][:],
+                lhsT=w1_codes.bitcast(FP4X4),
+                lhsT_scale=w1_s[:, c0 : c0 + P],
+                rhs=v_w[a][:, cols].bitcast(FP8X4),
+                rhs_scale=v_s[a][:, cols],
+                start=(a == 0), stop=(a == 1),
+            )
+
+        bw_sb = sb("bw_sb", [P, S], F32)
+
         def first_products(t):
-            a_sb = ring.tile([P, S], F32, name="a_sb")
-            bw_sb = ring.tile([P, S], F32, name="bw_sb")
+            a_sb = ring.tile([P, S], F32, name="a_sb", bufs=3)
+            b_sb = ring.tile([P, S], F32, name="b_sb", bufs=3)
             for h in range(2):
                 cols = slice(HALF * h, HALF * (h + 1))
-                a_bank, b_bank = banks[2 * h], banks[2 * h + 1]
                 for a in range(2):
-                    nc.tensor.matmul_mx(
-                        out=b_bank[:],
-                        lhsT=w2_w[t][:, P * a : P * (a + 1)].bitcast(FP8X4),
-                        lhsT_scale=w2_s[t][:, P * a : P * (a + 1)],
-                        rhs=v_w[a][:, cols].bitcast(FP8X4),
-                        rhs_scale=v_s[a][:, cols],
-                        start=(a == 0), stop=(a == 1),
-                    )
-                for a in range(2):
-                    c0 = H * a + P * t
-                    nc.tensor.matmul_mx(
-                        out=a_bank[:],
-                        lhsT=w1_w[:, 2 * c0 : 2 * (c0 + P)].bitcast(FP4X4),
-                        lhsT_scale=w1_s[:, c0 : c0 + P],
-                        rhs=v_w[a][:, cols].bitcast(FP8X4),
-                        rhs_scale=v_s[a][:, cols],
-                        start=(a == 0), stop=(a == 1),
-                    )
-                nc.scalar.copy(a_sb[:, cols], a_bank[:])
-                nc.vector.tensor_tensor(bw_sb[:, cols], b_bank[:], wgs_sb[h][:], MULT)
+                    first_pass(t, h, a)
+                nc.scalar.copy(b_sb[:, cols], banks[2 * h + 1][:])
+                nc.scalar.copy(a_sb[:, cols], banks[2 * h][:])
+            nc.gpsimd.tensor_tensor(bw_sb[:], b_sb[:], wgs_sb[:], MULT)
             return a_sb, bw_sb
 
         def gather_negated(dst, t, m0):
@@ -175,6 +187,15 @@ def tile_list_regression_bisect_features_kernel(
                 bank[:, 0:width].rearrange("p (b j u e) -> p b u j e", j=32, u=2, e=2),
             )
 
+        def turn_tiles(bank, diffs, t0, d_rows):
+            count = len(diffs)
+            for i, diff in enumerate(diffs):
+                nc.tensor.transpose(bank[:, P * i : P * (i + 1)], diff, ident[:])
+            nc.scalar.copy(
+                d_rows[:, 0, :].rearrange("p (u t j e) -> p t u j e", u=2, t=TILES, e=2)[:, t0 : t0 + count],
+                bank[:, 0 : P * count].rearrange("p (t j u e) -> p t u j e", j=32, u=2, e=2),
+            )
+
         def turn_back(bank, d_rows, b0, blocks, dst):
             for b in range(blocks):
                 words = d_rows[:, b0 + b, :].bitcast(F32)
@@ -186,48 +207,52 @@ def tile_list_regression_bisect_features_kernel(
                 bank[:, 0 : 2 * P * blocks].rearrange("p (b u m) -> p b m u", u=2, m=P),
             )
 
-        d_rows_a = sb("d_rows_a", [P, 4, H], BF16)
-        d_rows_b = sb("d_rows_b", [P, 2, H], BF16)
-        d_rows_c = sb("d_rows_c", [P, 1, H], BF16)
-        d_rows_d = sb("d_rows_d", [P, 1, H], BF16)
-        shared0 = sb("shared0", [P, 2 * HALF], F32)
+        d_rows = [sb("d_rows%d" % i, [P, blocks, H], BF16) for i, blocks in enumerate((2, 2, 2, 1, 1))]
+        QUARTER = 256
+        x2_b = [sb("x2_b%d" % t, [P, QUARTER], F32) for t in range(TILES)]
 
-        a_sb, bw_sb = first_products(0)
+        a_sb = ring.tile([P, S], F32, name="a_sb", bufs=3)
+        for h in range(2):
+            first_pass(0, h, 0)
         for h in range(2):
             cols = slice(HALF * h, HALF * (h + 1))
+            first_pass(0, h, 1)
+            nc.scalar.copy(a_sb[:, cols], banks[2 * h][:])
+            if h == 1:
+                quantise_w2(1, bw_sb[:, cols].bitcast(BF16))
+            nc.vector.tensor_tensor(bw_sb[:, cols], banks[2 * h + 1][:], wgs_sb[:, cols], MULT)
             nc.vector.tensor_tensor(page[0][:].indirect(idx2[:, 32 * h : 32 * (h + 1)]), a_sb[:, cols], bw_sb[:, cols], MULT)
-        quantise_w2(1, shared0[:, 256:768].bitcast(BF16))
         for t in range(TILES):
-            if t == 0:
-                x1, x2 = shared0[:, 0:HALF], shared0[:, HALF : 2 * HALF]
-            else:
-                nc.vector.tensor_tensor(page[t][:].indirect(idx2[:]), a_sb[:], bw_sb[:], MULT)
-                x12 = ring.tile([P, 2 * HALF], F32, name="x12")
-                x1, x2 = x12[:, 0:HALF], x12[:, HALF : 2 * HALF]
-            last_a, last_bw = a_sb, bw_sb
-            if 0 < t < TILES - 1:
-                a_sb, bw_sb = first_products(t + 1)
+            if t > 0:
+                nc.vector.tensor_tensor(page[t][:].indirect(idx2[:]), a_sb[:], bw[:], MULT)
+            x12 = ring.tile([P, 2 * HALF], F32, name="x12")
+            x1, x2 = x12[:, 0:HALF], x12[:, HALF : 2 * HALF]
+            last_a = a_sb
+            if t < TILES - 1:
+                a_sb, bw = first_products(t + 1)
             gather_negated(x1, t, 0)
-            nc.vector.tensor_copy(x2, page[t][:].indirect(idx4[:, 0:32]))
-            if t == 0:
-                a_sb, bw_sb = first_products(t + 1)
+            if t < TILES - 1:
+                nc.vector.tensor_copy(x2, page[t][:].indirect(idx4[:, 0:32]))
+            for h in range(2):
+                cols = slice(QUARTER * h, QUARTER * (h + 1))
+                if t == TILES - 1:
+                    nc.vector.tensor_copy(x2[:, cols], page[t][:].indirect(idx4[:, 16 * h : 16 * (h + 1)]))
+                turn(banks[4 + h], [x1[:, cols], x2[:, cols]], QUARTER, d_rows[h], t)
+            nc.vector.tensor_copy(x2_b[t][:], page[t][:].indirect(idx4[:, 32:48]))
             if t + 2 < TILES:
                 stage = ring.tile([P, 2 * HALF], BF16, name="stage", align_bytes=64)
                 quantise_w2(t + 2, stage[:])
-            turn(banks[4 + t % 2], [x1, x2], HALF, d_rows_a, t)
             if t == 2:
                 interleave(w4_bf[:], w4_raw[:])
                 nc.vector.quantize_mx(out=w4_w[:].bitcast(FP8X4), scales=w4_s[:], in_=w4_bf[:])
 
-        arena = sb("arena", [P, 2 * HALF], F32)
+        arena0 = sb("arena0", [P, HALF], F32)
+        arena1 = sb("arena1", [P, 2 * HALF], F32)
         d_w = sb("d_w", [P, M], U32)
         d_s = sb("d_s", [P, M], U8)
+        d_in_a = [arena0[:], arena1[:, 448:960]]
         for h in range(2):
-            turn_back(banks[6 + h], d_rows_a, 2 * h, 2, arena[:, HALF * h : HALF * (h + 1)])
-
-        x1_late = [last_a[:, 0:HALF], last_a[:, HALF:S], last_bw[:, 0:HALF], last_bw[:, HALF:S]]
-        for t in range(TILES):
-            gather_negated(x1_late[t], t, HALF)
+            turn_back(banks[6 + h], d_rows[h], 0, 2, d_in_a[h])
 
         def quantise_d(m0, width, src):
             nc.vector.quantize_mx(out=d_w[:, m0 : m0 + width].bitcast(FP8X4), scales=d_s[:, m0 : m0 + width], in_=src.bitcast(BF16))
@@ -244,64 +269,78 @@ def tile_list_regression_bisect_features_kernel(
 
         out_tiles = out.rearrange("(c p) m -> p c m", p=P)
 
-        quantise_d(0, HALF, arena[:])
-        act_a = [sb("act_a%d" % c, [P, HALF], F32) for c in range(TILES)]
-        out_a = [sb("out_a%d" % c, [P, HALF], F32)[:] for c in range(2)] + [x1_late[1], x1_late[2]]
-        for c in range(TILES):
-            second_product(banks[6 + c % 2][:], w3_w, w3_s, c, 0, HALF)
-            second_product(banks[c][:], w4_w, w4_s, c, 0, HALF)
-            nc.scalar.activation(act_a[c][:], banks[6 + c % 2][:], GELU)
-
-        def finish_a(c):
-            nc.vector.scalar_tensor_tensor(out_a[c], act_a[c][:], gain_sb[:, c : c + 1], banks[c][:], MULT, ADD)
-            nc.sync.dma_start(out_tiles[:, c, 0:HALF], out_a[c])
-
-        def products(c0, count, m0, width, y_bank, skip_bank, act):
+        def products(c0, count, m0, width, y_bank, skips, act):
             for i in range(count):
                 second_product(y_bank[:, width * i : width * (i + 1)], w3_w, w3_s, c0 + i, m0, width)
             for i in range(count):
-                second_product(skip_bank[:, width * i : width * (i + 1)], w4_w, w4_s, c0 + i, m0, width)
-            nc.scalar.activation(act[:], y_bank[:], GELU)
+                second_product(skips[i], w4_w, w4_s, c0 + i, m0, width)
+            nc.scalar.activation(act, y_bank[:].rearrange("p (i m) -> p i m", m=width), GELU)
 
         def finish(c0, count, m0, width, skip_bank, act, res):
             for i in range(count):
                 cols = slice(width * i, width * (i + 1))
                 nc.vector.scalar_tensor_tensor(res[:, cols], act[:, cols], gain_sb[:, c0 + i : c0 + i + 1], skip_bank[:, cols], MULT, ADD)
-            nc.sync.dma_start(out_tiles[:, c0 : c0 + count, m0 : m0 + width], res[:].rearrange("p (i m) -> p i m", m=width))
+            nc.sync.dma_start(out_tiles[:, c0 : c0 + count, m0 : m0 + width], res.rearrange("p (i m) -> p i m", m=width))
 
         d_in_b = sb("d_in_b", [P, HALF], F32)
         d_in_c = sb("d_in_c", [P, 256], F32)
         d_in_d = sb("d_in_d", [P, 256], F32)
-        act_late = [sb("act_late%d" % i, [P, HALF], F32) for i in range(4)]
-        out_late = [sb("out_late%d" % i, [P, HALF], F32) for i in range(4)]
+        act_a = sb("act_a", [P, TILES * HALF], F32)
+        act = [sb("act%d" % i, [P, HALF], F32) for i in range(4)]
+        res = [sb("res%d" % i, [P, HALF], F32)[:] for i in range(6)]
 
+        def split(ap, width):
+            return [ap[:, c0 : c0 + width] for c0 in range(0, HALF, width)]
+
+        def rows(ap, width):
+            return ap.rearrange("p (i m) -> p i m", m=width)
+
+        x1_late = [last_a[:, 0:HALF], last_a[:, HALF:S], arena0[:], arena1[:, 0:HALF]]
+
+        def gather_b(t):
+            gather_negated(x1_late[t], t, HALF)
+            turn(banks[4 + t % 2], [x2_b[t][:], x1_late[t][:, 0:256]], 256, d_rows[2], t)
+
+        for t in range(2):
+            gather_b(t)
+        for h in range(2):
+            cols = slice(QUARTER * h, QUARTER * (h + 1))
+            quantise_d(QUARTER * h, QUARTER, d_in_a[h])
+            gather_b(2 + h)
+            for g in range(2):
+                products(2 * g, 2, QUARTER * h, QUARTER, banks[6 + g], [banks[2 * g + i][:, cols] for i in range(2)],
+                         rows(act_a[:], HALF)[:, 2 * g : 2 * g + 2, cols])
+
+        def finish_a(c, res):
+            finish(c, 1, 0, HALF, banks[c], act_a[:, HALF * c : HALF * (c + 1)], res)
+
+        def gather_difference(dst, t, m0):
+            nc.vector.tensor_tensor(dst, page[t][:].indirect(idx4[:, m0 // 16 : (m0 + P) // 16]), x1_late[t][:, m0 - HALF : m0 - HALF + P], ADD)
+
+        turn_back(banks[5], d_rows[2], 0, 2, d_in_b[:])
+        diffs = split(arena1[:, HALF : 2 * HALF], P)
         for t in range(TILES):
-            x2 = arena[:, 256 * t : 256 * (t + 1)]
-            nc.vector.tensor_copy(x2, page[t][:].indirect(idx4[:, 32:48]))
-            turn(banks[4 + t % 2], [x1_late[t][:, 0:256], x2], 256, d_rows_b, t)
-        turn_back(banks[6], d_rows_b, 0, 2, d_in_b[:])
-        finish_a(0)
-        for t in range(TILES):
-            diff = act_a[0][:, P * t : P * (t + 1)]
-            nc.vector.tensor_tensor(diff, page[t][:].indirect(idx4[:, 48:56]), x1_late[t][:, 256:384], ADD)
-            turn(banks[4 + t % 2], [diff], P, d_rows_c, t)
-        turn_back(banks[7], d_rows_c, 0, 1, d_in_c[:])
-        finish_a(1)
+            gather_difference(diffs[t], t, 768)
+        turn_tiles(banks[4], diffs, 0, d_rows[3])
+        turn_back(banks[5], d_rows[3], 0, 1, d_in_c[:])
+        finish_a(0, res[0])
+        finish_a(1, res[1])
         quantise_d(HALF, 256, d_in_b[:])
-        products(0, 2, HALF, 256, banks[0], banks[1], act_late[0])
+        products(0, 2, HALF, 256, banks[6], split(banks[0], 256), rows(act[0][:], 256))
+        products(2, 2, HALF, 256, banks[7], split(banks[1], 256), rows(act[1][:], 256))
+        diffs = split(d_in_b, P)
         for t in range(TILES):
-            diff = d_in_b[:, P * t : P * (t + 1)]
-            nc.vector.tensor_tensor(diff, page[t][:].indirect(idx4[:, 56:64]), x1_late[t][:, 384:512], ADD)
-            turn(banks[4 + t % 2], [diff], P, d_rows_d, t)
-        turn_back(banks[7], d_rows_d, 0, 1, d_in_d[:])
+            gather_difference(diffs[t], t, 896)
+        turn_tiles(banks[4], diffs[0:3], 0, d_rows[4])
+        turn_tiles(banks[5], diffs[3:4], 3, d_rows[4])
+        turn_back(banks[4], d_rows[4], 0, 1, d_in_d[:])
         quantise_d(768, P, d_in_c[:])
-        finish_a(2)
-        finish_a(3)
+        finish_a(2, x1_late[1])
+        finish_a(3, x1_late[2])
         quantise_d(896, P, d_in_d[:])
-        products(2, 2, HALF, 256, banks[6], banks[2], act_late[1])
-        products(0, 4, 768, P, banks[4], banks[3], act_late[2])
-        products(0, 4, 896, P, banks[5], banks[7], act_late[3])
-        finish(0, 2, HALF, 256, banks[1], act_late[0], out_late[0])
-        finish(2, 2, HALF, 256, banks[2], act_late[1], out_late[1])
-        finish(0, 4, 768, P, banks[3], act_late[2], out_late[2])
-        finish(0, 4, 896, P, banks[7], act_late[3], out_late[3])
+        products(0, 4, 768, P, banks[5], split(banks[2], P), rows(act[2][:], P))
+        products(0, 4, 896, P, banks[4], split(banks[3], P), rows(act[3][:], P))
+        finish(0, 2, HALF, 256, banks[0], act[0], res[2])
+        finish(2, 2, HALF, 256, banks[1], act[1], res[3])
+        finish(0, 4, 768, P, banks[2], act[2], res[4])
+        finish(0, 4, 896, P, banks[3], act[3], res[5])

@@ -45,7 +45,9 @@ def tile_list_regression_bisect_features_kernel(
         tab_w = [sb("tab_w%d" % a, [P, T], U32) for a in range(2)]
         tab_s = sb("tab_s", [P, 2 * T], U8)
         v_w = [sb("v_w%d" % a, [P, S], U32) for a in range(2)]
-        v_s = [sb("v_s%d" % a, [P, S], U8) for a in range(2)]
+        picked_s = sb("picked_s", [P, 2 * S], U8)
+        v_planes = sb("v_planes", [P, 2 * S], U8)
+        v_s = [v_planes[:, S * a : S * (a + 1)] for a in range(2)]
         w1_first = sb("w1_first", [P, 2 * 2 * P], U8)
         w1_rest = sb("w1_rest", [P, 2 * 6 * P], U8)
         w1_s = sb("w1_s", [P, 2 * H], U8)
@@ -54,37 +56,37 @@ def tile_list_regression_bisect_features_kernel(
         w2_first = [sb("w2_first%d" % a, [P, 4, P], F32) for a in range(2)]
         w2_second = [sb("w2_second%d" % a, [P, 4, P], F32) for a in range(2)]
         w2_rest = [sb("w2_rest%d" % a, [P, 4, 2 * P], F32) for a in range(2)]
-        w2_w = [sb("w2_w%d" % t, [P, 2 * P], U32) for t in range(TILES)]
-        w2_s = [sb("w2_s%d" % t, [P, 2 * P], U8) for t in range(TILES)]
+        w2_w = sb("w2_w", [P, TILES * 2 * P], U32)
+        w2_s = sb("w2_s", [P, TILES * 2 * P], U8)
         w4_raw = sb("w4_raw", [P, 4, N], F32)
         w4_bf = sb("w4_bf", [P, 4 * N], BF16)
         w4_w = sb("w4_w", [P, N], U32)
         w4_s = sb("w4_s", [P, N], U8)
         wgs_sb = sb("wgs_sb", [P, S], F32)
+        shared = sb("shared", [P, 2 * S], F32)
+        bw_sb = shared[:, 0:S]
+        early = shared[:, 768:1280]
         gain_sb = sb("gain_sb", [P, TILES], F32)
         page = [sb("page%d" % t, [P, T2], F32) for t in range(TILES)]
         ident = sb("ident", [P, P], F32)
 
-        nc.vector.memset(tab_s[:, 0 : 4352].bitcast(I32), 0)
-        nc.gpsimd.memset(tab_s[:, 4352 : 2 * T].bitcast(I32), 0)
         nc.vector.memset(w1_s[:].bitcast(I32), 0)
+        nc.vector.memset(tab_s[0:112, :].bitcast(I32), 0)
+        nc.vector.memset(v_planes[:].bitcast(I32), 0)
         nc.vector.memset(w3_s[:].bitcast(I32), 0)
         make_identity(nc, ident[:])
 
-        for idx, src in ((idx1, offs), (idx2, offs2), (idx3, offs3), (idx4, offs4)):
-            nc.sync.dma_start(idx[:], src)
-        for q in range(4):
-            nc.sync.dma_start(
-                tab_s[32 * q : 32 * q + 4, :].bitcast(I32).rearrange("r (a c) -> r a c", a=2),
-                tab_scales[:, 4 * q : 4 * q + 4, :].bitcast(I32).rearrange("a r c -> r a c"),
-            )
+        nc.sync.dma_start(idx1[:], offs)
+        nc.sync.dma_start(
+            tab_s[112:128, :].bitcast(I32).rearrange("r (a c) -> r a c", a=2),
+            tab_scales.bitcast(I32).rearrange("a r c -> r a c"),
+        )
         w2_rows = w2.rearrange("(a p j) c -> a p j c", a=2, j=4)
         w1_rows = w1_words.bitcast(I32).rearrange("a p c -> p a c")
         tab_rows = [tab_words[a].rearrange("p t i -> p (t i)").bitcast(I32) for a in range(2)]
-        nc.sync.dma_start(tab_w[0][:, 0 : T // 2].bitcast(I32), tab_rows[0][:, 0 : T // 2])
         for a in range(2):
             nc.sync.dma_start(w2_first[a][:], w2_rows[a, :, :, 0:P])
-        nc.sync.dma_start(tab_w[0][:, T // 2 : T].bitcast(I32), tab_rows[0][:, T // 2 : T])
+        nc.sync.dma_start(tab_w[0][:].bitcast(I32), tab_rows[0])
         nc.sync.dma_start(w1_first[:].bitcast(I32).rearrange("p (a c) -> p a c", a=2), w1_rows[:, :, 0 : P // 2])
         for q in range(4):
             nc.sync.dma_start(
@@ -92,7 +94,8 @@ def tile_list_regression_bisect_features_kernel(
                 w1_scales[:, 4 * q : 4 * q + 4, :].bitcast(I32).rearrange("a r c -> r a c"),
             )
         nc.sync.dma_start(tab_w[1][:].bitcast(I32), tab_rows[1])
-        nc.sync.dma_start(wgs_sb[:, 0:HALF], wgs[:, 0:HALF])
+        nc.sync.dma_start(early, wgs[:, 0:HALF])
+        nc.sync.dma_start(idx2[:], offs2)
         nc.sync.dma_start(page[0][:], page0[0:P, :])
         nc.sync.dma_start(wgs_sb[:, HALF:S], wgs[:, HALF:S])
         for a in range(2):
@@ -100,6 +103,8 @@ def tile_list_regression_bisect_features_kernel(
         nc.sync.dma_start(w1_rest[:].bitcast(I32).rearrange("p (a c) -> p a c", a=2), w1_rows[:, :, P // 2 : 2 * P])
         for a in range(2):
             nc.sync.dma_start(w2_rest[a][:], w2_rows[a, :, :, 2 * P : H])
+        nc.sync.dma_start(idx3[:], offs3)
+        nc.sync.dma_start(idx4[:], offs4)
         nc.sync.dma_start(page[1][:], page0[P : 2 * P, :])
         nc.sync.dma_start(page[2][:], page0[2 * P : 3 * P, :])
         nc.sync.dma_start(w4_raw[:], w4.rearrange("(p j) n -> p j n", j=4))
@@ -119,16 +124,22 @@ def tile_list_regression_bisect_features_kernel(
                 src.rearrange("p j c -> p c j"),
             )
 
-        def quantise_w2(t, stage):
-            for a in range(2):
-                src = [w2_first[a][:], w2_second[a][:], w2_rest[a][:, :, 0:P], w2_rest[a][:, :, P : 2 * P]][t]
-                interleave(stage[:, HALF * a : HALF * (a + 1)], src)
-            nc.vector.quantize_mx(out=w2_w[t][:].bitcast(FP8X4), scales=w2_s[t][:], in_=stage)
+        def quantise_w2(t0, count, stage):
+            for i in range(count):
+                for a in range(2):
+                    src = [w2_first[a][:], w2_second[a][:], w2_rest[a][:, :, 0:P], w2_rest[a][:, :, P : 2 * P]][t0 + i]
+                    interleave(stage[:, HALF * (2 * i + a) : HALF * (2 * i + a + 1)], src)
+            cols = slice(2 * P * t0, 2 * P * (t0 + count))
+            nc.vector.quantize_mx(out=w2_w[:, cols].bitcast(FP8X4), scales=w2_s[:, cols], in_=stage)
 
-        stage0 = sb("stage0", [P, 2 * HALF], BF16)
-        quantise_w2(0, stage0[:])
         for a in range(2):
-            nc.vector.tensor_copy(v_s[a][:], tab_s[:, T * a : T * (a + 1)].indirect(idx1[:]))
+            nc.vector.tensor_copy(picked_s[:, S * a : S * (a + 1)], tab_s[:, T * a : T * (a + 1)].indirect(idx1[:]))
+        for q in range(4):
+            nc.gpsimd.dma_start(
+                v_planes[32 * q : 32 * q + 4, :].bitcast(I32), picked_s[112 + 4 * q : 116 + 4 * q, :].bitcast(I32)
+            )
+        stage0 = sb("stage0", [P, 2 * HALF], BF16)
+        quantise_w2(0, 1, stage0[:])
         nc.vector.tensor_copy(v_w[0][:], tab_w[0][:].indirect(idx1[:]))
         for h in range(2):
             nc.vector.tensor_copy(v_w[1][:, HALF * h : HALF * (h + 1)], tab_w[1][:].indirect(idx1[:, 32 * h : 32 * (h + 1)]))
@@ -137,8 +148,8 @@ def tile_list_regression_bisect_features_kernel(
             cols = slice(HALF * h, HALF * (h + 1))
             nc.tensor.matmul_mx(
                 out=banks[2 * h + 1][:],
-                lhsT=w2_w[t][:, P * a : P * (a + 1)].bitcast(FP8X4),
-                lhsT_scale=w2_s[t][:, P * a : P * (a + 1)],
+                lhsT=w2_w[:, P * (2 * t + a) : P * (2 * t + a + 1)].bitcast(FP8X4),
+                lhsT_scale=w2_s[:, P * (2 * t + a) : P * (2 * t + a + 1)],
                 rhs=v_w[a][:, cols].bitcast(FP8X4),
                 rhs_scale=v_s[a][:, cols],
                 start=(a == 0), stop=(a == 1),
@@ -157,7 +168,6 @@ def tile_list_regression_bisect_features_kernel(
                 start=(a == 0), stop=(a == 1),
             )
 
-        bw_sb = sb("bw_sb", [P, S], F32)
 
         def first_products(t):
             a_sb = ring.tile([P, S], F32, name="a_sb", bufs=3)
@@ -168,7 +178,7 @@ def tile_list_regression_bisect_features_kernel(
                     first_pass(t, h, a)
                 nc.scalar.copy(b_sb[:, cols], banks[2 * h + 1][:])
                 nc.scalar.copy(a_sb[:, cols], banks[2 * h][:])
-            nc.gpsimd.tensor_tensor(bw_sb[:], b_sb[:], wgs_sb[:], MULT)
+            nc.gpsimd.tensor_tensor(bw_sb, b_sb[:], wgs_sb[:], MULT)
             return a_sb, bw_sb
 
         def gather_negated(dst, t, m0):
@@ -212,6 +222,7 @@ def tile_list_regression_bisect_features_kernel(
         x2_b = [sb("x2_b%d" % t, [P, QUARTER], F32) for t in range(TILES)]
 
         a_sb = ring.tile([P, S], F32, name="a_sb", bufs=3)
+        nc.scalar.copy(wgs_sb[:, 0:HALF], early)
         for h in range(2):
             first_pass(0, h, 0)
         for h in range(2):
@@ -219,12 +230,12 @@ def tile_list_regression_bisect_features_kernel(
             first_pass(0, h, 1)
             nc.scalar.copy(a_sb[:, cols], banks[2 * h][:])
             if h == 1:
-                quantise_w2(1, bw_sb[:, cols].bitcast(BF16))
-            nc.vector.tensor_tensor(bw_sb[:, cols], banks[2 * h + 1][:], wgs_sb[:, cols], MULT)
+                quantise_w2(1, 1, early.bitcast(BF16))
+            nc.vector.tensor_tensor(bw_sb[:, cols], banks[2 * h + 1][:], (early, wgs_sb[:, cols])[h], MULT)
             nc.vector.tensor_tensor(page[0][:].indirect(idx2[:, 32 * h : 32 * (h + 1)]), a_sb[:, cols], bw_sb[:, cols], MULT)
         for t in range(TILES):
             if t > 0:
-                nc.vector.tensor_tensor(page[t][:].indirect(idx2[:]), a_sb[:], bw[:], MULT)
+                nc.vector.tensor_tensor(page[t][:].indirect(idx2[:]), a_sb[:], bw, MULT)
             x12 = ring.tile([P, 2 * HALF], F32, name="x12")
             x1, x2 = x12[:, 0:HALF], x12[:, HALF : 2 * HALF]
             last_a = a_sb
@@ -239,9 +250,8 @@ def tile_list_regression_bisect_features_kernel(
                     nc.vector.tensor_copy(x2[:, cols], page[t][:].indirect(idx4[:, 16 * h : 16 * (h + 1)]))
                 turn(banks[4 + h], [x1[:, cols], x2[:, cols]], QUARTER, d_rows[h], t)
             nc.vector.tensor_copy(x2_b[t][:], page[t][:].indirect(idx4[:, 32:48]))
-            if t + 2 < TILES:
-                stage = ring.tile([P, 2 * HALF], BF16, name="stage", align_bytes=64)
-                quantise_w2(t + 2, stage[:])
+            if t == 0:
+                quantise_w2(2, 2, shared[:, S : 2 * S].bitcast(BF16))
             if t == 2:
                 interleave(w4_bf[:], w4_raw[:])
                 nc.vector.quantize_mx(out=w4_w[:].bitcast(FP8X4), scales=w4_s[:], in_=w4_bf[:])

@@ -59,13 +59,13 @@ def tile_list_regression_bisect_features_kernel(
         w2_w = sb("w2_w", [P, TILES * 2 * P], U32)
         w2_s = sb("w2_s", [P, TILES * 2 * P], U8)
         w4_raw = sb("w4_raw", [P, 4, N], F32)
-        w4_bf = sb("w4_bf", [P, 4 * N], BF16)
         w4_w = sb("w4_w", [P, N], U32)
         w4_s = sb("w4_s", [P, N], U8)
         wgs_sb = sb("wgs_sb", [P, S], F32)
         shared = sb("shared", [P, 2 * S], F32)
         bw_sb = shared[:, 0:S]
         early = shared[:, 768:1280]
+        w4_bf = shared[:, 768:1792].bitcast(BF16)
         gain_sb = sb("gain_sb", [P, TILES], F32)
         page = [sb("page%d" % t, [P, T2], F32) for t in range(TILES)]
         ident = sb("ident", [P, P], F32)
@@ -252,9 +252,11 @@ def tile_list_regression_bisect_features_kernel(
             nc.vector.tensor_copy(x2_b[t][:], page[t][:].indirect(idx4[:, 32:48]))
             if t == 0:
                 quantise_w2(2, 2, shared[:, S : 2 * S].bitcast(BF16))
-            if t == 2:
-                interleave(w4_bf[:], w4_raw[:])
-                nc.vector.quantize_mx(out=w4_w[:].bitcast(FP8X4), scales=w4_s[:], in_=w4_bf[:])
+            if t == 0:
+                interleave(w4_bf[:, HALF : 4 * N], w4_raw[:, :, P:N])
+
+        interleave(w4_bf[:, 0:HALF], w4_raw[:, :, 0:P])
+        nc.vector.quantize_mx(out=w4_w[:].bitcast(FP8X4), scales=w4_s[:], in_=w4_bf)
 
         arena0 = sb("arena0", [P, HALF], F32)
         arena1 = sb("arena1", [P, 2 * HALF], F32)
@@ -286,11 +288,11 @@ def tile_list_regression_bisect_features_kernel(
                 second_product(skips[i], w4_w, w4_s, c0 + i, m0, width)
             nc.scalar.activation(act, y_bank[:].rearrange("p (i m) -> p i m", m=width), GELU)
 
-        def finish(c0, count, m0, width, skip_bank, act, res):
+        def finish(c0, count, m0, width, skip_bank, act, res, queue=nc.sync):
             for i in range(count):
                 cols = slice(width * i, width * (i + 1))
                 nc.vector.scalar_tensor_tensor(res[:, cols], act[:, cols], gain_sb[:, c0 + i : c0 + i + 1], skip_bank[:, cols], MULT, ADD)
-            nc.sync.dma_start(out_tiles[:, c0 : c0 + count, m0 : m0 + width], res.rearrange("p (i m) -> p i m", m=width))
+            queue.dma_start(out_tiles[:, c0 : c0 + count, m0 : m0 + width], res.rearrange("p (i m) -> p i m", m=width))
 
         d_in_b = sb("d_in_b", [P, HALF], F32)
         d_in_c = sb("d_in_c", [P, 256], F32)
@@ -353,4 +355,5 @@ def tile_list_regression_bisect_features_kernel(
         finish(0, 2, HALF, 256, banks[0], act[0], res[2])
         finish(2, 2, HALF, 256, banks[1], act[1], res[3])
         finish(0, 4, 768, P, banks[2], act[2], res[4])
-        finish(0, 4, 896, P, banks[3], act[3], res[5])
+        finish(0, 2, 896, P, banks[3], act[3], res[5][:, 0:256])
+        finish(2, 2, 896, P, banks[3][:, 256:HALF], act[3][:, 256:HALF], res[5][:, 256:HALF], nc.scalar)

@@ -43,9 +43,9 @@ def tile_list_regression_bisect_features_kernel(
         idx3 = keep.tile([P, M // 16], U16, name="idx3")
         idx4 = keep.tile([P, M // 16], U16, name="idx4")
         tab_w = [sb("tab_w%d" % a, [P, T], U32) for a in range(2)]
-        tab_s = sb("tab_s", [P, 2 * T], U8)
+        tab_s = sb("tab_s", [P, T], U8)
         v_w = [sb("v_w%d" % a, [P, S], U32) for a in range(2)]
-        picked_s = sb("picked_s", [P, 2 * S], U8)
+        picked_s = sb("picked_s", [P, S], U8)
         v_planes = sb("v_planes", [P, 2 * S], U8)
         v_s = [v_planes[:, S * a : S * (a + 1)] for a in range(2)]
         w1_first = sb("w1_first", [P, 2 * 2 * P], U8)
@@ -71,16 +71,15 @@ def tile_list_regression_bisect_features_kernel(
         ident = sb("ident", [P, P], F32)
 
         nc.vector.memset(w1_s[:].bitcast(I32), 0)
-        nc.vector.memset(tab_s[0:112, :].bitcast(I32), 0)
+        for a in range(2):
+            nc.vector.memset(tab_s[64 * a : 64 * a + 48, :].bitcast(I32), 0)
         nc.vector.memset(v_planes[:].bitcast(I32), 0)
         nc.vector.memset(w3_s[:].bitcast(I32), 0)
         make_identity(nc, ident[:])
 
         nc.sync.dma_start(idx1[:], offs)
-        nc.sync.dma_start(
-            tab_s[112:128, :].bitcast(I32).rearrange("r (a c) -> r a c", a=2),
-            tab_scales.bitcast(I32).rearrange("a r c -> r a c"),
-        )
+        for a in range(2):
+            nc.sync.dma_start(tab_s[64 * a + 48 : 64 * (a + 1), :].bitcast(I32), tab_scales[a].bitcast(I32))
         w2_rows = w2.rearrange("(a p j) c -> a p j c", a=2, j=4)
         w1_rows = w1_words.bitcast(I32).rearrange("a p c -> p a c")
         tab_rows = [tab_words[a].rearrange("p t i -> p (t i)").bitcast(I32) for a in range(2)]
@@ -89,7 +88,7 @@ def tile_list_regression_bisect_features_kernel(
         nc.sync.dma_start(tab_w[0][:].bitcast(I32), tab_rows[0])
         nc.sync.dma_start(w1_first[:].bitcast(I32).rearrange("p (a c) -> p a c", a=2), w1_rows[:, :, 0 : P // 2])
         for q in range(4):
-            nc.sync.dma_start(
+            nc.gpsimd.dma_start(
                 w1_s[32 * q : 32 * q + 4, :].bitcast(I32).rearrange("r (a c) -> r a c", a=2),
                 w1_scales[:, 4 * q : 4 * q + 4, :].bitcast(I32).rearrange("a r c -> r a c"),
             )
@@ -132,12 +131,11 @@ def tile_list_regression_bisect_features_kernel(
             cols = slice(2 * P * t0, 2 * P * (t0 + count))
             nc.vector.quantize_mx(out=w2_w[:, cols].bitcast(FP8X4), scales=w2_s[:, cols], in_=stage)
 
+        nc.vector.tensor_copy(picked_s[:], tab_s[:].indirect(idx1[:]))
         for a in range(2):
-            nc.vector.tensor_copy(picked_s[:, S * a : S * (a + 1)], tab_s[:, T * a : T * (a + 1)].indirect(idx1[:]))
-        for q in range(4):
-            nc.gpsimd.dma_start(
-                v_planes[32 * q : 32 * q + 4, :].bitcast(I32), picked_s[112 + 4 * q : 116 + 4 * q, :].bitcast(I32)
-            )
+            for q in range(4):
+                row = 64 * a + 48 + 4 * q
+                nc.gpsimd.dma_start(v_s[a][32 * q : 32 * q + 4, :].bitcast(I32), picked_s[row : row + 4, :].bitcast(I32))
         stage0 = sb("stage0", [P, 2 * HALF], BF16)
         quantise_w2(0, 1, stage0[:])
         nc.vector.tensor_copy(v_w[0][:], tab_w[0][:].indirect(idx1[:]))
@@ -219,7 +217,7 @@ def tile_list_regression_bisect_features_kernel(
 
         d_rows = [sb("d_rows%d" % i, [P, blocks, H], BF16) for i, blocks in enumerate((2, 2, 2, 1, 1))]
         QUARTER = 256
-        x2_b = [sb("x2_b%d" % t, [P, QUARTER], F32) for t in range(TILES)]
+        x2_early = [sb("x2_early%d" % t, [P, 3 * QUARTER], F32) for t in range(TILES)]
 
         a_sb = ring.tile([P, S], F32, name="a_sb", bufs=3)
         nc.scalar.copy(wgs_sb[:, 0:HALF], early)
@@ -236,20 +234,20 @@ def tile_list_regression_bisect_features_kernel(
         for t in range(TILES):
             if t > 0:
                 nc.vector.tensor_tensor(page[t][:].indirect(idx2[:]), a_sb[:], bw, MULT)
-            x12 = ring.tile([P, 2 * HALF], F32, name="x12")
-            x1, x2 = x12[:, 0:HALF], x12[:, HALF : 2 * HALF]
+            x1 = ring.tile([P, HALF], F32, name="x1")
+            x2 = x2_early[t]
             last_a = a_sb
             if t < TILES - 1:
                 a_sb, bw = first_products(t + 1)
-            gather_negated(x1, t, 0)
+            gather_negated(x1[:], t, 0)
             if t < TILES - 1:
-                nc.vector.tensor_copy(x2, page[t][:].indirect(idx4[:, 0:32]))
+                nc.vector.tensor_copy(x2[:], page[t][:].indirect(idx4[:, 0:48]))
+            else:
+                for h in range(3):
+                    nc.vector.tensor_copy(x2[:, QUARTER * h : QUARTER * (h + 1)], page[t][:].indirect(idx4[:, 16 * h : 16 * (h + 1)]))
             for h in range(2):
                 cols = slice(QUARTER * h, QUARTER * (h + 1))
-                if t == TILES - 1:
-                    nc.vector.tensor_copy(x2[:, cols], page[t][:].indirect(idx4[:, 16 * h : 16 * (h + 1)]))
                 turn(banks[4 + h], [x1[:, cols], x2[:, cols]], QUARTER, d_rows[h], t)
-            nc.vector.tensor_copy(x2_b[t][:], page[t][:].indirect(idx4[:, 32:48]))
             if t == 0:
                 quantise_w2(2, 2, shared[:, S : 2 * S].bitcast(BF16))
             if t == 0:
@@ -311,7 +309,7 @@ def tile_list_regression_bisect_features_kernel(
 
         def gather_b(t):
             gather_negated(x1_late[t], t, HALF)
-            turn(banks[4 + t % 2], [x2_b[t][:], x1_late[t][:, 0:256]], 256, d_rows[2], t)
+            turn(banks[4 + t % 2], [x2_early[t][:, HALF : 3 * QUARTER], x1_late[t][:, 0:256]], 256, d_rows[2], t)
 
         for t in range(2):
             gather_b(t)

@@ -16,6 +16,7 @@ FP8X4 = mybir.dt.float8_e4m3fn_x4
 FP4X4 = mybir.dt.float4_e2m1fn_x4
 MULT = mybir.AluOpType.mult
 ADD = mybir.AluOpType.add
+SUBTRACT = mybir.AluOpType.subtract
 GELU = mybir.ActivationFunctionType.Gelu_apprx_tanh
 
 P = 128
@@ -48,7 +49,7 @@ def tile_list_regression_bisect_features_kernel(
         picked_s = sb("picked_s", [P, S], U8)
         v_planes = sb("v_planes", [P, 2 * S], U8)
         v_s = [v_planes[:, S * a : S * (a + 1)] for a in range(2)]
-        w1_first = sb("w1_first", [P, 2 * 2 * P], U8)
+        w1_first = keep.tile([P, 2 * 2 * P], U8, name="w1_first", tag="after_first", align_bytes=64)
         w1_rest = sb("w1_rest", [P, 2 * 6 * P], U8)
         w1_s = sb("w1_s", [P, 2 * H], U8)
         w3_w = sb("w3_w", [P, N], U32)
@@ -59,41 +60,36 @@ def tile_list_regression_bisect_features_kernel(
         w2_w = sb("w2_w", [P, TILES * 2 * P], U32)
         w2_s = sb("w2_s", [P, TILES * 2 * P], U8)
         w4_raw = sb("w4_raw", [P, 4, N], F32)
-        w4_w = sb("w4_w", [P, N], U32)
         w4_s = sb("w4_s", [P, N], U8)
         wgs_sb = sb("wgs_sb", [P, S], F32)
-        shared = sb("shared", [P, 2 * S], F32)
-        bw_sb = shared[:, 0:S]
-        early = shared[:, 768:1280]
-        w4_bf = shared[:, 768:1792].bitcast(BF16)
         gain_sb = sb("gain_sb", [P, TILES], F32)
         page = [sb("page%d" % t, [P, T2], F32) for t in range(TILES)]
         ident = sb("ident", [P, P], F32)
+        warm = sb("warm", [P, 8], F32)
 
+        nc.vector.memset(tab_s[0:96, :].bitcast(I32), 0)
         nc.vector.memset(w1_s[:].bitcast(I32), 0)
-        for a in range(2):
-            nc.vector.memset(tab_s[64 * a : 64 * a + 48, :].bitcast(I32), 0)
         nc.vector.memset(v_planes[:].bitcast(I32), 0)
         nc.vector.memset(w3_s[:].bitcast(I32), 0)
         make_identity(nc, ident[:])
+        nc.scalar.activation(warm[:], ident[:, 0:8], GELU)
 
         nc.sync.dma_start(idx1[:], offs)
-        for a in range(2):
-            nc.sync.dma_start(tab_s[64 * a + 48 : 64 * (a + 1), :].bitcast(I32), tab_scales[a].bitcast(I32))
+        nc.sync.dma_start(tab_s[96:P, :].bitcast(I32), tab_scales.bitcast(I32).rearrange("a q t -> q a t"))
         w2_rows = w2.rearrange("(a p j) c -> a p j c", a=2, j=4)
         w1_rows = w1_words.bitcast(I32).rearrange("a p c -> p a c")
         tab_rows = [tab_words[a].rearrange("p t i -> p (t i)").bitcast(I32) for a in range(2)]
+        nc.sync.dma_start(tab_w[0][:].bitcast(I32), tab_rows[0])
         for a in range(2):
             nc.sync.dma_start(w2_first[a][:], w2_rows[a, :, :, 0:P])
-        nc.sync.dma_start(tab_w[0][:].bitcast(I32), tab_rows[0])
-        nc.sync.dma_start(w1_first[:].bitcast(I32).rearrange("p (a c) -> p a c", a=2), w1_rows[:, :, 0 : P // 2])
         for q in range(4):
             nc.gpsimd.dma_start(
                 w1_s[32 * q : 32 * q + 4, :].bitcast(I32).rearrange("r (a c) -> r a c", a=2),
                 w1_scales[:, 4 * q : 4 * q + 4, :].bitcast(I32).rearrange("a r c -> r a c"),
             )
         nc.sync.dma_start(tab_w[1][:].bitcast(I32), tab_rows[1])
-        nc.sync.dma_start(early, wgs[:, 0:HALF])
+        nc.sync.dma_start(w1_first[:].bitcast(I32).rearrange("p (a c) -> p a c", a=2), w1_rows[:, :, 0 : P // 2])
+        nc.sync.dma_start(wgs_sb[:, 0:HALF], wgs[:, 0:HALF])
         nc.sync.dma_start(idx2[:], offs2)
         nc.sync.dma_start(page[0][:], page0[0:P, :])
         nc.sync.dma_start(wgs_sb[:, HALF:S], wgs[:, HALF:S])
@@ -105,8 +101,8 @@ def tile_list_regression_bisect_features_kernel(
         nc.sync.dma_start(idx3[:], offs3)
         nc.sync.dma_start(idx4[:], offs4)
         nc.sync.dma_start(page[1][:], page0[P : 2 * P, :])
-        nc.sync.dma_start(page[2][:], page0[2 * P : 3 * P, :])
         nc.sync.dma_start(w4_raw[:], w4.rearrange("(p j) n -> p j n", j=4))
+        nc.sync.dma_start(page[2][:], page0[2 * P : 3 * P, :])
         nc.sync.dma_start(w3_w[:].bitcast(I32), w3_words[0].rearrange("p n i -> p (n i)").bitcast(I32))
         for q in range(4):
             nc.sync.dma_start(
@@ -123,26 +119,29 @@ def tile_list_regression_bisect_features_kernel(
                 src.rearrange("p j c -> p c j"),
             )
 
-        def quantise_w2(t0, count, stage):
-            for i in range(count):
-                for a in range(2):
-                    src = [w2_first[a][:], w2_second[a][:], w2_rest[a][:, :, 0:P], w2_rest[a][:, :, P : 2 * P]][t0 + i]
-                    interleave(stage[:, HALF * (2 * i + a) : HALF * (2 * i + a + 1)], src)
-            cols = slice(2 * P * t0, 2 * P * (t0 + count))
+        def cast_w2(t, stage):
+            for a in range(2):
+                src = [w2_first[a][:], w2_second[a][:], w2_rest[a][:, :, 0:P], w2_rest[a][:, :, P : 2 * P]][t]
+                interleave(stage[:, HALF * a : HALF * (a + 1)], src)
+
+        def quantise_w2(t, stage):
+            cols = slice(2 * P * t, 2 * P * (t + 1))
             nc.vector.quantize_mx(out=w2_w[:, cols].bitcast(FP8X4), scales=w2_s[:, cols], in_=stage)
 
         nc.vector.tensor_copy(picked_s[:], tab_s[:].indirect(idx1[:]))
-        for a in range(2):
-            for q in range(4):
-                row = 64 * a + 48 + 4 * q
-                nc.gpsimd.dma_start(v_s[a][32 * q : 32 * q + 4, :].bitcast(I32), picked_s[row : row + 4, :].bitcast(I32))
-        stage0 = sb("stage0", [P, 2 * HALF], BF16)
-        quantise_w2(0, 1, stage0[:])
+        for q in range(4):
+            nc.gpsimd.dma_start(
+                v_planes[32 * q : 32 * q + 4, :].bitcast(I32).rearrange("r (a c) -> r a c", a=2),
+                picked_s[96 + 8 * q : 96 + 8 * (q + 1), :].bitcast(I32),
+            )
         nc.vector.tensor_copy(v_w[0][:], tab_w[0][:].indirect(idx1[:]))
+        stage0 = sb("stage0", [P, 2 * HALF], BF16)
+        cast_w2(0, stage0[:])
+        quantise_w2(0, stage0[:])
         for h in range(2):
             nc.vector.tensor_copy(v_w[1][:, HALF * h : HALF * (h + 1)], tab_w[1][:].indirect(idx1[:, 32 * h : 32 * (h + 1)]))
 
-        def first_pass(t, h, a):
+        def pass_b(t, h, a):
             cols = slice(HALF * h, HALF * (h + 1))
             nc.tensor.matmul_mx(
                 out=banks[2 * h + 1][:],
@@ -152,6 +151,9 @@ def tile_list_regression_bisect_features_kernel(
                 rhs_scale=v_s[a][:, cols],
                 start=(a == 0), stop=(a == 1),
             )
+
+        def pass_a(t, h, a):
+            cols = slice(HALF * h, HALF * (h + 1))
             c0 = H * a + P * t
             if t == 0:
                 w1_codes = w1_first[:, 2 * P * a : 2 * P * (a + 1)]
@@ -166,21 +168,14 @@ def tile_list_regression_bisect_features_kernel(
                 start=(a == 0), stop=(a == 1),
             )
 
+        def gather_negated(dst, t):
+            nc.vector.tensor_scalar(dst, page[t][:].indirect(idx3[:, 0 : HALF // 16]), -1.0, 0.0, MULT, ADD)
 
-        def first_products(t):
-            a_sb = ring.tile([P, S], F32, name="a_sb", bufs=3)
-            b_sb = ring.tile([P, S], F32, name="b_sb", bufs=3)
-            for h in range(2):
-                cols = slice(HALF * h, HALF * (h + 1))
-                for a in range(2):
-                    first_pass(t, h, a)
-                nc.scalar.copy(b_sb[:, cols], banks[2 * h + 1][:])
-                nc.scalar.copy(a_sb[:, cols], banks[2 * h][:])
-            nc.gpsimd.tensor_tensor(bw_sb, b_sb[:], wgs_sb[:], MULT)
-            return a_sb, bw_sb
+        def gather(dst, t, idx, m0, width):
+            nc.vector.tensor_copy(dst, page[t][:].indirect(idx[:, m0 // 16 : (m0 + width) // 16]))
 
-        def gather_negated(dst, t, m0):
-            nc.vector.tensor_scalar(dst, page[t][:].indirect(idx3[:, m0 // 16 : (m0 + HALF) // 16]), -1.0, 0.0, MULT, ADD)
+        def gather_difference(dst, t, m0, width, x1):
+            nc.vector.tensor_tensor(dst, page[t][:].indirect(idx4[:, m0 // 16 : (m0 + width) // 16]), x1, SUBTRACT)
 
         def turn(bank, parts, width, d_rows, t):
             blocks = width // P
@@ -217,53 +212,83 @@ def tile_list_regression_bisect_features_kernel(
 
         d_rows = [sb("d_rows%d" % i, [P, blocks, H], BF16) for i, blocks in enumerate((2, 2, 2, 1, 1))]
         QUARTER = 256
-        x2_early = [sb("x2_early%d" % t, [P, 3 * QUARTER], F32) for t in range(TILES)]
+        x1_c2 = [sb("x1_c2_%d" % t, [P, QUARTER], F32) for t in range(TILES)]
 
-        a_sb = ring.tile([P, S], F32, name="a_sb", bufs=3)
-        nc.scalar.copy(wgs_sb[:, 0:HALF], early)
+        a_first = sb("a_first", [P, S], F32)
+        a_sb = a_first
+        bw_first = sb("bw_first", [P, HALF], F32)
         for h in range(2):
-            first_pass(0, h, 0)
+            pass_b(0, h, 0)
+            pass_a(0, h, 0)
         for h in range(2):
-            cols = slice(HALF * h, HALF * (h + 1))
-            first_pass(0, h, 1)
-            nc.scalar.copy(a_sb[:, cols], banks[2 * h][:])
-            if h == 1:
-                quantise_w2(1, 1, early.bitcast(BF16))
-            nc.vector.tensor_tensor(bw_sb[:, cols], banks[2 * h + 1][:], (early, wgs_sb[:, cols])[h], MULT)
-            nc.vector.tensor_tensor(page[0][:].indirect(idx2[:, 32 * h : 32 * (h + 1)]), a_sb[:, cols], bw_sb[:, cols], MULT)
+            pass_b(0, h, 1)
+            pass_a(0, h, 1)
+            nc.scalar.copy(a_sb[:, HALF * h : HALF * (h + 1)], banks[2 * h][:])
+        shared = keep.tile([P, 2496], F32, name="shared", tag="after_first", align_bytes=64)
+        bw = shared[:, 0:S]
+        stage1 = shared[:, 832:1344].bitcast(BF16)
+        stage2 = shared[:, S : S + HALF].bitcast(BF16)
+        stage3 = a_first[:, HALF:S].bitcast(BF16)
+        stage4 = shared[:, 1472:2496].bitcast(BF16)
+        nc.vector.tensor_tensor(bw_first[:], banks[1][:], wgs_sb[:, 0:HALF], MULT)
+        nc.vector.tensor_tensor(page[0][:].indirect(idx2[:, 0:32]), a_sb[:, 0:HALF], bw_first[:], MULT)
+        cast_w2(1, stage1)
+        quantise_w2(1, stage1)
+        nc.vector.tensor_tensor(bw[:, HALF:S], banks[3][:], wgs_sb[:, HALF:S], MULT)
+        nc.vector.tensor_tensor(page[0][:].indirect(idx2[:, 32:64]), a_sb[:, HALF:S], bw[:, HALF:S], MULT)
+        cast_w2(2, stage2)
+        quantise_w2(2, stage2)
+
+        def first_products(t):
+            a_next = ring.tile([P, S], F32, name="a_next")
+            if t < TILES - 1:
+                b_next = ring.tile([P, S], F32, name="b_next")
+            else:
+                b_next = keep.tile([P, S], F32, name="b_last", tag="after_last_b", align_bytes=64)
+            for h in range(2):
+                for a in range(2):
+                    pass_b(t, h, a)
+                nc.scalar.copy(b_next[:, HALF * h : HALF * (h + 1)], banks[2 * h + 1][:])
+            for h in range(2):
+                for a in range(2):
+                    pass_a(t, h, a)
+                nc.scalar.copy(a_next[:, HALF * h : HALF * (h + 1)], banks[2 * h][:])
+            nc.gpsimd.tensor_tensor(bw, b_next[:], wgs_sb[:], MULT)
+            return a_next
+
         for t in range(TILES):
             if t > 0:
                 nc.vector.tensor_tensor(page[t][:].indirect(idx2[:]), a_sb[:], bw, MULT)
-            x1 = ring.tile([P, HALF], F32, name="x1")
-            x2 = x2_early[t]
-            last_a = a_sb
-            if t < TILES - 1:
-                a_sb, bw = first_products(t + 1)
-            gather_negated(x1[:], t, 0)
-            if t < TILES - 1:
-                nc.vector.tensor_copy(x2[:], page[t][:].indirect(idx4[:, 0:48]))
+            if t == 0:
+                x1 = shared[:, S : S + HALF]
+            elif t == 1:
+                x1 = a_first[:, HALF:S]
             else:
-                for h in range(3):
-                    nc.vector.tensor_copy(x2[:, QUARTER * h : QUARTER * (h + 1)], page[t][:].indirect(idx4[:, 16 * h : 16 * (h + 1)]))
+                x1 = ring.tile([P, HALF], F32, name="x1")[:]
+            x2 = ring.tile([P, HALF], F32, name="x2")[:]
+            if t < TILES - 1:
+                a_sb = first_products(t + 1)
+            if t == 0:
+                cast_w2(3, stage3)
+            gather_negated(x1, t)
+            if t < TILES - 1:
+                gather(x2, t, idx4, 0, HALF)
+            else:
+                for h in range(2):
+                    gather(x2[:, QUARTER * h : QUARTER * (h + 1)], t, idx4, QUARTER * h, QUARTER)
+            gather(x1_c2[t][:], t, idx3, HALF, QUARTER)
             for h in range(2):
                 cols = slice(QUARTER * h, QUARTER * (h + 1))
                 turn(banks[4 + h], [x1[:, cols], x2[:, cols]], QUARTER, d_rows[h], t)
             if t == 0:
-                quantise_w2(2, 2, shared[:, S : 2 * S].bitcast(BF16))
-            if t == 0:
-                interleave(w4_bf[:, HALF : 4 * N], w4_raw[:, :, P:N])
+                quantise_w2(3, stage3)
+                interleave(stage4, w4_raw[:])
+            if t == TILES - 1:
+                w4_w = keep.tile([P, N], U32, name="w4_w", tag="after_last_b", align_bytes=64)
+                nc.vector.quantize_mx(out=w4_w[:].bitcast(FP8X4), scales=w4_s[:], in_=stage4)
 
-        interleave(w4_bf[:, 0:HALF], w4_raw[:, :, 0:P])
-        nc.vector.quantize_mx(out=w4_w[:].bitcast(FP8X4), scales=w4_s[:], in_=w4_bf)
-
-        arena0 = sb("arena0", [P, HALF], F32)
-        arena1 = sb("arena1", [P, 2 * HALF], F32)
         d_w = sb("d_w", [P, M], U32)
         d_s = sb("d_s", [P, M], U8)
-        d_in_a = [arena0[:], arena1[:, 448:960]]
-        for h in range(2):
-            turn_back(banks[6 + h], d_rows[h], 0, 2, d_in_a[h])
-
         def quantise_d(m0, width, src):
             nc.vector.quantize_mx(out=d_w[:, m0 : m0 + width].bitcast(FP8X4), scales=d_s[:, m0 : m0 + width], in_=src.bitcast(BF16))
 
@@ -279,12 +304,14 @@ def tile_list_regression_bisect_features_kernel(
 
         out_tiles = out.rearrange("(c p) m -> p c m", p=P)
 
-        def products(c0, count, m0, width, y_bank, skips, act):
+        def gelu_branch(c0, count, m0, width, bank, act):
             for i in range(count):
-                second_product(y_bank[:, width * i : width * (i + 1)], w3_w, w3_s, c0 + i, m0, width)
+                second_product(bank[:, width * i : width * (i + 1)], w3_w, w3_s, c0 + i, m0, width)
+            nc.scalar.activation(act, bank[:, 0 : width * count].rearrange("p (i m) -> p i m", m=width), GELU)
+
+        def skip_branch(c0, count, m0, width, bank):
             for i in range(count):
-                second_product(skips[i], w4_w, w4_s, c0 + i, m0, width)
-            nc.scalar.activation(act, y_bank[:].rearrange("p (i m) -> p i m", m=width), GELU)
+                second_product(bank[:, width * i : width * (i + 1)], w4_w, w4_s, c0 + i, m0, width)
 
         def finish(c0, count, m0, width, skip_bank, act, res, queue=nc.sync):
             for i in range(count):
@@ -292,66 +319,78 @@ def tile_list_regression_bisect_features_kernel(
                 nc.vector.scalar_tensor_tensor(res[:, cols], act[:, cols], gain_sb[:, c0 + i : c0 + i + 1], skip_bank[:, cols], MULT, ADD)
             queue.dma_start(out_tiles[:, c0 : c0 + count, m0 : m0 + width], res.rearrange("p (i m) -> p i m", m=width))
 
-        d_in_b = sb("d_in_b", [P, HALF], F32)
-        d_in_c = sb("d_in_c", [P, 256], F32)
-        d_in_d = sb("d_in_d", [P, 256], F32)
-        act_a = sb("act_a", [P, TILES * HALF], F32)
-        act = [sb("act%d" % i, [P, HALF], F32) for i in range(4)]
-        res = [sb("res%d" % i, [P, HALF], F32)[:] for i in range(6)]
+        def rows(ap, width):
+            return ap.rearrange("p (i m) -> p i m", m=width)
 
         def split(ap, width):
             return [ap[:, c0 : c0 + width] for c0 in range(0, HALF, width)]
 
-        def rows(ap, width):
-            return ap.rearrange("p (i m) -> p i m", m=width)
+        arena = sb("arena", [P, 1280], F32)
+        d_in = [sb("d_in0", [P, HALF], F32)[:], arena[:, 192:704], sb("d_in2", [P, HALF], F32)[:],
+                sb("d_in3", [P, QUARTER], F32)[:], sb("d_in4", [P, QUARTER], F32)[:]]
+        x1_c3 = [arena[:, 0:256], arena[:, 256:512], arena[:, 640:896], sb("x1_c3_last", [P, QUARTER], F32)[:]]
+        diff_a = sb("diff_a", [P, 3 * P], F32)
+        act_a = sb("act_a", [P, TILES * HALF], F32)
+        act = [sb("act%d" % i, [P, HALF], F32) for i in range(4)]
+        res = [sb("res%d" % i, [P, HALF], F32)[:] for i in range(6)]
 
-        x1_late = [last_a[:, 0:HALF], last_a[:, HALF:S], arena0[:], arena1[:, 0:HALF]]
+        def finish_a(c, bank, dst):
+            finish(c, 1, 0, HALF, bank, act_a[:, HALF * c : HALF * (c + 1)], dst)
 
-        def gather_b(t):
-            gather_negated(x1_late[t], t, HALF)
-            turn(banks[4 + t % 2], [x2_early[t][:, HALF : 3 * QUARTER], x1_late[t][:, 0:256]], 256, d_rows[2], t)
-
-        for t in range(2):
-            gather_b(t)
-        for h in range(2):
-            cols = slice(QUARTER * h, QUARTER * (h + 1))
-            quantise_d(QUARTER * h, QUARTER, d_in_a[h])
-            gather_b(2 + h)
+        def gelu_a(h):
             for g in range(2):
-                products(2 * g, 2, QUARTER * h, QUARTER, banks[6 + g], [banks[2 * g + i][:, cols] for i in range(2)],
-                         rows(act_a[:], HALF)[:, 2 * g : 2 * g + 2, cols])
+                gelu_branch(2 * g, 2, QUARTER * h, QUARTER, banks[2 * h + g],
+                            rows(act_a[:], HALF)[:, 2 * g : 2 * g + 2, QUARTER * h : QUARTER * (h + 1)])
 
-        def finish_a(c, res):
-            finish(c, 1, 0, HALF, banks[c], act_a[:, HALF * c : HALF * (c + 1)], res)
-
-        def gather_difference(dst, t, m0):
-            nc.vector.tensor_tensor(dst, page[t][:].indirect(idx4[:, m0 // 16 : (m0 + P) // 16]), x1_late[t][:, m0 - HALF : m0 - HALF + P], ADD)
-
-        turn_back(banks[5], d_rows[2], 0, 2, d_in_b[:])
-        diffs = split(arena1[:, HALF : 2 * HALF], P)
+        for h in range(2):
+            turn_back(banks[6 + h], d_rows[h], 0, 2, d_in[h])
+        gather(x1_c3[3], 3, idx3, 768, QUARTER)
+        diffs = [x1[:, 0:QUARTER], x2[:, 0:QUARTER]] + split(d_in[0], QUARTER)
+        for t in range(2):
+            gather_difference(diffs[t], t, HALF, QUARTER, x1_c2[t][:])
+        quantise_d(0, QUARTER, d_in[0])
+        gelu_a(0)
+        quantise_d(QUARTER, QUARTER, d_in[1])
+        for t in range(2, TILES):
+            gather_difference(diffs[t], t, HALF, QUARTER, x1_c2[t][:])
         for t in range(TILES):
-            gather_difference(diffs[t], t, 768)
-        turn_tiles(banks[4], diffs, 0, d_rows[3])
-        turn_back(banks[5], d_rows[3], 0, 1, d_in_c[:])
-        finish_a(0, res[0])
-        finish_a(1, res[1])
-        quantise_d(HALF, 256, d_in_b[:])
-        products(0, 2, HALF, 256, banks[6], split(banks[0], 256), rows(act[0][:], 256))
-        products(2, 2, HALF, 256, banks[7], split(banks[1], 256), rows(act[1][:], 256))
-        diffs = split(d_in_b, P)
+            turn(banks[6 + t // 2][:, QUARTER * (t % 2) : QUARTER * (t % 2 + 1)], [diffs[t]], QUARTER, d_rows[2], t)
+        turn_back(banks[4], d_rows[2], 0, 2, d_in[2])
+        gelu_a(1)
+        for c in range(2):
+            skip_branch(c, 1, 0, HALF, banks[c])
+        for t in range(TILES - 1):
+            gather(x1_c3[t], t, idx3, 768, QUARTER)
+        diffs = [diff_a[:, P * t : P * (t + 1)] for t in range(TILES - 1)] + [arena[:, 512:640]]
         for t in range(TILES):
-            gather_difference(diffs[t], t, 896)
-        turn_tiles(banks[4], diffs[0:3], 0, d_rows[4])
-        turn_tiles(banks[5], diffs[3:4], 3, d_rows[4])
-        turn_back(banks[4], d_rows[4], 0, 1, d_in_d[:])
-        quantise_d(768, P, d_in_c[:])
-        finish_a(2, x1_late[1])
-        finish_a(3, x1_late[2])
-        quantise_d(896, P, d_in_d[:])
-        products(0, 4, 768, P, banks[5], split(banks[2], P), rows(act[2][:], P))
-        products(0, 4, 896, P, banks[4], split(banks[3], P), rows(act[3][:], P))
-        finish(0, 2, HALF, 256, banks[0], act[0], res[2])
-        finish(2, 2, HALF, 256, banks[1], act[1], res[3])
-        finish(0, 4, 768, P, banks[2], act[2], res[4])
-        finish(0, 2, 896, P, banks[3], act[3], res[5][:, 0:256])
-        finish(2, 2, 896, P, banks[3][:, 256:HALF], act[3][:, 256:HALF], res[5][:, 256:HALF], nc.scalar)
+            gather_difference(diffs[t], t, 768, P, x1_c3[t][:, 0:P])
+        turn_tiles(banks[5], diffs, 0, d_rows[3])
+        quantise_d(HALF, QUARTER, d_in[2])
+        turn_back(banks[6], d_rows[3], 0, 1, d_in[3])
+        for g in range(2):
+            gelu_branch(2 * g, 2, HALF, QUARTER, banks[2 + g], rows(act[g][:], QUARTER))
+        diffs = split(d_in[2], P)
+        for t in range(TILES):
+            gather_difference(diffs[t], t, 896, P, x1_c3[t][:, P:QUARTER])
+        turn_tiles(banks[7], diffs[0:3], 0, d_rows[4])
+        turn_tiles(banks[4], diffs[3:4], 3, d_rows[4])
+        quantise_d(768, P, d_in[3])
+        turn_back(banks[5], d_rows[4], 0, 1, d_in[4])
+        gelu_branch(0, 4, 768, P, banks[2], rows(act[2][:], P))
+        quantise_d(896, P, d_in[4])
+        gelu_branch(0, 4, 896, P, banks[4], rows(act[3][:], P))
+        finish_a(0, banks[0], arena[:, 768:1280])
+        finish_a(1, banks[1], arena[:, 0:HALF])
+        for c in range(2, TILES):
+            skip_branch(c, 1, 0, HALF, banks[c - 2])
+        skip_branch(0, 2, HALF, QUARTER, banks[3])
+        skip_branch(0, 4, 768, P, banks[6])
+        skip_branch(0, 4, 896, P, banks[7])
+        finish_a(2, banks[0], res[0])
+        skip_branch(2, 2, HALF, QUARTER, banks[0])
+        finish_a(3, banks[1], res[1])
+        finish(0, 2, HALF, QUARTER, banks[3], act[0], res[2])
+        finish(2, 2, HALF, QUARTER, banks[0], act[1], res[3])
+        finish(0, 4, 768, P, banks[6], act[2], res[4])
+        finish(0, 2, 896, P, banks[7], act[3], res[5][:, 0:QUARTER])
+        finish(2, 2, 896, P, banks[7][:, QUARTER:HALF], act[3][:, QUARTER:HALF], res[5][:, QUARTER:HALF], nc.scalar)

@@ -16,7 +16,6 @@ FP8X4 = mybir.dt.float8_e4m3fn_x4
 FP4X4 = mybir.dt.float4_e2m1fn_x4
 MULT = mybir.AluOpType.mult
 ADD = mybir.AluOpType.add
-SUBTRACT = mybir.AluOpType.subtract
 GELU = mybir.ActivationFunctionType.Gelu_apprx_tanh
 
 P = 128
@@ -67,8 +66,8 @@ def tile_list_regression_bisect_features_kernel(
         ident = sb("ident", [P, P], F32)
         warm = sb("warm", [P, 8], F32)
 
-        nc.vector.memset(tab_s[0:96, :].bitcast(I32), 0)
         nc.vector.memset(w1_s[:].bitcast(I32), 0)
+        nc.vector.memset(tab_s[0:96, :].bitcast(I32), 0)
         nc.vector.memset(v_planes[:].bitcast(I32), 0)
         nc.vector.memset(w3_s[:].bitcast(I32), 0)
         make_identity(nc, ident[:])
@@ -168,14 +167,11 @@ def tile_list_regression_bisect_features_kernel(
                 start=(a == 0), stop=(a == 1),
             )
 
-        def gather_negated(dst, t):
-            nc.vector.tensor_scalar(dst, page[t][:].indirect(idx3[:, 0 : HALF // 16]), -1.0, 0.0, MULT, ADD)
+        def gather_negated(dst, t, m0):
+            nc.vector.tensor_scalar(dst, page[t][:].indirect(idx3[:, m0 // 16 : (m0 + HALF) // 16]), -1.0, 0.0, MULT, ADD)
 
         def gather(dst, t, idx, m0, width):
             nc.vector.tensor_copy(dst, page[t][:].indirect(idx[:, m0 // 16 : (m0 + width) // 16]))
-
-        def gather_difference(dst, t, m0, width, x1):
-            nc.vector.tensor_tensor(dst, page[t][:].indirect(idx4[:, m0 // 16 : (m0 + width) // 16]), x1, SUBTRACT)
 
         def turn(bank, parts, width, d_rows, t):
             blocks = width // P
@@ -190,10 +186,14 @@ def tile_list_regression_bisect_features_kernel(
                 bank[:, 0:width].rearrange("p (b j u e) -> p b u j e", j=32, u=2, e=2),
             )
 
-        def turn_tiles(bank, diffs, t0, d_rows):
-            count = len(diffs)
-            for i, diff in enumerate(diffs):
-                nc.tensor.transpose(bank[:, P * i : P * (i + 1)], diff, ident[:])
+        def turn_tiles(bank, x1s, x2s, t0, d_rows):
+            count = len(x1s)
+            for k, parts in enumerate((x1s, x2s)):
+                for i, part in enumerate(parts):
+                    nc.tensor.matmul(
+                        bank[:, P * i : P * (i + 1)], part, ident[:],
+                        start=(k == 0 and i == 0), stop=(k == 1 and i == count - 1), is_transpose=True,
+                    )
             nc.scalar.copy(
                 d_rows[:, 0, :].rearrange("p (u t j e) -> p t u j e", u=2, t=TILES, e=2)[:, t0 : t0 + count],
                 bank[:, 0 : P * count].rearrange("p (t j u e) -> p t u j e", j=32, u=2, e=2),
@@ -212,7 +212,7 @@ def tile_list_regression_bisect_features_kernel(
 
         d_rows = [sb("d_rows%d" % i, [P, blocks, H], BF16) for i, blocks in enumerate((2, 2, 2, 1, 1))]
         QUARTER = 256
-        x1_c2 = [sb("x1_c2_%d" % t, [P, QUARTER], F32) for t in range(TILES)]
+        x2_c2 = [sb("x2_c2_%d" % t, [P, QUARTER], F32) for t in range(TILES)]
 
         a_first = sb("a_first", [P, S], F32)
         a_sb = a_first
@@ -270,13 +270,13 @@ def tile_list_regression_bisect_features_kernel(
                 a_sb = first_products(t + 1)
             if t == 0:
                 cast_w2(3, stage3)
-            gather_negated(x1, t)
+            gather_negated(x1, t, 0)
             if t < TILES - 1:
                 gather(x2, t, idx4, 0, HALF)
             else:
                 for h in range(2):
                     gather(x2[:, QUARTER * h : QUARTER * (h + 1)], t, idx4, QUARTER * h, QUARTER)
-            gather(x1_c2[t][:], t, idx3, HALF, QUARTER)
+            gather(x2_c2[t][:], t, idx4, HALF, QUARTER)
             for h in range(2):
                 cols = slice(QUARTER * h, QUARTER * (h + 1))
                 turn(banks[4 + h], [x1[:, cols], x2[:, cols]], QUARTER, d_rows[h], t)
@@ -322,17 +322,14 @@ def tile_list_regression_bisect_features_kernel(
         def rows(ap, width):
             return ap.rearrange("p (i m) -> p i m", m=width)
 
-        def split(ap, width):
-            return [ap[:, c0 : c0 + width] for c0 in range(0, HALF, width)]
-
         arena = sb("arena", [P, 1280], F32)
         d_in = [sb("d_in0", [P, HALF], F32)[:], arena[:, 192:704], sb("d_in2", [P, HALF], F32)[:],
                 sb("d_in3", [P, QUARTER], F32)[:], sb("d_in4", [P, QUARTER], F32)[:]]
-        x1_c3 = [arena[:, 0:256], arena[:, 256:512], arena[:, 640:896], sb("x1_c3_last", [P, QUARTER], F32)[:]]
-        diff_a = sb("diff_a", [P, 3 * P], F32)
+        x1_late = [x1, d_in[0], arena[:, 512:1024], sb("x1_last", [P, HALF], F32)[:]]
+        x2_c3 = [arena[:, 0:256], arena[:, 256:512], x1_late[0][:, 0:QUARTER], x1_late[1][:, 0:QUARTER]]
         act_a = sb("act_a", [P, TILES * HALF], F32)
         act = [sb("act%d" % i, [P, HALF], F32) for i in range(4)]
-        res = [sb("res%d" % i, [P, HALF], F32)[:] for i in range(6)]
+        res = [sb("res%d" % i, [P, HALF], F32)[:] for i in range(8)]
 
         def finish_a(c, bank, dst):
             finish(c, 1, 0, HALF, bank, act_a[:, HALF * c : HALF * (c + 1)], dst)
@@ -342,55 +339,53 @@ def tile_list_regression_bisect_features_kernel(
                 gelu_branch(2 * g, 2, QUARTER * h, QUARTER, banks[2 * h + g],
                             rows(act_a[:], HALF)[:, 2 * g : 2 * g + 2, QUARTER * h : QUARTER * (h + 1)])
 
+        def turn_c2(t, bank):
+            turn(bank, [x1_late[t][:, 0:QUARTER], x2_c2[t][:]], QUARTER, d_rows[2], t)
+
         for h in range(2):
             turn_back(banks[6 + h], d_rows[h], 0, 2, d_in[h])
-        gather(x1_c3[3], 3, idx3, 768, QUARTER)
-        diffs = [x1[:, 0:QUARTER], x2[:, 0:QUARTER]] + split(d_in[0], QUARTER)
-        for t in range(2):
-            gather_difference(diffs[t], t, HALF, QUARTER, x1_c2[t][:])
+        gather_negated(x1_late[3], 3, HALF)
+        gather_negated(x1_late[0], 0, HALF)
         quantise_d(0, QUARTER, d_in[0])
         gelu_a(0)
         quantise_d(QUARTER, QUARTER, d_in[1])
-        for t in range(2, TILES):
-            gather_difference(diffs[t], t, HALF, QUARTER, x1_c2[t][:])
-        for t in range(TILES):
-            turn(banks[6 + t // 2][:, QUARTER * (t % 2) : QUARTER * (t % 2 + 1)], [diffs[t]], QUARTER, d_rows[2], t)
-        turn_back(banks[4], d_rows[2], 0, 2, d_in[2])
+        gather_negated(x1_late[1], 1, HALF)
+        gather_negated(x1_late[2], 2, HALF)
+        turn_c2(3, banks[6])
+        turn_c2(0, banks[7])
         gelu_a(1)
+        turn_c2(1, banks[6])
+        turn_c2(2, banks[7])
+        turn_back(banks[4], d_rows[2], 0, 2, d_in[2])
         for c in range(2):
             skip_branch(c, 1, 0, HALF, banks[c])
-        for t in range(TILES - 1):
-            gather(x1_c3[t], t, idx3, 768, QUARTER)
-        diffs = [diff_a[:, P * t : P * (t + 1)] for t in range(TILES - 1)] + [arena[:, 512:640]]
         for t in range(TILES):
-            gather_difference(diffs[t], t, 768, P, x1_c3[t][:, 0:P])
-        turn_tiles(banks[5], diffs, 0, d_rows[3])
+            gather(x2_c3[t], t, idx4, 768, QUARTER)
+        for c in range(2):
+            finish_a(c, banks[c], res[c])
         quantise_d(HALF, QUARTER, d_in[2])
-        turn_back(banks[6], d_rows[3], 0, 1, d_in[3])
+        for b in range(2):
+            x1s = [x1_late[t][:, QUARTER + P * b : QUARTER + P * (b + 1)] for t in range(TILES)]
+            x2s = [x2_c3[t][:, P * b : P * (b + 1)] for t in range(TILES)]
+            turn_tiles(banks[(5, 6)[b]], x1s, x2s, 0, d_rows[3 + b])
+        turn_back(banks[7], d_rows[3], 0, 1, d_in[3])
+        turn_back(banks[5], d_rows[4], 0, 1, d_in[4])
         for g in range(2):
             gelu_branch(2 * g, 2, HALF, QUARTER, banks[2 + g], rows(act[g][:], QUARTER))
-        diffs = split(d_in[2], P)
-        for t in range(TILES):
-            gather_difference(diffs[t], t, 896, P, x1_c3[t][:, P:QUARTER])
-        turn_tiles(banks[7], diffs[0:3], 0, d_rows[4])
-        turn_tiles(banks[4], diffs[3:4], 3, d_rows[4])
-        quantise_d(768, P, d_in[3])
-        turn_back(banks[5], d_rows[4], 0, 1, d_in[4])
-        gelu_branch(0, 4, 768, P, banks[2], rows(act[2][:], P))
-        quantise_d(896, P, d_in[4])
-        gelu_branch(0, 4, 896, P, banks[4], rows(act[3][:], P))
-        finish_a(0, banks[0], arena[:, 768:1280])
-        finish_a(1, banks[1], arena[:, 0:HALF])
         for c in range(2, TILES):
             skip_branch(c, 1, 0, HALF, banks[c - 2])
-        skip_branch(0, 2, HALF, QUARTER, banks[3])
-        skip_branch(0, 4, 768, P, banks[6])
-        skip_branch(0, 4, 896, P, banks[7])
-        finish_a(2, banks[0], res[0])
-        skip_branch(2, 2, HALF, QUARTER, banks[0])
-        finish_a(3, banks[1], res[1])
-        finish(0, 2, HALF, QUARTER, banks[3], act[0], res[2])
-        finish(2, 2, HALF, QUARTER, banks[0], act[1], res[3])
-        finish(0, 4, 768, P, banks[6], act[2], res[4])
-        finish(0, 2, 896, P, banks[7], act[3], res[5][:, 0:QUARTER])
-        finish(2, 2, 896, P, banks[7][:, QUARTER:HALF], act[3][:, QUARTER:HALF], res[5][:, QUARTER:HALF], nc.scalar)
+        quantise_d(768, P, d_in[3])
+        quantise_d(896, P, d_in[4])
+        skip_branch(0, 2, HALF, QUARTER, banks[4])
+        skip_branch(2, 2, HALF, QUARTER, banks[6])
+        gelu_branch(0, 4, 768, P, banks[2], rows(act[2][:], P))
+        gelu_branch(0, 4, 896, P, banks[3], rows(act[3][:], P))
+        skip_branch(0, 4, 768, P, banks[7])
+        skip_branch(0, 4, 896, P, banks[5])
+        finish_a(2, banks[0], res[6])
+        finish_a(3, banks[1], res[7])
+        finish(0, 2, HALF, QUARTER, banks[4], act[0], res[2])
+        finish(2, 2, HALF, QUARTER, banks[6], act[1], res[3])
+        finish(0, 4, 768, P, banks[7], act[2], res[4])
+        finish(0, 2, 896, P, banks[5], act[3], res[5][:, 0:QUARTER])
+        finish(2, 2, 896, P, banks[5][:, QUARTER:HALF], act[3][:, QUARTER:HALF], res[5][:, QUARTER:HALF], nc.scalar)

@@ -186,14 +186,10 @@ def tile_list_regression_bisect_features_kernel(
                 bank[:, 0:width].rearrange("p (b j u e) -> p b u j e", j=32, u=2, e=2),
             )
 
-        def turn_tiles(bank, x1s, x2s, t0, d_rows):
-            count = len(x1s)
-            for k, parts in enumerate((x1s, x2s)):
-                for i, part in enumerate(parts):
-                    nc.tensor.matmul(
-                        bank[:, P * i : P * (i + 1)], part, ident[:],
-                        start=(k == 0 and i == 0), stop=(k == 1 and i == count - 1), is_transpose=True,
-                    )
+        def turn_tiles(bank, diffs, t0, d_rows):
+            count = len(diffs)
+            for i, diff in enumerate(diffs):
+                nc.tensor.transpose(bank[:, P * i : P * (i + 1)], diff, ident[:])
             nc.scalar.copy(
                 d_rows[:, 0, :].rearrange("p (u t j e) -> p t u j e", u=2, t=TILES, e=2)[:, t0 : t0 + count],
                 bank[:, 0 : P * count].rearrange("p (t j u e) -> p t u j e", j=32, u=2, e=2),
@@ -360,14 +356,13 @@ def tile_list_regression_bisect_features_kernel(
         for c in range(2):
             skip_branch(c, 1, 0, HALF, banks[c])
         for t in range(TILES):
-            gather(x2_c3[t], t, idx4, 768, QUARTER)
+            nc.vector.tensor_tensor(x2_c3[t], page[t][:].indirect(idx4[:, 768 // 16 : M // 16]), x1_late[t][:, QUARTER:HALF], ADD)
         for c in range(2):
             finish_a(c, banks[c], res[c])
         quantise_d(HALF, QUARTER, d_in[2])
         for b in range(2):
-            x1s = [x1_late[t][:, QUARTER + P * b : QUARTER + P * (b + 1)] for t in range(TILES)]
             x2s = [x2_c3[t][:, P * b : P * (b + 1)] for t in range(TILES)]
-            turn_tiles(banks[(5, 6)[b]], x1s, x2s, 0, d_rows[3 + b])
+            turn_tiles(banks[(5, 6)[b]], x2s, 0, d_rows[3 + b])
         turn_back(banks[7], d_rows[3], 0, 1, d_in[3])
         turn_back(banks[5], d_rows[4], 0, 1, d_in[4])
         for g in range(2):

@@ -16,6 +16,7 @@ FP8X4 = mybir.dt.float8_e4m3fn_x4
 FP4X4 = mybir.dt.float4_e2m1fn_x4
 MULT = mybir.AluOpType.mult
 ADD = mybir.AluOpType.add
+SUBTRACT = mybir.AluOpType.subtract
 GELU = mybir.ActivationFunctionType.Gelu_apprx_tanh
 
 P = 128
@@ -173,6 +174,9 @@ def tile_list_regression_bisect_features_kernel(
         def gather(dst, t, idx, m0, width):
             nc.vector.tensor_copy(dst, page[t][:].indirect(idx[:, m0 // 16 : (m0 + width) // 16]))
 
+        def gather_difference(dst, t, m0, x1, width=256):
+            nc.vector.tensor_tensor(dst, page[t][:].indirect(idx4[:, m0 // 16 : (m0 + width) // 16]), x1, SUBTRACT)
+
         def turn(bank, parts, width, d_rows, t):
             blocks = width // P
             for i, part in enumerate(parts):
@@ -186,15 +190,6 @@ def tile_list_regression_bisect_features_kernel(
                 bank[:, 0:width].rearrange("p (b j u e) -> p b u j e", j=32, u=2, e=2),
             )
 
-        def turn_tiles(bank, diffs, t0, d_rows):
-            count = len(diffs)
-            for i, diff in enumerate(diffs):
-                nc.tensor.transpose(bank[:, P * i : P * (i + 1)], diff, ident[:])
-            nc.scalar.copy(
-                d_rows[:, 0, :].rearrange("p (u t j e) -> p t u j e", u=2, t=TILES, e=2)[:, t0 : t0 + count],
-                bank[:, 0 : P * count].rearrange("p (t j u e) -> p t u j e", j=32, u=2, e=2),
-            )
-
         def turn_back(bank, d_rows, b0, blocks, dst):
             for b in range(blocks):
                 words = d_rows[:, b0 + b, :].bitcast(F32)
@@ -206,9 +201,9 @@ def tile_list_regression_bisect_features_kernel(
                 bank[:, 0 : 2 * P * blocks].rearrange("p (b u m) -> p b m u", u=2, m=P),
             )
 
-        d_rows = [sb("d_rows%d" % i, [P, blocks, H], BF16) for i, blocks in enumerate((2, 2, 2, 1, 1))]
+        d_rows = [sb("d_rows%d" % i, [P, blocks, H], BF16) for i, blocks in enumerate((2, 2, 2, 2))]
         QUARTER = 256
-        x2_c2 = [sb("x2_c2_%d" % t, [P, QUARTER], F32) for t in range(TILES)]
+        x1_c2 = [sb("x1_c2_%d" % t, [P, QUARTER], F32) for t in range(TILES - 1)]
 
         a_first = sb("a_first", [P, S], F32)
         a_sb = a_first
@@ -252,36 +247,39 @@ def tile_list_regression_bisect_features_kernel(
             nc.gpsimd.tensor_tensor(bw, b_next[:], wgs_sb[:], MULT)
             return a_next
 
-        for t in range(TILES):
+        last = TILES - 1
+        x1_early = [shared[:, S : S + HALF], a_first[:, HALF:S], sb("x1_third", [P, HALF], F32)[:]]
+        for t in range(last):
             if t > 0:
                 nc.vector.tensor_tensor(page[t][:].indirect(idx2[:]), a_sb[:], bw, MULT)
-            if t == 0:
-                x1 = shared[:, S : S + HALF]
-            elif t == 1:
-                x1 = a_first[:, HALF:S]
-            else:
-                x1 = ring.tile([P, HALF], F32, name="x1")[:]
             x2 = ring.tile([P, HALF], F32, name="x2")[:]
-            if t < TILES - 1:
-                a_sb = first_products(t + 1)
+            a_sb = first_products(t + 1)
             if t == 0:
                 cast_w2(3, stage3)
-            gather_negated(x1, t, 0)
-            if t < TILES - 1:
-                gather(x2, t, idx4, 0, HALF)
-            else:
-                for h in range(2):
-                    gather(x2[:, QUARTER * h : QUARTER * (h + 1)], t, idx4, QUARTER * h, QUARTER)
-            gather(x2_c2[t][:], t, idx4, HALF, QUARTER)
+            gather_negated(x1_early[t], t, 0)
+            gather(x2, t, idx4, 0, HALF)
+            gather(x1_c2[t][:], t, idx3, HALF, QUARTER)
             for h in range(2):
                 cols = slice(QUARTER * h, QUARTER * (h + 1))
-                turn(banks[4 + h], [x1[:, cols], x2[:, cols]], QUARTER, d_rows[h], t)
+                turn(banks[4 + h], [x1_early[t][:, cols], x2[:, cols]], QUARTER, d_rows[h], t)
             if t == 0:
                 quantise_w2(3, stage3)
                 interleave(stage4, w4_raw[:])
-            if t == TILES - 1:
-                w4_w = keep.tile([P, N], U32, name="w4_w", tag="after_last_b", align_bytes=64)
-                nc.vector.quantize_mx(out=w4_w[:].bitcast(FP8X4), scales=w4_s[:], in_=stage4)
+
+        nc.vector.tensor_tensor(page[last][:].indirect(idx2[:]), a_sb[:], bw, MULT)
+        x1_pair = sb("x1_pair", [P, 960], F32)
+        x1_last = x1_pair[:, 448:960]
+        diff_last = [sb("diff_last%d" % h, [P, QUARTER], F32)[:] for h in range(2)]
+        for h in range(2):
+            gather(x1_last[:, QUARTER * h : QUARTER * (h + 1)], last, idx3, QUARTER * h, QUARTER)
+        for h in range(2):
+            gather_difference(diff_last[h], last, QUARTER * h, x1_last[:, QUARTER * h : QUARTER * (h + 1)])
+            turn(banks[4 + h], [diff_last[h]], QUARTER, d_rows[h], last)
+        x1_tail = x1_pair[:, 0:HALF]
+        diff_tail = sb("diff_tail", [P, HALF], F32)
+        gather(x1_tail, last, idx3, HALF, HALF)
+        w4_w = keep.tile([P, N], U32, name="w4_w", tag="after_last_b", align_bytes=64)
+        nc.vector.quantize_mx(out=w4_w[:].bitcast(FP8X4), scales=w4_s[:], in_=stage4)
 
         d_w = sb("d_w", [P, M], U32)
         d_s = sb("d_s", [P, M], U8)
@@ -318,14 +316,17 @@ def tile_list_regression_bisect_features_kernel(
         def rows(ap, width):
             return ap.rearrange("p (i m) -> p i m", m=width)
 
-        arena = sb("arena", [P, 1280], F32)
-        d_in = [sb("d_in0", [P, HALF], F32)[:], arena[:, 192:704], sb("d_in2", [P, HALF], F32)[:],
-                sb("d_in3", [P, QUARTER], F32)[:], sb("d_in4", [P, QUARTER], F32)[:]]
-        x1_late = [x1, d_in[0], arena[:, 512:1024], sb("x1_last", [P, HALF], F32)[:]]
-        x2_c3 = [arena[:, 0:256], arena[:, 256:512], x1_late[0][:, 0:QUARTER], x1_late[1][:, 0:QUARTER]]
+        res = [sb("res%d" % i, [P, HALF], F32)[:] for i in range(6)]
+        res_pair = sb("res_pair", [P, 2 * HALF], F32)
+        arena = sb("arena", [P, 3 * QUARTER], F32)
+        arena0 = sb("arena0", [P, 3 * QUARTER], F32)
+        d_in = [arena0[:, P : P + HALF], arena[:, 192:704], res_pair[:, QUARTER : 3 * QUARTER],
+                res[2][:, 0:QUARTER], res[3][:, 0:QUARTER]]
+        diff_c2 = [diff_last[0], arena0[:, 0:QUARTER], arena0[:, QUARTER:HALF], diff_tail[:, 0:QUARTER]]
+        x1_c3 = [diff_last[1], arena0[:, HALF : 3 * QUARTER], arena[:, 256:512]]
+        diff_c3 = [arena[:, 0:256], arena[:, 512:768], diff_c2[0], diff_tail[:, QUARTER:HALF]]
         act_a = sb("act_a", [P, TILES * HALF], F32)
         act = [sb("act%d" % i, [P, HALF], F32) for i in range(4)]
-        res = [sb("res%d" % i, [P, HALF], F32)[:] for i in range(8)]
 
         def finish_a(c, bank, dst):
             finish(c, 1, 0, HALF, bank, act_a[:, HALF * c : HALF * (c + 1)], dst)
@@ -336,51 +337,57 @@ def tile_list_regression_bisect_features_kernel(
                             rows(act_a[:], HALF)[:, 2 * g : 2 * g + 2, QUARTER * h : QUARTER * (h + 1)])
 
         def turn_c2(t, bank):
-            turn(bank, [x1_late[t][:, 0:QUARTER], x2_c2[t][:]], QUARTER, d_rows[2], t)
+            turn(bank, [diff_c2[t]], QUARTER, d_rows[2], t)
 
         for h in range(2):
             turn_back(banks[6 + h], d_rows[h], 0, 2, d_in[h])
-        gather_negated(x1_late[3], 3, HALF)
-        gather_negated(x1_late[0], 0, HALF)
+        gather_difference(diff_c2[0], 0, HALF, x1_c2[0][:])
+        gather_difference(diff_tail[:], last, HALF, x1_tail, HALF)
+        gather(x1_c3[0], 0, idx3, 768, QUARTER)
         quantise_d(0, QUARTER, d_in[0])
         gelu_a(0)
+        for t in (1, 2):
+            gather_difference(diff_c2[t], t, HALF, x1_c2[t][:])
         quantise_d(QUARTER, QUARTER, d_in[1])
-        gather_negated(x1_late[1], 1, HALF)
-        gather_negated(x1_late[2], 2, HALF)
+        for t in (1, 2):
+            gather(x1_c3[t], t, idx3, 768, QUARTER)
         turn_c2(3, banks[6])
         turn_c2(0, banks[7])
-        gelu_a(1)
         turn_c2(1, banks[6])
         turn_c2(2, banks[7])
-        turn_back(banks[4], d_rows[2], 0, 2, d_in[2])
+        gelu_a(1)
+        order = (3, 0, 1, 2)
+        for t in order[1:]:
+            gather_difference(diff_c3[t], t, 768, x1_c3[t])
+        for i in range(2):
+            turn(banks[6 + i], [diff_c3[order[i]]], QUARTER, d_rows[3], order[i])
+        turn_back(banks[2], d_rows[2], 0, 2, d_in[2])
+        skip_banks = [banks[0], banks[1], banks[4], banks[5]]
         for c in range(2):
-            skip_branch(c, 1, 0, HALF, banks[c])
-        for t in range(TILES):
-            nc.vector.tensor_tensor(x2_c3[t], page[t][:].indirect(idx4[:, 768 // 16 : M // 16]), x1_late[t][:, QUARTER:HALF], ADD)
+            skip_branch(c, 1, 0, HALF, skip_banks[c])
+        for i in range(2):
+            turn(banks[6 + i], [diff_c3[order[2 + i]]], QUARTER, d_rows[3], order[2 + i])
+        for c in range(2, TILES):
+            skip_branch(c, 1, 0, HALF, skip_banks[c])
         for c in range(2):
             finish_a(c, banks[c], res[c])
         quantise_d(HALF, QUARTER, d_in[2])
         for b in range(2):
-            x2s = [x2_c3[t][:, P * b : P * (b + 1)] for t in range(TILES)]
-            turn_tiles(banks[(5, 6)[b]], x2s, 0, d_rows[3 + b])
-        turn_back(banks[7], d_rows[3], 0, 1, d_in[3])
-        turn_back(banks[5], d_rows[4], 0, 1, d_in[4])
+            turn_back(banks[6 + b], d_rows[3], b, 1, d_in[3 + b])
         for g in range(2):
             gelu_branch(2 * g, 2, HALF, QUARTER, banks[2 + g], rows(act[g][:], QUARTER))
-        for c in range(2, TILES):
-            skip_branch(c, 1, 0, HALF, banks[c - 2])
         quantise_d(768, P, d_in[3])
         quantise_d(896, P, d_in[4])
-        skip_branch(0, 2, HALF, QUARTER, banks[4])
-        skip_branch(2, 2, HALF, QUARTER, banks[6])
+        skip_branch(0, 2, HALF, QUARTER, banks[0])
+        skip_branch(2, 2, HALF, QUARTER, banks[1])
         gelu_branch(0, 4, 768, P, banks[2], rows(act[2][:], P))
         gelu_branch(0, 4, 896, P, banks[3], rows(act[3][:], P))
-        skip_branch(0, 4, 768, P, banks[7])
-        skip_branch(0, 4, 896, P, banks[5])
-        finish_a(2, banks[0], res[6])
-        finish_a(3, banks[1], res[7])
-        finish(0, 2, HALF, QUARTER, banks[4], act[0], res[2])
-        finish(2, 2, HALF, QUARTER, banks[6], act[1], res[3])
-        finish(0, 4, 768, P, banks[7], act[2], res[4])
-        finish(0, 2, 896, P, banks[5], act[3], res[5][:, 0:QUARTER])
-        finish(2, 2, 896, P, banks[5][:, QUARTER:HALF], act[3][:, QUARTER:HALF], res[5][:, QUARTER:HALF], nc.scalar)
+        skip_branch(0, 4, 768, P, banks[6])
+        skip_branch(0, 4, 896, P, banks[7])
+        finish_a(2, banks[4], res_pair[:, 0:HALF])
+        finish_a(3, banks[5], res_pair[:, HALF : 2 * HALF])
+        finish(0, 2, HALF, QUARTER, banks[0], act[0], res[2])
+        finish(2, 2, HALF, QUARTER, banks[1], act[1], res[3])
+        finish(0, 4, 768, P, banks[6], act[2], res[4])
+        finish(0, 2, 896, P, banks[7], act[3], res[5][:, 0:QUARTER])
+        finish(2, 2, 896, P, banks[7][:, QUARTER:HALF], act[3][:, QUARTER:HALF], res[5][:, QUARTER:HALF], nc.scalar)

@@ -65,14 +65,12 @@ def tile_list_regression_bisect_features_kernel(
         gain_sb = sb("gain_sb", [P, TILES], F32)
         page = [sb("page%d" % t, [P, T2], F32) for t in range(TILES)]
         ident = sb("ident", [P, P], F32)
-        warm = sb("warm", [P, 8], F32)
 
         nc.vector.memset(w1_s[:].bitcast(I32), 0)
         nc.vector.memset(tab_s[0:96, :].bitcast(I32), 0)
         nc.vector.memset(v_planes[:].bitcast(I32), 0)
         nc.vector.memset(w3_s[:].bitcast(I32), 0)
         make_identity(nc, ident[:])
-        nc.scalar.activation(warm[:], ident[:, 0:8], GELU)
 
         nc.sync.dma_start(idx1[:], offs)
         nc.sync.dma_start(tab_s[96:P, :].bitcast(I32), tab_scales.bitcast(I32).rearrange("a q t -> q a t"))

@@ -166,9 +166,6 @@ def tile_list_regression_bisect_features_kernel(
                 start=(a == 0), stop=(a == 1),
             )
 
-        def gather_negated(dst, t, m0):
-            nc.vector.tensor_scalar(dst, page[t][:].indirect(idx3[:, m0 // 16 : (m0 + HALF) // 16]), -1.0, 0.0, MULT, ADD)
-
         def gather(dst, t, idx, m0, width):
             nc.vector.tensor_copy(dst, page[t][:].indirect(idx[:, m0 // 16 : (m0 + width) // 16]))
 
@@ -201,9 +198,8 @@ def tile_list_regression_bisect_features_kernel(
 
         d_rows = [sb("d_rows%d" % i, [P, blocks, H], BF16) for i, blocks in enumerate((2, 2, 2, 2))]
         QUARTER = 256
-        x1_c2 = [sb("x1_c2_%d" % t, [P, QUARTER], F32) for t in range(TILES - 1)]
 
-        a_first = sb("a_first", [P, S], F32)
+        a_first = sb("a_first", [P, S + QUARTER], F32)
         a_sb = a_first
         bw_first = sb("bw_first", [P, HALF], F32)
         for h in range(2):
@@ -213,12 +209,12 @@ def tile_list_regression_bisect_features_kernel(
             pass_b(0, h, 1)
             pass_a(0, h, 1)
             nc.scalar.copy(a_sb[:, HALF * h : HALF * (h + 1)], banks[2 * h][:])
-        shared = keep.tile([P, 2496], F32, name="shared", tag="after_first", align_bytes=64)
+        shared = keep.tile([P, 3264], F32, name="shared", tag="after_first", align_bytes=64)
         bw = shared[:, 0:S]
         stage1 = shared[:, 832:1344].bitcast(BF16)
         stage2 = shared[:, S : S + HALF].bitcast(BF16)
         stage3 = a_first[:, HALF:S].bitcast(BF16)
-        stage4 = shared[:, 1472:2496].bitcast(BF16)
+        stage4 = shared[:, 2240:3264].bitcast(BF16)
         nc.vector.tensor_tensor(bw_first[:], banks[1][:], wgs_sb[:, 0:HALF], MULT)
         nc.vector.tensor_tensor(page[0][:].indirect(idx2[:, 0:32]), a_sb[:, 0:HALF], bw_first[:], MULT)
         cast_w2(1, stage1)
@@ -246,7 +242,9 @@ def tile_list_regression_bisect_features_kernel(
             return a_next
 
         last = TILES - 1
-        x1_early = [shared[:, S : S + HALF], a_first[:, HALF:S], sb("x1_third", [P, HALF], F32)[:]]
+        x1_wide = [shared[:, S : S + 768], a_first[:, HALF : HALF + 768], sb("x1_third", [P, 768], F32)[:]]
+        x1_c2 = [wide[:, HALF:768] for wide in x1_wide]
+        x1_early = [shared[:, 1792:2304], sb("x1_negated1", [P, HALF], F32)[:], sb("x1_negated2", [P, HALF], F32)[:]]
         for t in range(last):
             if t > 0:
                 nc.vector.tensor_tensor(page[t][:].indirect(idx2[:]), a_sb[:], bw, MULT)
@@ -254,9 +252,9 @@ def tile_list_regression_bisect_features_kernel(
             a_sb = first_products(t + 1)
             if t == 0:
                 cast_w2(3, stage3)
-            gather_negated(x1_early[t], t, 0)
+            gather(x1_wide[t], t, idx3, 0, 768)
             gather(x2, t, idx4, 0, HALF)
-            gather(x1_c2[t][:], t, idx3, HALF, QUARTER)
+            nc.scalar.mul(x1_early[t], x1_wide[t][:, 0:HALF], -1.0)
             for h in range(2):
                 cols = slice(QUARTER * h, QUARTER * (h + 1))
                 turn(banks[4 + h], [x1_early[t][:, cols], x2[:, cols]], QUARTER, d_rows[h], t)
@@ -339,13 +337,13 @@ def tile_list_regression_bisect_features_kernel(
 
         for h in range(2):
             turn_back(banks[6 + h], d_rows[h], 0, 2, d_in[h])
-        gather_difference(diff_c2[0], 0, HALF, x1_c2[0][:])
+        gather_difference(diff_c2[0], 0, HALF, x1_c2[0])
         gather_difference(diff_tail[:], last, HALF, x1_tail, HALF)
         gather(x1_c3[0], 0, idx3, 768, QUARTER)
         quantise_d(0, QUARTER, d_in[0])
         gelu_a(0)
         for t in (1, 2):
-            gather_difference(diff_c2[t], t, HALF, x1_c2[t][:])
+            gather_difference(diff_c2[t], t, HALF, x1_c2[t])
         quantise_d(QUARTER, QUARTER, d_in[1])
         for t in (1, 2):
             gather(x1_c3[t], t, idx3, 768, QUARTER)

@@ -1,7 +1,6 @@
 from contextlib import ExitStack
 
 import concourse.mybir as mybir
-from concourse.masks import make_identity
 
 K, H, N, T, S, T2, M = 1024, 512, 512, 4096, 1024, 2048, 1024
 FLOPS = 2 * 2 * K * H * S + 2 * 2 * H * N * M
@@ -21,6 +20,7 @@ GELU = mybir.ActivationFunctionType.Gelu_apprx_tanh
 
 P = 128
 HALF = 512
+CHUNK = 256
 TILES = 4
 
 
@@ -31,11 +31,34 @@ def tile_list_regression_bisect_features_kernel(
     nc = tc.nc
     with ExitStack() as ctx:
         keep = ctx.enter_context(tc.tile_pool(name="keep", bufs=1))
-        ring = ctx.enter_context(tc.tile_pool(name="ring", bufs=2))
+        laid = ctx.enter_context(tc.tile_pool(name="laid", bufs=1))
         psum = ctx.enter_context(tc.psum_pool(name="psum", bufs=1))
 
         def sb(name, shape, dtype):
             return keep.tile(shape, dtype, name=name, align_bytes=64)
+
+        def at(offset, name, shape, dtype):
+            return laid.tile(shape, dtype, name=name, align_bytes=64, offset=offset)
+
+        KB = 1024
+        TAB0, TAB1, W2A = 0, 16 * KB, 32 * KB
+        TABS = W2A + 8 * KB - 64
+        PAGE0 = TABS + 4 * KB - 64
+        W4 = PAGE0 + 8 * KB
+        STAGE0 = W4 + 8 * KB - 64
+        PAGE2 = STAGE0 + 2 * KB - 64
+        W3 = PAGE2 + 8 * KB
+        W1 = W3 + 2 * KB - 64
+        STAGE1 = W1 + 2 * KB
+        A1 = STAGE1 + 2 * KB - 64
+        STAGE23 = A1 + 4 * KB
+        A2 = STAGE23 + 4 * KB - 64
+        B1 = A2 + 4 * KB
+        H12 = B1 + 4 * KB
+        B2 = H12 + 4 * KB
+        A3 = B2 + 4 * KB
+        X1_HEAD = A3 + 4 * KB
+        D_LOW = X1_HEAD + KB - 64
 
         banks = [psum.tile([P, HALF], F32, name="bank%d" % i) for i in range(8)]
 
@@ -43,347 +66,301 @@ def tile_list_regression_bisect_features_kernel(
         idx2 = keep.tile([P, S // 16], U16, name="idx2")
         idx3 = keep.tile([P, M // 16], U16, name="idx3")
         idx4 = keep.tile([P, M // 16], U16, name="idx4")
-        tab_w = [sb("tab_w%d" % a, [P, T], U32) for a in range(2)]
-        tab_s = sb("tab_s", [P, T], U8)
+        tab_w = [at((TAB0, TAB1)[a], "tab_w%d" % a, [P, T], U32) for a in range(2)]
+        tab_s = at(TABS, "tab_s", [P, T], U8)
         v_w = [sb("v_w%d" % a, [P, S], U32) for a in range(2)]
         picked_s = sb("picked_s", [P, S], U8)
         v_planes = sb("v_planes", [P, 2 * S], U8)
-        v_s = [v_planes[:, S * a : S * (a + 1)] for a in range(2)]
-        w1_first = keep.tile([P, 2 * 2 * P], U8, name="w1_first", tag="after_first", align_bytes=64)
-        w1_rest = sb("w1_rest", [P, 2 * 6 * P], U8)
+        w1_raw = at(W1, "w1_raw", [P, 2 * 2 * H], U8)
+        w1_w = sb("w1_w", [P, 2 * 2 * H], U8)
+        w1_raw_s = sb("w1_raw_s", [P, 2 * H], U8)
         w1_s = sb("w1_s", [P, 2 * H], U8)
-        w3_w = sb("w3_w", [P, N], U32)
-        w3_s = sb("w3_s", [P, N], U8)
-        w2_first = [sb("w2_first%d" % a, [P, 4, P], F32) for a in range(2)]
-        w2_second = [sb("w2_second%d" % a, [P, 4, P], F32) for a in range(2)]
-        w2_rest = [sb("w2_rest%d" % a, [P, 4, 2 * P], F32) for a in range(2)]
-        w2_w = sb("w2_w", [P, TILES * 2 * P], U32)
-        w2_s = sb("w2_s", [P, TILES * 2 * P], U8)
-        w4_raw = sb("w4_raw", [P, 4, N], F32)
+        w3_w = at(W3, "w3_w", [P, N], U32)
+        w3_s = at(W1 + 64, "w3_s", [P, N], U8)
+        gain_sb = at(W1 + KB, "gain_sb", [P, TILES], F32)
+        w2_raw = [at((W2A, TAB0)[g], "w2_raw%d" % g, [P, 2 * 4 * 2 * P], F32) for g in range(2)]
+        w4_raw = at(W4, "w4_raw", [P, 4, N], F32)
+        stage = [at((STAGE0, STAGE1)[t], "stage%d" % t, [P, 2 * HALF], BF16) for t in range(2)]
+        stage_high = at(STAGE23, "stage_high", [P, 4 * HALF], BF16)
+        stage4 = at(B1, "stage4", [P, 4 * N], BF16)
+        low_w = sb("low_w", [P, 4 * P], U32)
+        low_s = sb("low_s", [P, 4 * P], U8)
+        high_w = sb("high_w", [P, 4 * P], U32)
+        high_s = sb("high_s", [P, 4 * P], U8)
+        w4_w = at(H12, "w4_w", [P, N], U32)
         w4_s = sb("w4_s", [P, N], U8)
-        wgs_sb = sb("wgs_sb", [P, S], F32)
-        gain_sb = sb("gain_sb", [P, TILES], F32)
-        page = [sb("page%d" % t, [P, T2], F32) for t in range(TILES)]
-        ident = sb("ident", [P, P], F32)
+        wgs_low = [at((TABS + 64, TAB0 + 8 * KB)[h], "wgs_low%d" % h, [P, HALF], F32) for h in range(2)]
+        wgs_high = at(TAB1 + 8 * KB, "wgs_high", [P, 2 * S], F32)
+        page = [at((PAGE0, TAB1, PAGE2, W2A)[t], "page%d" % t, [P, T2], F32) for t in range(TILES)]
 
-        nc.vector.memset(w1_s[:].bitcast(I32), 0)
+        nc.vector.memset(w1_raw_s[:].bitcast(I32), 0)
         nc.vector.memset(tab_s[0:96, :].bitcast(I32), 0)
         nc.vector.memset(v_planes[:].bitcast(I32), 0)
-        nc.vector.memset(w3_s[:].bitcast(I32), 0)
-        make_identity(nc, ident[:])
+
+        w2_rows = w2.rearrange("(a p j) c -> a p j c", a=2, j=4)
+        tab_rows = [tab_words[a].rearrange("p t i -> p (t i)").bitcast(I32) for a in range(2)]
+        wgs_rows = wgs.rearrange("(p i) j -> p i j", i=4)
+        page_low = page0.rearrange("(g p i) t -> g p i t", g=2, i=4)
+        page_high = page0.rearrange("(p i) t -> i p t", i=4)
+
+        w2_view = [raw[:].rearrange("p (a j c) -> p a j c", a=2, j=4) for raw in w2_raw]
+
+        def load_wgs_low(h, g):
+            nc.sync.dma_start(wgs_low[h][64 * g : 64 * (g + 1), :], wgs_rows[:, 0:2, HALF * h : HALF * (h + 1)])
+
+        def load_w2(g, a):
+            nc.sync.dma_start(w2_view[g][:, a], w2_rows[a, :, :, 2 * P * g : 2 * P * (g + 1)])
 
         nc.sync.dma_start(idx1[:], offs)
         nc.sync.dma_start(tab_s[96:P, :].bitcast(I32), tab_scales.bitcast(I32).rearrange("a q t -> q a t"))
-        w2_rows = w2.rearrange("(a p j) c -> a p j c", a=2, j=4)
-        w1_rows = w1_words.bitcast(I32).rearrange("a p c -> p a c")
-        tab_rows = [tab_words[a].rearrange("p t i -> p (t i)").bitcast(I32) for a in range(2)]
         nc.sync.dma_start(tab_w[0][:].bitcast(I32), tab_rows[0])
-        for a in range(2):
-            nc.sync.dma_start(w2_first[a][:], w2_rows[a, :, :, 0:P])
-        for q in range(4):
-            nc.gpsimd.dma_start(
-                w1_s[32 * q : 32 * q + 4, :].bitcast(I32).rearrange("r (a c) -> r a c", a=2),
-                w1_scales[:, 4 * q : 4 * q + 4, :].bitcast(I32).rearrange("a r c -> r a c"),
-            )
-        nc.sync.dma_start(tab_w[1][:].bitcast(I32), tab_rows[1])
-        nc.sync.dma_start(w1_first[:].bitcast(I32).rearrange("p (a c) -> p a c", a=2), w1_rows[:, :, 0 : P // 2])
-        nc.sync.dma_start(wgs_sb[:, 0:HALF], wgs[:, 0:HALF])
         nc.sync.dma_start(idx2[:], offs2)
-        nc.sync.dma_start(page[0][:], page0[0:P, :])
-        nc.sync.dma_start(wgs_sb[:, HALF:S], wgs[:, HALF:S])
-        for a in range(2):
-            nc.sync.dma_start(w2_second[a][:], w2_rows[a, :, :, P : 2 * P])
-        nc.sync.dma_start(w1_rest[:].bitcast(I32).rearrange("p (a c) -> p a c", a=2), w1_rows[:, :, P // 2 : 2 * P])
-        for a in range(2):
-            nc.sync.dma_start(w2_rest[a][:], w2_rows[a, :, :, 2 * P : H])
         nc.sync.dma_start(idx3[:], offs3)
         nc.sync.dma_start(idx4[:], offs4)
-        nc.sync.dma_start(page[1][:], page0[P : 2 * P, :])
-        nc.sync.dma_start(w4_raw[:], w4.rearrange("(p j) n -> p j n", j=4))
-        nc.sync.dma_start(page[2][:], page0[2 * P : 3 * P, :])
-        nc.sync.dma_start(w3_w[:].bitcast(I32), w3_words[0].rearrange("p n i -> p (n i)").bitcast(I32))
-        for q in range(4):
-            nc.sync.dma_start(
-                w3_s[32 * q : 32 * q + 4, :].bitcast(I32),
-                w3_scales[0, 4 * q : 4 * q + 4, :].bitcast(I32),
-            )
-        with nc.allow_non_contiguous_dma(reason="one gain value to each partition"):
-            nc.sync.dma_start(gain_sb[:], gain.rearrange("(c p) -> p c", p=P))
-        nc.sync.dma_start(page[TILES - 1][:], page0[P * (TILES - 1) : P * TILES, :])
-
-        def interleave(dst, src):
-            nc.scalar.copy(
-                dst.rearrange("p (c j) -> p c j", j=4),
-                src.rearrange("p j c -> p c j"),
-            )
-
-        def cast_w2(t, stage):
-            for a in range(2):
-                src = [w2_first[a][:], w2_second[a][:], w2_rest[a][:, :, 0:P], w2_rest[a][:, :, P : 2 * P]][t]
-                interleave(stage[:, HALF * a : HALF * (a + 1)], src)
-
-        def quantise_w2(t, stage):
-            cols = slice(2 * P * t, 2 * P * (t + 1))
-            nc.vector.quantize_mx(out=w2_w[:, cols].bitcast(FP8X4), scales=w2_s[:, cols], in_=stage)
-
-        nc.vector.tensor_copy(picked_s[:], tab_s[:].indirect(idx1[:]))
+        nc.sync.dma_start(w1_raw[:].bitcast(I32).rearrange("p (a c) -> p a c", a=2), w1_words.bitcast(I32).rearrange("a p c -> p a c"))
+        nc.sync.dma_start(tab_w[1][:].bitcast(I32), tab_rows[1])
         for q in range(4):
             nc.gpsimd.dma_start(
+                w1_raw_s[32 * q : 32 * q + 4, :].bitcast(I32).rearrange("r (a c) -> r a c", a=2),
+                w1_scales[:, 4 * q : 4 * q + 4, :].bitcast(I32).rearrange("a r c -> r a c"),
+            )
+        nc.vector.tensor_copy(picked_s[:], tab_s[:].indirect(idx1[:]))
+        for q in range(4):
+            nc.sync.dma_start(
                 v_planes[32 * q : 32 * q + 4, :].bitcast(I32).rearrange("r (a c) -> r a c", a=2),
                 picked_s[96 + 8 * q : 96 + 8 * (q + 1), :].bitcast(I32),
             )
+        for a in range(2):
+            load_w2(0, a)
+        for g in range(2):
+            load_wgs_low(0, g)
+        nc.sync.dma_start(page[0][:], page_low[0, :, 0:2, :])
         nc.vector.tensor_copy(v_w[0][:], tab_w[0][:].indirect(idx1[:]))
-        stage0 = sb("stage0", [P, 2 * HALF], BF16)
-        cast_w2(0, stage0[:])
-        quantise_w2(0, stage0[:])
+        for a in range(2):
+            load_w2(1, a)
+        for g in range(2):
+            load_wgs_low(1, g)
+
+        nc.vector.tensor_copy(
+            w1_w[:].bitcast(I32).rearrange("p (a c) -> p a c", a=2)[:, :, 0:P],
+            w1_raw[:].bitcast(I32).rearrange("p (a c u) -> p a c u", a=2, u=2)[:, :, :, 0],
+        )
+        nc.gpsimd.tensor_copy(
+            w1_s[:].rearrange("p (a c) -> p a c", a=2)[:, :, 0 : 2 * P].rearrange("p a (c i) -> p a c i", i=2),
+            w1_raw_s[:].rearrange("p (a c i) -> p a c i", a=2, i=4)[:, :, :, 0:2],
+        )
+        nc.vector.tensor_copy(
+            w1_w[:].bitcast(U16).rearrange("p (a t c) -> p a t c", a=2, t=4)[:, :, 2:4, :],
+            w1_raw[:].bitcast(U16).rearrange("p (a c i) -> p a i c", a=2, i=4)[:, :, 2:4, :],
+        )
+        nc.gpsimd.tensor_copy(
+            w1_s[:].rearrange("p (a t c) -> p a t c", a=2, t=4)[:, :, 2:4, :],
+            w1_raw_s[:].rearrange("p (a c i) -> p a i c", a=2, i=4)[:, :, 2:4, :],
+        )
+        nc.sync.dma_start(w3_w[:].bitcast(I32), w3_words[0].rearrange("p n i -> p (n i)").bitcast(I32))
+        nc.gpsimd.memset(w3_s[:].bitcast(I32), 0)
+        for q in range(4):
+            nc.sync.dma_start(w3_s[32 * q : 32 * q + 4, :].bitcast(I32), w3_scales[0, 4 * q : 4 * q + 4, :].bitcast(I32))
+        with nc.allow_non_contiguous_dma(reason="one gain value to each partition"):
+            nc.sync.dma_start(gain_sb[:], gain.rearrange("(c p) -> p c", p=P))
         for h in range(2):
             nc.vector.tensor_copy(v_w[1][:, HALF * h : HALF * (h + 1)], tab_w[1][:].indirect(idx1[:, 32 * h : 32 * (h + 1)]))
+        nc.sync.dma_start(page[1][:], page_low[1, :, 0:2, :])
+        for g in range(4):
+            nc.sync.dma_start(wgs_high[32 * g : 32 * (g + 1), :].rearrange("p (i j) -> p i j", i=2), wgs_rows[:, 2:4, :])
+
+        def cast_low(t, a):
+            nc.scalar.copy(
+                stage[t][:, HALF * a : HALF * (a + 1)].rearrange("p (c i j) -> p c i j", i=2, j=4),
+                w2_view[t][:, a].rearrange("p j (c i) -> p c i j", i=4)[:, :, 0:2, :],
+            )
+
+        def cast_high(g):
+            nc.scalar.copy(
+                stage_high[:].rearrange("p (t a g c j) -> p g a c t j", t=2, a=2, g=2, j=4)[:, g],
+                w2_view[g].rearrange("p a j (c i) -> p a c i j", i=4)[:, :, :, 2:4, :],
+            )
+
+        def quantise(codes, scales, c0, src):
+            width = src.shape[1] // 4
+            nc.vector.quantize_mx(out=codes[:, c0 : c0 + width].bitcast(FP8X4), scales=scales[:, c0 : c0 + width], in_=src)
+
+        def mx(dst, w, w_scale, x, x_scale, start, stop):
+            nc.tensor.matmul_mx(out=dst, lhsT=w, lhsT_scale=w_scale, rhs=x, rhs_scale=x_scale, start=start, stop=stop)
+
+        def bank_a(t, h):
+            return banks[((0, 2), (1, 3), (4, 5), (1, 3))[t][h]]
+
+        def bank_b(t, h):
+            return banks[((1, 3), (4, 5), (0, 2), (6, 7))[t][h]]
 
         def pass_b(t, h, a):
-            cols = slice(HALF * h, HALF * (h + 1))
-            nc.tensor.matmul_mx(
-                out=banks[2 * h + 1][:],
-                lhsT=w2_w[:, P * (2 * t + a) : P * (2 * t + a + 1)].bitcast(FP8X4),
-                lhsT_scale=w2_s[:, P * (2 * t + a) : P * (2 * t + a + 1)],
-                rhs=v_w[a][:, cols].bitcast(FP8X4),
-                rhs_scale=v_s[a][:, cols],
-                start=(a == 0), stop=(a == 1),
-            )
+            codes, scales = (low_w, low_s) if t < 2 else (high_w, high_s)
+            c0 = P * (2 * (t % 2) + a)
+            mx(bank_b(t, h)[:], codes[:, c0 : c0 + P].bitcast(FP8X4), scales[:, c0 : c0 + P],
+               v_w[a][:, HALF * h : HALF * (h + 1)].bitcast(FP8X4), v_planes[:, S * a + HALF * h : S * a + HALF * (h + 1)], a == 0, a == 1)
 
         def pass_a(t, h, a):
-            cols = slice(HALF * h, HALF * (h + 1))
             c0 = H * a + P * t
-            if t == 0:
-                w1_codes = w1_first[:, 2 * P * a : 2 * P * (a + 1)]
+            mx(bank_a(t, h)[:], w1_w[:, 2 * c0 : 2 * (c0 + P)].bitcast(FP4X4), w1_s[:, c0 : c0 + P],
+               v_w[a][:, HALF * h : HALF * (h + 1)].bitcast(FP8X4), v_planes[:, S * a + HALF * h : S * a + HALF * (h + 1)], a == 0, a == 1)
+
+        a_sb = [sb("a_first", [P, HALF], F32)] + [at(A1, "a_sb1", [P, S], F32), at(A2, "a_sb2", [P, S], F32), at(A3, "a_sb3", [P, S], F32)]
+        b_sb = [None, at(B1, "b_sb1", [P, S], F32), at(B2, "b_sb2", [P, S], F32), sb("b_sb3", [P, S], F32)]
+        bw_high = sb("bw_high", [P, S], F32)
+        bw = [sb("bw0", [P, S], F32), sb("bw1", [P, S], F32), bw_high, bw_high]
+        h_both = at(H12, "h_both", [P, S], F32)
+        h_sb = [at(STAGE23, "h_first", [P, HALF], F32), h_both, h_both, sb("h_last", [P, S], F32)]
+        x1 = [sb("x1_%d" % t, [P, M], F32) for t in range(2)]
+        x2 = [sb("x2_%d" % t, [P, M], F32) for t in range(2)]
+        rounded = [at((B2, A3)[t], "rounded%d" % t, [P, M], BF16) for t in range(2)]
+
+        for a in range(2):
+            cast_low(0, a)
+            quantise(low_w, low_s, P * a, stage[0][:, HALF * a : HALF * (a + 1)])
+        nc.sync.dma_start(w4_raw[:], w4.rearrange("(p j) n -> p j n", j=4))
+        nc.sync.dma_start(page[2][:], page_high[2])
+        for h in range(2):
+            pass_a(0, h, 0)
+            pass_b(0, h, 0)
+            pass_a(0, h, 1)
+            pass_b(0, h, 1)
+        nc.scalar.copy(a_sb[0][:], bank_a(0, 0)[:])
+        nc.vector.tensor_tensor(bw[0][:, 0:HALF], bank_b(0, 0)[:], wgs_low[0][:], MULT)
+        nc.vector.tensor_tensor(page[0][:].indirect(idx2[:, 0:32]), a_sb[0][:], bw[0][:, 0:HALF], MULT)
+        cast_high(0)
+        nc.sync.dma_start(page[3][:], page_high[3])
+        for a in range(2):
+            cast_low(1, a)
+        cast_high(1)
+        nc.vector.tensor_tensor(bw[0][:, HALF:S], bank_b(0, 1)[:], wgs_low[1][:], MULT)
+        quantise(low_w, low_s, 2 * P, stage[1][:])
+        quantise(high_w, high_s, 0, stage_high[:])
+        nc.vector.tensor_tensor(h_sb[0][:], bank_a(0, 1)[:], bw[0][:, HALF:S], MULT)
+        nc.vector.tensor_copy(page[0][:].indirect(idx2[:, 32:64]), h_sb[0][:])
+
+        def first_products(t):
+            for h in range(2):
+                for a in range(2):
+                    pass_b(t, h, a)
+                nc.scalar.copy(b_sb[t][:, HALF * h : HALF * (h + 1)], bank_b(t, h)[:])
+            for h in range(2):
+                for a in range(2):
+                    pass_a(t, h, a)
+                nc.scalar.copy(a_sb[t][:, HALF * h : HALF * (h + 1)], bank_a(t, h)[:])
+
+        def weigh(t):
+            if t < 2:
+                for h in range(2):
+                    cols = slice(HALF * h, HALF * (h + 1))
+                    nc.gpsimd.tensor_tensor(bw[t][:, cols], b_sb[t][:, cols], wgs_low[h][:], MULT)
             else:
-                w1_codes = w1_rest[:, 2 * P * (3 * a + t - 1) : 2 * P * (3 * a + t)]
-            nc.tensor.matmul_mx(
-                out=banks[2 * h][:],
-                lhsT=w1_codes.bitcast(FP4X4),
-                lhsT_scale=w1_s[:, c0 : c0 + P],
-                rhs=v_w[a][:, cols].bitcast(FP8X4),
-                rhs_scale=v_s[a][:, cols],
-                start=(a == 0), stop=(a == 1),
-            )
+                nc.gpsimd.tensor_tensor(bw[t][:, 0:S], b_sb[t][:], wgs_high[:, S * (t - 2) : S * (t - 1)], MULT)
+
+        def join(t):
+            nc.gpsimd.tensor_tensor(h_sb[t][:], a_sb[t][:], bw[t][:], MULT)
+
+        def scatter(t):
+            nc.vector.tensor_copy(page[t][:].indirect(idx2[:]), h_sb[t][:])
 
         def gather(dst, t, idx, m0, width):
             nc.vector.tensor_copy(dst, page[t][:].indirect(idx[:, m0 // 16 : (m0 + width) // 16]))
 
-        def gather_difference(dst, t, m0, x1, width=256):
-            nc.vector.tensor_tensor(dst, page[t][:].indirect(idx4[:, m0 // 16 : (m0 + width) // 16]), x1, SUBTRACT)
+        def gather_difference(dst, t, m0, width, first):
+            nc.vector.tensor_tensor(dst, page[t][:].indirect(idx4[:, m0 // 16 : (m0 + width) // 16]), first, SUBTRACT)
 
-        def turn(bank, parts, width, d_rows, t):
-            blocks = width // P
-            for i, part in enumerate(parts):
-                for b in range(blocks):
-                    nc.tensor.matmul(
-                        bank[:, P * b : P * (b + 1)], part[:, P * b : P * (b + 1)], ident[:],
-                        start=(i == 0 and b == 0), stop=(i == len(parts) - 1 and b == blocks - 1), is_transpose=True,
-                    )
-            nc.scalar.copy(
-                d_rows[:].rearrange("p b (u t j e) -> p t b u j e", u=2, t=TILES, e=2)[:, t],
-                bank[:, 0:width].rearrange("p (b j u e) -> p b u j e", j=32, u=2, e=2),
-            )
+        d_low = at(D_LOW, "d_low", [P, 2, M], BF16)
+        d_in = sb("d_in", [P, 4 * M], BF16)
+        d_cols = d_in[:].rearrange("p (m i) -> p m i", i=4)
 
-        def turn_back(bank, d_rows, b0, blocks, dst):
-            for b in range(blocks):
-                words = d_rows[:, b0 + b, :].bitcast(F32)
-                for u in range(2):
-                    c0 = P * (2 * b + u)
-                    nc.tensor.transpose(bank[:, c0 : c0 + P], words[:, P * u : P * (u + 1)], ident[:])
-            nc.scalar.copy(
-                dst.rearrange("p (b m u) -> p b m u", u=2, m=P),
-                bank[:, 0 : 2 * P * blocks].rearrange("p (b u m) -> p b m u", u=2, m=P),
-            )
+        def low_difference(t):
+            nc.gpsimd.tensor_tensor(rounded[t][:], x2[t][:, 0:M], x1[t][:], SUBTRACT)
+            nc.sync.dma_start(d_low[64 * t : 64 * (t + 1), :, :], rounded[t][:])
 
-        d_rows = [sb("d_rows%d" % i, [P, blocks, H], BF16) for i, blocks in enumerate((2, 2, 2, 2))]
-        QUARTER = 256
+        for t in (1, 2, 3):
+            first_products(t)
+        weigh(1)
+        join(1)
+        nc.scalar.copy(stage4[:].rearrange("p (c j) -> p c j", j=4), w4_raw[:].rearrange("p j c -> p c j"))
+        gather(x1[0][:], 0, idx3, 0, M)
+        gather(x2[0][:], 0, idx4, 0, M)
+        scatter(1)
+        gather(x1[1][:], 1, idx3, 0, M)
+        gather(x2[1][:], 1, idx4, 0, M)
+        weigh(2)
+        low_difference(0)
+        join(2)
+        weigh(3)
+        join(3)
+        low_difference(1)
+        nc.scalar.copy(d_cols[:, :, 0:2], d_low[:].rearrange("p i m -> p m i"))
+        for t in (2, 3):
+            scatter(t)
+        quantise(w4_w, w4_s, 0, stage4[:])
 
-        a_first = sb("a_first", [P, S + QUARTER], F32)
-        a_sb = a_first
-        bw_first = sb("bw_first", [P, HALF], F32)
-        for h in range(2):
-            pass_b(0, h, 0)
-            pass_a(0, h, 0)
-        for h in range(2):
-            pass_b(0, h, 1)
-            pass_a(0, h, 1)
-            nc.scalar.copy(a_sb[:, HALF * h : HALF * (h + 1)], banks[2 * h][:])
-        shared = keep.tile([P, 3264], F32, name="shared", tag="after_first", align_bytes=64)
-        bw = shared[:, 0:S]
-        stage1 = shared[:, 832:1344].bitcast(BF16)
-        stage2 = shared[:, S : S + HALF].bitcast(BF16)
-        stage3 = a_first[:, HALF:S].bitcast(BF16)
-        stage4 = shared[:, 2240:3264].bitcast(BF16)
-        nc.vector.tensor_tensor(bw_first[:], banks[1][:], wgs_sb[:, 0:HALF], MULT)
-        nc.vector.tensor_tensor(page[0][:].indirect(idx2[:, 0:32]), a_sb[:, 0:HALF], bw_first[:], MULT)
-        cast_w2(1, stage1)
-        quantise_w2(1, stage1)
-        nc.vector.tensor_tensor(bw[:, HALF:S], banks[3][:], wgs_sb[:, HALF:S], MULT)
-        nc.vector.tensor_tensor(page[0][:].indirect(idx2[:, 32:64]), a_sb[:, HALF:S], bw[:, HALF:S], MULT)
-        cast_w2(2, stage2)
-        quantise_w2(2, stage2)
-
-        def first_products(t):
-            a_next = ring.tile([P, S], F32, name="a_next")
-            if t < TILES - 1:
-                b_next = ring.tile([P, S], F32, name="b_next")
-            else:
-                b_next = keep.tile([P, S], F32, name="b_last", tag="after_last_b", align_bytes=64)
-            for h in range(2):
-                for a in range(2):
-                    pass_b(t, h, a)
-                nc.scalar.copy(b_next[:, HALF * h : HALF * (h + 1)], banks[2 * h + 1][:])
-            for h in range(2):
-                for a in range(2):
-                    pass_a(t, h, a)
-                nc.scalar.copy(a_next[:, HALF * h : HALF * (h + 1)], banks[2 * h][:])
-            nc.gpsimd.tensor_tensor(bw, b_next[:], wgs_sb[:], MULT)
-            return a_next
-
-        last = TILES - 1
-        x1_wide = [shared[:, S : S + 768], a_first[:, HALF : HALF + 768], sb("x1_third", [P, 768], F32)[:]]
-        x1_c2 = [wide[:, HALF:768] for wide in x1_wide]
-        x1_early = [shared[:, 1792:2304], sb("x1_negated1", [P, HALF], F32)[:], sb("x1_negated2", [P, HALF], F32)[:]]
-        for t in range(last):
-            if t > 0:
-                nc.vector.tensor_tensor(page[t][:].indirect(idx2[:]), a_sb[:], bw, MULT)
-            x2 = ring.tile([P, HALF], F32, name="x2")[:]
-            a_sb = first_products(t + 1)
-            if t == 0:
-                cast_w2(3, stage3)
-            gather(x1_wide[t], t, idx3, 0, 768)
-            gather(x2, t, idx4, 0, HALF)
-            nc.scalar.mul(x1_early[t], x1_wide[t][:, 0:HALF], -1.0)
-            for h in range(2):
-                cols = slice(QUARTER * h, QUARTER * (h + 1))
-                turn(banks[4 + h], [x1_early[t][:, cols], x2[:, cols]], QUARTER, d_rows[h], t)
-            if t == 0:
-                quantise_w2(3, stage3)
-                interleave(stage4, w4_raw[:])
-
-        nc.vector.tensor_tensor(page[last][:].indirect(idx2[:]), a_sb[:], bw, MULT)
-        x1_pair = sb("x1_pair", [P, 960], F32)
-        x1_last = x1_pair[:, 448:960]
-        diff_last = [sb("diff_last%d" % h, [P, QUARTER], F32)[:] for h in range(2)]
-        for h in range(2):
-            gather(x1_last[:, QUARTER * h : QUARTER * (h + 1)], last, idx3, QUARTER * h, QUARTER)
-        for h in range(2):
-            gather_difference(diff_last[h], last, QUARTER * h, x1_last[:, QUARTER * h : QUARTER * (h + 1)])
-            turn(banks[4 + h], [diff_last[h]], QUARTER, d_rows[h], last)
-        x1_tail = x1_pair[:, 0:HALF]
-        diff_tail = sb("diff_tail", [P, HALF], F32)
-        gather(x1_tail, last, idx3, HALF, HALF)
-        w4_w = keep.tile([P, N], U32, name="w4_w", tag="after_last_b", align_bytes=64)
-        nc.vector.quantize_mx(out=w4_w[:].bitcast(FP8X4), scales=w4_s[:], in_=stage4)
-
+        act = at(TAB0, "act", [P, TILES * 4 * CHUNK], F32)
+        res = sb("res", [P, TILES * 4 * CHUNK], F32)
         d_w = sb("d_w", [P, M], U32)
         d_s = sb("d_s", [P, M], U8)
-        def quantise_d(m0, width, src):
-            nc.vector.quantize_mx(out=d_w[:, m0 : m0 + width].bitcast(FP8X4), scales=d_s[:, m0 : m0 + width], in_=src.bitcast(BF16))
-
-        def second_product(dst, w_w, w_s, c, m0, width):
-            nc.tensor.matmul_mx(
-                out=dst,
-                lhsT=w_w[:, P * c : P * (c + 1)].bitcast(FP8X4),
-                lhsT_scale=w_s[:, P * c : P * (c + 1)],
-                rhs=d_w[:, m0 : m0 + width].bitcast(FP8X4),
-                rhs_scale=d_s[:, m0 : m0 + width],
-                start=True, stop=True,
-            )
-
+        high = sb("high", [P, 7 * CHUNK], F32)
+        x1_head = at(X1_HEAD, "x1_head", [P, CHUNK], F32)
+        d_high = [high[:, CHUNK : 3 * CHUNK], high[:, 3 * CHUNK : 5 * CHUNK], high[:, 5 * CHUNK : 7 * CHUNK], act[:, 2 * CHUNK : 4 * CHUNK]]
+        x1_two = at(D_LOW + 64, "x1_two", [P, M], F32)
+        x1_three = [x1_head[:]] + [high[:, CHUNK * c : CHUNK * (c + 1)] for c in range(3)]
         out_tiles = out.rearrange("(c p) m -> p c m", p=P)
 
-        def gelu_branch(c0, count, m0, width, bank, act):
-            for i in range(count):
-                second_product(bank[:, width * i : width * (i + 1)], w3_w, w3_s, c0 + i, m0, width)
-            nc.scalar.activation(act, bank[:, 0 : width * count].rearrange("p (i m) -> p i m", m=width), GELU)
+        def high_difference(c, t):
+            first = x1_two[:, CHUNK * c : CHUNK * (c + 1)] if t == 2 else x1_three[c]
+            gather_difference(d_high[c][:, CHUNK * (t - 2) : CHUNK * (t - 1)], t, CHUNK * c, CHUNK, first)
 
-        def skip_branch(c0, count, m0, width, bank):
-            for i in range(count):
-                second_product(bank[:, width * i : width * (i + 1)], w4_w, w4_s, c0 + i, m0, width)
+        def round_high(c):
+            nc.scalar.copy(d_cols[:, CHUNK * c : CHUNK * (c + 1), 2:4], d_high[c].rearrange("p (i m) -> p m i", i=2))
 
-        def finish(c0, count, m0, width, skip_bank, act, res, queue=nc.sync):
-            for i in range(count):
-                cols = slice(width * i, width * (i + 1))
-                nc.vector.scalar_tensor_tensor(res[:, cols], act[:, cols], gain_sb[:, c0 + i : c0 + i + 1], skip_bank[:, cols], MULT, ADD)
-            queue.dma_start(out_tiles[:, c0 : c0 + count, m0 : m0 + width], res.rearrange("p (i m) -> p i m", m=width))
-
-        def rows(ap, width):
-            return ap.rearrange("p (i m) -> p i m", m=width)
-
-        res = [sb("res%d" % i, [P, HALF], F32)[:] for i in range(6)]
-        res_pair = sb("res_pair", [P, 2 * HALF], F32)
-        arena = sb("arena", [P, 3 * QUARTER], F32)
-        arena0 = sb("arena0", [P, 3 * QUARTER], F32)
-        d_in = [arena0[:, P : P + HALF], arena[:, 192:704], res_pair[:, QUARTER : 3 * QUARTER],
-                res[2][:, 0:QUARTER], res[3][:, 0:QUARTER]]
-        diff_c2 = [diff_last[0], arena0[:, 0:QUARTER], arena0[:, QUARTER:HALF], diff_tail[:, 0:QUARTER]]
-        x1_c3 = [diff_last[1], arena0[:, HALF : 3 * QUARTER], arena[:, 256:512]]
-        diff_c3 = [arena[:, 0:256], arena[:, 512:768], diff_c2[0], diff_tail[:, QUARTER:HALF]]
-        act_a = sb("act_a", [P, TILES * HALF], F32)
-        act = [sb("act%d" % i, [P, HALF], F32) for i in range(4)]
-
-        def finish_a(c, bank, dst):
-            finish(c, 1, 0, HALF, bank, act_a[:, HALF * c : HALF * (c + 1)], dst)
-
-        def gelu_a(h):
+        def second_products(c):
+            cols = slice(CHUNK * c, CHUNK * (c + 1))
+            quantise(d_w, d_s, CHUNK * c, d_in[:, 4 * CHUNK * c : 4 * CHUNK * (c + 1)])
+            first_bank = 4 * (c % 2)
             for g in range(2):
-                gelu_branch(2 * g, 2, QUARTER * h, QUARTER, banks[2 * h + g],
-                            rows(act_a[:], HALF)[:, 2 * g : 2 * g + 2, QUARTER * h : QUARTER * (h + 1)])
+                for i in range(2):
+                    n = 2 * g + i
+                    mx(banks[first_bank + g][:, CHUNK * i : CHUNK * (i + 1)], w3_w[:, P * n : P * (n + 1)].bitcast(FP8X4), w3_s[:, P * n : P * (n + 1)],
+                       d_w[:, cols].bitcast(FP8X4), d_s[:, cols], True, True)
+                nc.scalar.activation(act[:, CHUNK * (4 * c + 2 * g) : CHUNK * (4 * c + 2 * g + 2)], banks[first_bank + g][:], GELU)
+            for n in range(TILES):
+                c0 = P * n
+                mx(banks[first_bank + 2 + n // 2][:, CHUNK * (n % 2) : CHUNK * (n % 2 + 1)], w4_w[:, c0 : c0 + P].bitcast(FP8X4), w4_s[:, c0 : c0 + P],
+                   d_w[:, cols].bitcast(FP8X4), d_s[:, cols], True, True)
 
-        def turn_c2(t, bank):
-            turn(bank, [diff_c2[t]], QUARTER, d_rows[2], t)
+        def finish(c):
+            for g in range(2):
+                for i in range(2):
+                    n = 2 * g + i
+                    cols = slice(CHUNK * (4 * c + n), CHUNK * (4 * c + n + 1))
+                    nc.vector.scalar_tensor_tensor(res[:, cols], act[:, cols], gain_sb[:, n : n + 1],
+                                                   banks[4 * (c % 2) + 2 + g][:, CHUNK * i : CHUNK * (i + 1)], MULT, ADD)
+                queue = nc.scalar if (c, g) == (3, 1) else nc.sync
+                queue.dma_start(out_tiles[:, 2 * g : 2 * g + 2, CHUNK * c : CHUNK * (c + 1)],
+                                res[:, CHUNK * (4 * c + 2 * g) : CHUNK * (4 * c + 2 * g + 2)].rearrange("p (i m) -> p i m", i=2))
 
-        for h in range(2):
-            turn_back(banks[6 + h], d_rows[h], 0, 2, d_in[h])
-        gather_difference(diff_c2[0], 0, HALF, x1_c2[0])
-        gather_difference(diff_tail[:], last, HALF, x1_tail, HALF)
-        gather(x1_c3[0], 0, idx3, 768, QUARTER)
-        quantise_d(0, QUARTER, d_in[0])
-        gelu_a(0)
-        for t in (1, 2):
-            gather_difference(diff_c2[t], t, HALF, x1_c2[t])
-        quantise_d(QUARTER, QUARTER, d_in[1])
-        for t in (1, 2):
-            gather(x1_c3[t], t, idx3, 768, QUARTER)
-        turn_c2(3, banks[6])
-        turn_c2(0, banks[7])
-        turn_c2(1, banks[6])
-        turn_c2(2, banks[7])
-        gelu_a(1)
-        order = (3, 0, 1, 2)
-        for t in order[1:]:
-            gather_difference(diff_c3[t], t, 768, x1_c3[t])
-        for i in range(2):
-            turn(banks[6 + i], [diff_c3[order[i]]], QUARTER, d_rows[3], order[i])
-        turn_back(banks[2], d_rows[2], 0, 2, d_in[2])
-        skip_banks = [banks[0], banks[1], banks[4], banks[5]]
-        for c in range(2):
-            skip_branch(c, 1, 0, HALF, skip_banks[c])
-        for i in range(2):
-            turn(banks[6 + i], [diff_c3[order[2 + i]]], QUARTER, d_rows[3], order[2 + i])
-        for c in range(2, TILES):
-            skip_branch(c, 1, 0, HALF, skip_banks[c])
-        for c in range(2):
-            finish_a(c, banks[c], res[c])
-        quantise_d(HALF, QUARTER, d_in[2])
-        for b in range(2):
-            turn_back(banks[6 + b], d_rows[3], b, 1, d_in[3 + b])
-        for g in range(2):
-            gelu_branch(2 * g, 2, HALF, QUARTER, banks[2 + g], rows(act[g][:], QUARTER))
-        quantise_d(768, P, d_in[3])
-        quantise_d(896, P, d_in[4])
-        skip_branch(0, 2, HALF, QUARTER, banks[0])
-        skip_branch(2, 2, HALF, QUARTER, banks[1])
-        gelu_branch(0, 4, 768, P, banks[2], rows(act[2][:], P))
-        gelu_branch(0, 4, 896, P, banks[3], rows(act[3][:], P))
-        skip_branch(0, 4, 768, P, banks[6])
-        skip_branch(0, 4, 896, P, banks[7])
-        finish_a(2, banks[4], res_pair[:, 0:HALF])
-        finish_a(3, banks[5], res_pair[:, HALF : 2 * HALF])
-        finish(0, 2, HALF, QUARTER, banks[0], act[0], res[2])
-        finish(2, 2, HALF, QUARTER, banks[1], act[1], res[3])
-        finish(0, 4, 768, P, banks[6], act[2], res[4])
-        finish(0, 2, 896, P, banks[7], act[3], res[5][:, 0:QUARTER])
-        finish(2, 2, 896, P, banks[7][:, QUARTER:HALF], act[3][:, QUARTER:HALF], res[5][:, QUARTER:HALF], nc.scalar)
+        gather(x1_two[:, 0:CHUNK], 2, idx3, 0, CHUNK)
+        gather(x1_three[0], 3, idx3, 0, CHUNK)
+        high_difference(0, 2)
+        high_difference(0, 3)
+        round_high(0)
+        gather(x1_two[:, CHUNK:M], 2, idx3, CHUNK, M - CHUNK)
+        second_products(0)
+        gather(high[:, 0 : 3 * CHUNK], 3, idx3, CHUNK, M - CHUNK)
+        for c in (1, 2):
+            high_difference(c, 2)
+            high_difference(c, 3)
+            round_high(c)
+        second_products(1)
+        finish(0)
+        high_difference(3, 2)
+        second_products(2)
+        high_difference(3, 3)
+        round_high(3)
+        finish(1)
+        second_products(3)
+        finish(2)
+        finish(3)

@@ -44,18 +44,20 @@ def tile_list_regression_bisect_features_kernel(
         TAB0, TAB1, W2A = 0, 16 * KB, 32 * KB
         TABS = W2A + 8 * KB - 64
         PAGE0 = TABS + 4 * KB - 64
-        W4 = PAGE0 + 8 * KB
-        STAGE0 = W4 + 8 * KB - 64
-        PAGE2 = STAGE0 + 2 * KB - 64
-        W3 = PAGE2 + 8 * KB
+        W4 = PAGE0 + 8 * KB + 64
+        STAGE00 = W4 + 8 * KB - 64
+        PAGE2 = STAGE00 + KB - 64
+        STAGE01 = PAGE2 + 8 * KB
+        A0 = STAGE01 + KB - 64
+        W3 = A0 + 2 * KB
         W1 = W3 + 2 * KB - 64
-        STAGE1 = W1 + 2 * KB
-        A1 = STAGE1 + 2 * KB - 64
+        X1_FIRST = W1 + 2 * KB
+        STAGE1 = X1_FIRST + 2 * KB
+        A1 = STAGE1 + 2 * KB
         STAGE23 = A1 + 4 * KB
-        A2 = STAGE23 + 4 * KB - 64
+        A2 = STAGE23 + 4 * KB
         B1 = A2 + 4 * KB
-        H12 = B1 + 4 * KB
-        B2 = H12 + 4 * KB
+        B2 = B1 + 4 * KB
         A3 = B2 + 4 * KB
         X1_HEAD = A3 + 4 * KB
         D_LOW = X1_HEAD + KB - 64
@@ -80,14 +82,15 @@ def tile_list_regression_bisect_features_kernel(
         gain_sb = at(W1 + KB, "gain_sb", [P, TILES], F32)
         w2_raw = [at((W2A, TAB0)[g], "w2_raw%d" % g, [P, 2 * 4 * 2 * P], F32) for g in range(2)]
         w4_raw = at(W4, "w4_raw", [P, 4, N], F32)
-        stage = [at((STAGE0, STAGE1)[t], "stage%d" % t, [P, 2 * HALF], BF16) for t in range(2)]
+        stage1 = at(STAGE1, "stage1", [P, 2 * HALF], BF16)
+        stage = [[at((STAGE00, STAGE01)[a], "stage0%d" % a, [P, HALF], BF16)[:] for a in range(2)], [stage1[:, 0:HALF], stage1[:, HALF : 2 * HALF]]]
         stage_high = at(STAGE23, "stage_high", [P, 4 * HALF], BF16)
         stage4 = at(B1, "stage4", [P, 4 * N], BF16)
         low_w = sb("low_w", [P, 4 * P], U32)
         low_s = sb("low_s", [P, 4 * P], U8)
         high_w = sb("high_w", [P, 4 * P], U32)
         high_s = sb("high_s", [P, 4 * P], U8)
-        w4_w = at(H12, "w4_w", [P, N], U32)
+        w4_w = sb("w4_w", [P, N], U32)
         w4_s = sb("w4_s", [P, N], U8)
         wgs_low = [at((TABS + 64, TAB0 + 8 * KB)[h], "wgs_low%d" % h, [P, HALF], F32) for h in range(2)]
         wgs_high = at(TAB1 + 8 * KB, "wgs_high", [P, 2 * S], F32)
@@ -99,14 +102,15 @@ def tile_list_regression_bisect_features_kernel(
 
         w2_rows = w2.rearrange("(a p j) c -> a p j c", a=2, j=4)
         tab_rows = [tab_words[a].rearrange("p t i -> p (t i)").bitcast(I32) for a in range(2)]
-        wgs_rows = wgs.rearrange("(p i) j -> p i j", i=4)
-        page_low = page0.rearrange("(g p i) t -> g p i t", g=2, i=4)
+        wgs_even = wgs.rearrange("(q e) j -> q e j", e=2)[:, 0:1, :]
+        wgs_odd = wgs.rearrange("(p u e) j -> p u e j", u=2, e=2)[:, :, 1, :]
+        page_low = page0.rearrange("(t g q e) c -> t e q g c", t=2, g=2, e=2)
         page_high = page0.rearrange("(p i) t -> i p t", i=4)
 
         w2_view = [raw[:].rearrange("p (a j c) -> p a j c", a=2, j=4) for raw in w2_raw]
 
-        def load_wgs_low(h, g):
-            nc.sync.dma_start(wgs_low[h][64 * g : 64 * (g + 1), :], wgs_rows[:, 0:2, HALF * h : HALF * (h + 1)])
+        def load_wgs_low(h):
+            nc.sync.dma_start(wgs_low[h][:], wgs_even[:, :, HALF * h : HALF * (h + 1)].to_broadcast([64, 2, HALF]))
 
         def load_w2(g, a):
             nc.sync.dma_start(w2_view[g][:, a], w2_rows[a, :, :, 2 * P * g : 2 * P * (g + 1)])
@@ -132,31 +136,24 @@ def tile_list_regression_bisect_features_kernel(
             )
         for a in range(2):
             load_w2(0, a)
-        for g in range(2):
-            load_wgs_low(0, g)
-        nc.sync.dma_start(page[0][:], page_low[0, :, 0:2, :])
+        load_wgs_low(0)
+        nc.sync.dma_start(page[0][:], page_low[0, 0])
         nc.vector.tensor_copy(v_w[0][:], tab_w[0][:].indirect(idx1[:]))
+        load_wgs_low(1)
         for a in range(2):
             load_w2(1, a)
-        for g in range(2):
-            load_wgs_low(1, g)
 
-        nc.vector.tensor_copy(
-            w1_w[:].bitcast(I32).rearrange("p (a c) -> p a c", a=2)[:, :, 0:P],
-            w1_raw[:].bitcast(I32).rearrange("p (a c u) -> p a c u", a=2, u=2)[:, :, :, 0],
-        )
-        nc.gpsimd.tensor_copy(
-            w1_s[:].rearrange("p (a c) -> p a c", a=2)[:, :, 0 : 2 * P].rearrange("p a (c i) -> p a c i", i=2),
-            w1_raw_s[:].rearrange("p (a c i) -> p a c i", a=2, i=4)[:, :, :, 0:2],
-        )
-        nc.vector.tensor_copy(
-            w1_w[:].bitcast(U16).rearrange("p (a t c) -> p a t c", a=2, t=4)[:, :, 2:4, :],
-            w1_raw[:].bitcast(U16).rearrange("p (a c i) -> p a i c", a=2, i=4)[:, :, 2:4, :],
-        )
-        nc.gpsimd.tensor_copy(
-            w1_s[:].rearrange("p (a t c) -> p a t c", a=2, t=4)[:, :, 2:4, :],
-            w1_raw_s[:].rearrange("p (a c i) -> p a i c", a=2, i=4)[:, :, 2:4, :],
-        )
+        def even_columns(dst, src):
+            return (dst.rearrange("p (a t q g) -> p a t q g", a=2, t=4, g=2)[:, :, 0:2],
+                    src.rearrange("p (a t g q e) -> p e a t q g", a=2, t=2, g=2, e=2)[:, 0])
+
+        def odd_columns(dst, src):
+            return (dst.rearrange("p (a t c) -> p a t c", a=2, t=4)[:, :, 2:4, :],
+                    src.rearrange("p (a c u e) -> p e a u c", a=2, u=2, e=2)[:, 1])
+
+        for columns in (even_columns, odd_columns):
+            nc.vector.tensor_copy(*columns(w1_w[:].bitcast(U16), w1_raw[:].bitcast(U16)))
+            nc.gpsimd.tensor_copy(*columns(w1_s[:], w1_raw_s[:]))
         nc.sync.dma_start(w3_w[:].bitcast(I32), w3_words[0].rearrange("p n i -> p (n i)").bitcast(I32))
         nc.gpsimd.memset(w3_s[:].bitcast(I32), 0)
         for q in range(4):
@@ -165,20 +162,20 @@ def tile_list_regression_bisect_features_kernel(
             nc.sync.dma_start(gain_sb[:], gain.rearrange("(c p) -> p c", p=P))
         for h in range(2):
             nc.vector.tensor_copy(v_w[1][:, HALF * h : HALF * (h + 1)], tab_w[1][:].indirect(idx1[:, 32 * h : 32 * (h + 1)]))
-        nc.sync.dma_start(page[1][:], page_low[1, :, 0:2, :])
+        nc.sync.dma_start(page[1][:], page_low[1, 0])
         for g in range(4):
-            nc.sync.dma_start(wgs_high[32 * g : 32 * (g + 1), :].rearrange("p (i j) -> p i j", i=2), wgs_rows[:, 2:4, :])
+            nc.sync.dma_start(wgs_high[32 * g : 32 * (g + 1), :].rearrange("p (i j) -> p i j", i=2), wgs_odd)
 
         def cast_low(t, a):
             nc.scalar.copy(
-                stage[t][:, HALF * a : HALF * (a + 1)].rearrange("p (c i j) -> p c i j", i=2, j=4),
-                w2_view[t][:, a].rearrange("p j (c i) -> p c i j", i=4)[:, :, 0:2, :],
+                stage[t][a].rearrange("p (c u g j) -> p c g u j", u=2, g=2, j=4),
+                w2_view[t][:, a].rearrange("p j (g c u e) -> p e c g u j", g=2, u=2, e=2)[:, 0],
             )
 
         def cast_high(g):
             nc.scalar.copy(
                 stage_high[:].rearrange("p (t a g c j) -> p g a c t j", t=2, a=2, g=2, j=4)[:, g],
-                w2_view[g].rearrange("p a j (c i) -> p a c i j", i=4)[:, :, :, 2:4, :],
+                w2_view[g].rearrange("p a j (c u e) -> p e a c u j", u=2, e=2)[:, 1],
             )
 
         def quantise(codes, scales, c0, src):
@@ -205,60 +202,52 @@ def tile_list_regression_bisect_features_kernel(
             mx(bank_a(t, h)[:], w1_w[:, 2 * c0 : 2 * (c0 + P)].bitcast(FP4X4), w1_s[:, c0 : c0 + P],
                v_w[a][:, HALF * h : HALF * (h + 1)].bitcast(FP8X4), v_planes[:, S * a + HALF * h : S * a + HALF * (h + 1)], a == 0, a == 1)
 
-        a_sb = [sb("a_first", [P, HALF], F32)] + [at(A1, "a_sb1", [P, S], F32), at(A2, "a_sb2", [P, S], F32), at(A3, "a_sb3", [P, S], F32)]
-        b_sb = [None, at(B1, "b_sb1", [P, S], F32), at(B2, "b_sb2", [P, S], F32), sb("b_sb3", [P, S], F32)]
+        a_sb = [at(A0, "a_sb0", [P, HALF], F32)] + [at(A1, "a_sb1", [P, S], F32), at(A2, "a_sb2", [P, S], F32), at(A3, "a_sb3", [P, S], F32)]
+        b_sb = [sb("b_sb0", [P, S], F32), at(B1, "b_sb1", [P, S], F32), at(B2, "b_sb2", [P, S], F32), sb("b_sb3", [P, S], F32)]
         bw_high = sb("bw_high", [P, S], F32)
-        bw = [sb("bw0", [P, S], F32), sb("bw1", [P, S], F32), bw_high, bw_high]
-        h_both = at(H12, "h_both", [P, S], F32)
-        h_sb = [at(STAGE23, "h_first", [P, HALF], F32), h_both, h_both, sb("h_last", [P, S], F32)]
-        x1 = [sb("x1_%d" % t, [P, M], F32) for t in range(2)]
-        x2 = [sb("x2_%d" % t, [P, M], F32) for t in range(2)]
+        bw = [sb("bw0", [P, S], F32), None, bw_high, bw_high]
+        h_sb = [sb("h_first", [P, S], F32), sb("h_sb1", [P, S], F32), at(B1, "h_sb2", [P, S], F32), sb("h_last", [P, S], F32)]
+        x1 = [at(X1_FIRST, "x1_0", [P, M], F32), at(W4 - 64, "x1_1", [P, M], F32)]
+        x2 = [at(STAGE23, "x2_0", [P, M], F32), at(W4 + 4 * KB - 64, "x2_1", [P, M], F32)]
         rounded = [at((B2, A3)[t], "rounded%d" % t, [P, M], BF16) for t in range(2)]
 
         for a in range(2):
             cast_low(0, a)
-            quantise(low_w, low_s, P * a, stage[0][:, HALF * a : HALF * (a + 1)])
+            quantise(low_w, low_s, P * a, stage[0][a])
         nc.sync.dma_start(w4_raw[:], w4.rearrange("(p j) n -> p j n", j=4))
-        nc.sync.dma_start(page[2][:], page_high[2])
+        nc.sync.dma_start(page[2][:], page_high[1])
         for h in range(2):
             pass_a(0, h, 0)
             pass_b(0, h, 0)
             pass_a(0, h, 1)
             pass_b(0, h, 1)
-        nc.scalar.copy(a_sb[0][:], bank_a(0, 0)[:])
-        nc.vector.tensor_tensor(bw[0][:, 0:HALF], bank_b(0, 0)[:], wgs_low[0][:], MULT)
-        nc.vector.tensor_tensor(page[0][:].indirect(idx2[:, 0:32]), a_sb[0][:], bw[0][:, 0:HALF], MULT)
+        nc.vector.tensor_tensor(bw[0][:, 0:HALF], bank_a(0, 0)[:], wgs_low[0][:], MULT)
+        nc.vector.tensor_tensor(h_sb[0][:, 0:HALF], bank_b(0, 0)[:], bw[0][:, 0:HALF], MULT)
+        nc.scalar.copy(b_sb[0][:, HALF:S], bank_b(0, 1)[:])
+        nc.scalar.copy(a_sb[0][:], bank_a(0, 1)[:])
         cast_high(0)
         nc.sync.dma_start(page[3][:], page_high[3])
         for a in range(2):
             cast_low(1, a)
         cast_high(1)
-        nc.vector.tensor_tensor(bw[0][:, HALF:S], bank_b(0, 1)[:], wgs_low[1][:], MULT)
-        quantise(low_w, low_s, 2 * P, stage[1][:])
-        quantise(high_w, high_s, 0, stage_high[:])
-        nc.vector.tensor_tensor(h_sb[0][:], bank_a(0, 1)[:], bw[0][:, HALF:S], MULT)
-        nc.vector.tensor_copy(page[0][:].indirect(idx2[:, 32:64]), h_sb[0][:])
 
         def first_products(t):
             for h in range(2):
                 for a in range(2):
                     pass_b(t, h, a)
                 nc.scalar.copy(b_sb[t][:, HALF * h : HALF * (h + 1)], bank_b(t, h)[:])
-            for h in range(2):
                 for a in range(2):
                     pass_a(t, h, a)
                 nc.scalar.copy(a_sb[t][:, HALF * h : HALF * (h + 1)], bank_a(t, h)[:])
 
         def weigh(t):
-            if t < 2:
-                for h in range(2):
-                    cols = slice(HALF * h, HALF * (h + 1))
-                    nc.gpsimd.tensor_tensor(bw[t][:, cols], b_sb[t][:, cols], wgs_low[h][:], MULT)
-            else:
-                nc.gpsimd.tensor_tensor(bw[t][:, 0:S], b_sb[t][:], wgs_high[:, S * (t - 2) : S * (t - 1)], MULT)
+            nc.gpsimd.tensor_tensor(bw[t][:], b_sb[t][:], wgs_high[:, S * (t - 2) : S * (t - 1)], MULT)
 
         def join(t):
             nc.gpsimd.tensor_tensor(h_sb[t][:], a_sb[t][:], bw[t][:], MULT)
+
+        def scatter_half(t, h):
+            nc.vector.tensor_copy(page[t][:].indirect(idx2[:, 32 * h : 32 * (h + 1)]), h_sb[t][:, HALF * h : HALF * (h + 1)])
 
         def scatter(t):
             nc.vector.tensor_copy(page[t][:].indirect(idx2[:]), h_sb[t][:])
@@ -275,16 +264,28 @@ def tile_list_regression_bisect_features_kernel(
 
         def low_difference(t):
             nc.gpsimd.tensor_tensor(rounded[t][:], x2[t][:, 0:M], x1[t][:], SUBTRACT)
-            nc.sync.dma_start(d_low[64 * t : 64 * (t + 1), :, :], rounded[t][:])
+            for g in range(2):
+                nc.sync.dma_start(d_low[64 * t + 32 * g : 64 * t + 32 * (g + 1), :, :], rounded[t][g:P:2, :])
 
+        nc.gpsimd.tensor_tensor(bw[0][:, HALF:S], b_sb[0][:, HALF:S], wgs_low[1][:], MULT)
+        nc.gpsimd.tensor_tensor(h_sb[0][:, HALF:S], a_sb[0][:], bw[0][:, HALF:S], MULT)
+        for h in range(2):
+            scatter_half(0, h)
+        quantise(low_w, low_s, 2 * P, stage1[:])
+        quantise(high_w, high_s, 0, stage_high[:])
         for t in (1, 2, 3):
             first_products(t)
-        weigh(1)
-        join(1)
+        aw = [bw[0][:, HALF:S], at(A0, "aw_second", [P, HALF], F32)[:]]
+        for h in range(2):
+            nc.gpsimd.tensor_tensor(aw[h], a_sb[1][:, HALF * h : HALF * (h + 1)], wgs_low[h][:], MULT)
+        for h in range(2):
+            cols = slice(HALF * h, HALF * (h + 1))
+            nc.gpsimd.tensor_tensor(h_sb[1][:, cols], b_sb[1][:, cols], aw[h], MULT)
         nc.scalar.copy(stage4[:].rearrange("p (c j) -> p c j", j=4), w4_raw[:].rearrange("p j c -> p c j"))
         gather(x1[0][:], 0, idx3, 0, M)
         gather(x2[0][:], 0, idx4, 0, M)
         scatter(1)
+        quantise(w4_w, w4_s, 0, stage4[:])
         gather(x1[1][:], 1, idx3, 0, M)
         gather(x2[1][:], 1, idx4, 0, M)
         weigh(2)
@@ -293,10 +294,9 @@ def tile_list_regression_bisect_features_kernel(
         weigh(3)
         join(3)
         low_difference(1)
-        nc.scalar.copy(d_cols[:, :, 0:2], d_low[:].rearrange("p i m -> p m i"))
+        nc.scalar.copy(d_cols[:, :, 0:4:2], d_low[:].rearrange("p i m -> p m i"))
         for t in (2, 3):
             scatter(t)
-        quantise(w4_w, w4_s, 0, stage4[:])
 
         act = at(TAB0, "act", [P, TILES * 4 * CHUNK], F32)
         res = sb("res", [P, TILES * 4 * CHUNK], F32)
@@ -314,7 +314,7 @@ def tile_list_regression_bisect_features_kernel(
             gather_difference(d_high[c][:, CHUNK * (t - 2) : CHUNK * (t - 1)], t, CHUNK * c, CHUNK, first)
 
         def round_high(c):
-            nc.scalar.copy(d_cols[:, CHUNK * c : CHUNK * (c + 1), 2:4], d_high[c].rearrange("p (i m) -> p m i", i=2))
+            nc.scalar.copy(d_cols[:, CHUNK * c : CHUNK * (c + 1), 1:4:2], d_high[c].rearrange("p (i m) -> p m i", i=2))
 
         def second_products(c):
             cols = slice(CHUNK * c, CHUNK * (c + 1))
@@ -342,12 +342,12 @@ def tile_list_regression_bisect_features_kernel(
                 queue.dma_start(out_tiles[:, 2 * g : 2 * g + 2, CHUNK * c : CHUNK * (c + 1)],
                                 res[:, CHUNK * (4 * c + 2 * g) : CHUNK * (4 * c + 2 * g + 2)].rearrange("p (i m) -> p i m", i=2))
 
-        gather(x1_two[:, 0:CHUNK], 2, idx3, 0, CHUNK)
+        gather(x1_two[:, 0:HALF], 2, idx3, 0, HALF)
         gather(x1_three[0], 3, idx3, 0, CHUNK)
         high_difference(0, 2)
         high_difference(0, 3)
         round_high(0)
-        gather(x1_two[:, CHUNK:M], 2, idx3, CHUNK, M - CHUNK)
+        gather(x1_two[:, HALF:M], 2, idx3, HALF, HALF)
         second_products(0)
         gather(high[:, 0 : 3 * CHUNK], 3, idx3, CHUNK, M - CHUNK)
         for c in (1, 2):

@@ -52,8 +52,9 @@ def tile_list_regression_bisect_features_kernel(
         W3 = A0 + 2 * KB
         W1 = W3 + 2 * KB - 64
         X1_FIRST = W1 + 2 * KB
-        STAGE1 = X1_FIRST + 2 * KB
-        A1 = STAGE1 + 2 * KB
+        STAGE11 = X1_FIRST + 3 * KB
+        STAGE10 = STAGE11 + KB
+        A1 = STAGE10 + 2 * KB
         STAGE23 = A1 + 4 * KB
         A2 = STAGE23 + 4 * KB
         B1 = A2 + 4 * KB
@@ -82,8 +83,7 @@ def tile_list_regression_bisect_features_kernel(
         gain_sb = at(W1 + KB, "gain_sb", [P, TILES], F32)
         w2_raw = [at((W2A, TAB0)[g], "w2_raw%d" % g, [P, 2 * 4 * 2 * P], F32) for g in range(2)]
         w4_raw = at(W4, "w4_raw", [P, 4, N], F32)
-        stage1 = at(STAGE1, "stage1", [P, 2 * HALF], BF16)
-        stage = [[at((STAGE00, STAGE01)[a], "stage0%d" % a, [P, HALF], BF16)[:] for a in range(2)], [stage1[:, 0:HALF], stage1[:, HALF : 2 * HALF]]]
+        stage = [[at(((STAGE00, STAGE01), (STAGE10, STAGE11))[t][a], "stage%d%d" % (t, a), [P, HALF], BF16)[:] for a in range(2)] for t in range(2)]
         stage_high = at(STAGE23, "stage_high", [P, 4 * HALF], BF16)
         stage4 = at(B1, "stage4", [P, 4 * N], BF16)
         low_w = sb("low_w", [P, 4 * P], U32)
@@ -99,6 +99,10 @@ def tile_list_regression_bisect_features_kernel(
         nc.vector.memset(w1_raw_s[:].bitcast(I32), 0)
         nc.vector.memset(tab_s[0:96, :].bitcast(I32), 0)
         nc.vector.memset(v_planes[:].bitcast(I32), 0)
+
+        warm = sb("warm", [P, 16], F32)
+        nc.gpsimd.memset(warm[:, 0:8], 0.0)
+        nc.scalar.activation(warm[:, 8:16], warm[:, 0:8], GELU)
 
         w2_rows = w2.rearrange("(a p j) c -> a p j c", a=2, j=4)
         tab_rows = [tab_words[a].rearrange("p t i -> p (t i)").bitcast(I32) for a in range(2)]
@@ -271,11 +275,11 @@ def tile_list_regression_bisect_features_kernel(
         nc.gpsimd.tensor_tensor(h_sb[0][:, HALF:S], a_sb[0][:], bw[0][:, HALF:S], MULT)
         for h in range(2):
             scatter_half(0, h)
-        quantise(low_w, low_s, 2 * P, stage1[:])
+            quantise(low_w, low_s, P * (2 + h), stage[1][h])
         quantise(high_w, high_s, 0, stage_high[:])
         for t in (1, 2, 3):
             first_products(t)
-        aw = [bw[0][:, HALF:S], at(A0, "aw_second", [P, HALF], F32)[:]]
+        aw = [at(STAGE10, "aw_first", [P, HALF], F32)[:], at(A0, "aw_second", [P, HALF], F32)[:]]
         for h in range(2):
             nc.gpsimd.tensor_tensor(aw[h], a_sb[1][:, HALF * h : HALF * (h + 1)], wgs_low[h][:], MULT)
         for h in range(2):
@@ -302,45 +306,46 @@ def tile_list_regression_bisect_features_kernel(
         res = sb("res", [P, TILES * 4 * CHUNK], F32)
         d_w = sb("d_w", [P, M], U32)
         d_s = sb("d_s", [P, M], U8)
-        high = sb("high", [P, 7 * CHUNK], F32)
+        high = sb("high", [P, 10 * CHUNK], F32)
         x1_head = at(X1_HEAD, "x1_head", [P, CHUNK], F32)
-        d_high = [high[:, CHUNK : 3 * CHUNK], high[:, 3 * CHUNK : 5 * CHUNK], high[:, 5 * CHUNK : 7 * CHUNK], act[:, 2 * CHUNK : 4 * CHUNK]]
+
+        def pair(tile, c0, pitch=CHUNK):
+            return [tile[:, c0 + pitch * i : c0 + pitch * i + CHUNK] for i in range(2)], tile[:, c0 : c0 + 2 * pitch].rearrange("p (i m) -> p i m", i=2)[:, :, 0:CHUNK]
+
+        d_high = [pair(high, CHUNK), pair(high, 3 * CHUNK), pair(high, 5 * CHUNK, HALF), pair(high, 6 * CHUNK, HALF)]
+        acts = {(c, g): pair(act, CHUNK * (4 * c + 2 * g)) for c in range(4) for g in range(2)}
+        sums = {(c, g): pair(res, CHUNK * (4 * c + 2 * g)) for c in range(4) for g in range(2)}
+        sums[0, 0], sums[0, 1] = d_high[2], d_high[3]
         x1_two = at(D_LOW + 64, "x1_two", [P, M], F32)
         x1_three = [x1_head[:]] + [high[:, CHUNK * c : CHUNK * (c + 1)] for c in range(3)]
         out_tiles = out.rearrange("(c p) m -> p c m", p=P)
 
         def high_difference(c, t):
             first = x1_two[:, CHUNK * c : CHUNK * (c + 1)] if t == 2 else x1_three[c]
-            gather_difference(d_high[c][:, CHUNK * (t - 2) : CHUNK * (t - 1)], t, CHUNK * c, CHUNK, first)
+            gather_difference(d_high[c][0][t - 2], t, CHUNK * c, CHUNK, first)
 
         def round_high(c):
-            nc.scalar.copy(d_cols[:, CHUNK * c : CHUNK * (c + 1), 1:4:2], d_high[c].rearrange("p (i m) -> p m i", i=2))
+            nc.scalar.copy(d_cols[:, CHUNK * c : CHUNK * (c + 1), 1:4:2], d_high[c][1].rearrange("p i m -> p m i"))
 
-        def second_products(c):
-            cols = slice(CHUNK * c, CHUNK * (c + 1))
+        def quantise_d(c):
             quantise(d_w, d_s, CHUNK * c, d_in[:, 4 * CHUNK * c : 4 * CHUNK * (c + 1)])
-            first_bank = 4 * (c % 2)
-            for g in range(2):
-                for i in range(2):
-                    n = 2 * g + i
-                    mx(banks[first_bank + g][:, CHUNK * i : CHUNK * (i + 1)], w3_w[:, P * n : P * (n + 1)].bitcast(FP8X4), w3_s[:, P * n : P * (n + 1)],
-                       d_w[:, cols].bitcast(FP8X4), d_s[:, cols], True, True)
-                nc.scalar.activation(act[:, CHUNK * (4 * c + 2 * g) : CHUNK * (4 * c + 2 * g + 2)], banks[first_bank + g][:], GELU)
-            for n in range(TILES):
-                c0 = P * n
-                mx(banks[first_bank + 2 + n // 2][:, CHUNK * (n % 2) : CHUNK * (n % 2 + 1)], w4_w[:, c0 : c0 + P].bitcast(FP8X4), w4_s[:, c0 : c0 + P],
-                   d_w[:, cols].bitcast(FP8X4), d_s[:, cols], True, True)
 
-        def finish(c):
-            for g in range(2):
+        def second_products(c, g):
+            cols = slice(CHUNK * c, CHUNK * (c + 1))
+            for codes, scales, bank in ((w3_w, w3_s, banks[4 * (c % 2) + g]), (w4_w, w4_s, banks[4 * (c % 2) + 2 + g])):
                 for i in range(2):
                     n = 2 * g + i
-                    cols = slice(CHUNK * (4 * c + n), CHUNK * (4 * c + n + 1))
-                    nc.vector.scalar_tensor_tensor(res[:, cols], act[:, cols], gain_sb[:, n : n + 1],
-                                                   banks[4 * (c % 2) + 2 + g][:, CHUNK * i : CHUNK * (i + 1)], MULT, ADD)
-                queue = nc.scalar if (c, g) == (3, 1) else nc.sync
-                queue.dma_start(out_tiles[:, 2 * g : 2 * g + 2, CHUNK * c : CHUNK * (c + 1)],
-                                res[:, CHUNK * (4 * c + 2 * g) : CHUNK * (4 * c + 2 * g + 2)].rearrange("p (i m) -> p i m", i=2))
+                    mx(bank[:, CHUNK * i : CHUNK * (i + 1)], codes[:, P * n : P * (n + 1)].bitcast(FP8X4), scales[:, P * n : P * (n + 1)],
+                       d_w[:, cols].bitcast(FP8X4), d_s[:, cols], True, True)
+            nc.scalar.activation(acts[c, g][1], banks[4 * (c % 2) + g][:].rearrange("p (i m) -> p i m", i=2), GELU)
+
+        def finish(c, g):
+            for i in range(2):
+                n = 2 * g + i
+                nc.vector.scalar_tensor_tensor(sums[c, g][0][i], acts[c, g][0][i], gain_sb[:, n : n + 1],
+                                               banks[4 * (c % 2) + 2 + g][:, CHUNK * i : CHUNK * (i + 1)], MULT, ADD)
+            queue = nc.scalar if (c, g) == (3, 1) else nc.sync
+            queue.dma_start(out_tiles[:, 2 * g : 2 * g + 2, CHUNK * c : CHUNK * (c + 1)], sums[c, g][1])
 
         gather(x1_two[:, 0:HALF], 2, idx3, 0, HALF)
         gather(x1_three[0], 3, idx3, 0, CHUNK)
@@ -348,19 +353,28 @@ def tile_list_regression_bisect_features_kernel(
         high_difference(0, 3)
         round_high(0)
         gather(x1_two[:, HALF:M], 2, idx3, HALF, HALF)
-        second_products(0)
+        quantise_d(0)
+        for g in range(2):
+            second_products(0, g)
         gather(high[:, 0 : 3 * CHUNK], 3, idx3, CHUNK, M - CHUNK)
-        for c in (1, 2):
-            high_difference(c, 2)
-            high_difference(c, 3)
-            round_high(c)
-        second_products(1)
-        finish(0)
-        high_difference(3, 2)
-        second_products(2)
+        for t in (2, 3):
+            high_difference(1, t)
+        round_high(1)
+        gather_difference(high[:, 5 * CHUNK : 7 * CHUNK], 2, HALF, HALF, x1_two[:, HALF:M])
+        high_difference(2, 3)
+        round_high(2)
+        quantise_d(1)
         high_difference(3, 3)
         round_high(3)
-        finish(1)
-        second_products(3)
-        finish(2)
-        finish(3)
+        for g in range(2):
+            second_products(1, g)
+        for g in range(2):
+            finish(0, g)
+            quantise_d(2 + g)
+            second_products(2, g)
+        for g in range(2):
+            finish(1, g)
+            second_products(3, g)
+        for c in (2, 3):
+            for g in range(2):
+                finish(c, g)

@@ -61,7 +61,7 @@ def tile_list_regression_bisect_features_kernel(
         B2 = B1 + 4 * KB
         A3 = B2 + 4 * KB
         X1_HEAD = A3 + 4 * KB
-        D_LOW = X1_HEAD + KB - 64
+        D_LOW = X1_HEAD + 2 * KB - 64
 
         banks = [psum.tile([P, HALF], F32, name="bank%d" % i) for i in range(8)]
 
@@ -306,22 +306,23 @@ def tile_list_regression_bisect_features_kernel(
         res = sb("res", [P, TILES * 4 * CHUNK], F32)
         d_w = sb("d_w", [P, M], U32)
         d_s = sb("d_s", [P, M], U8)
-        high = sb("high", [P, 10 * CHUNK], F32)
-        x1_head = at(X1_HEAD, "x1_head", [P, CHUNK], F32)
+        high = sb("high", [P, 12 * CHUNK], F32)
+        x1_two = at(D_LOW + 64, "x1_two", [P, HALF], F32)
+        x1_three = at(X1_HEAD, "x1_three", [P, HALF], F32)
 
         def pair(tile, c0, pitch=CHUNK):
             return [tile[:, c0 + pitch * i : c0 + pitch * i + CHUNK] for i in range(2)], tile[:, c0 : c0 + 2 * pitch].rearrange("p (i m) -> p i m", i=2)[:, :, 0:CHUNK]
 
-        d_high = [pair(high, CHUNK), pair(high, 3 * CHUNK), pair(high, 5 * CHUNK, HALF), pair(high, 6 * CHUNK, HALF)]
+        d_high = [pair(high, 0), pair(high, 2 * CHUNK), pair(high, 4 * CHUNK + P, HALF), pair(high, 9 * CHUNK)]
         acts = {(c, g): pair(act, CHUNK * (4 * c + 2 * g)) for c in range(4) for g in range(2)}
         sums = {(c, g): pair(res, CHUNK * (4 * c + 2 * g)) for c in range(4) for g in range(2)}
-        sums[0, 0], sums[0, 1] = d_high[2], d_high[3]
-        x1_two = at(D_LOW + 64, "x1_two", [P, M], F32)
-        x1_three = [x1_head[:]] + [high[:, CHUNK * c : CHUNK * (c + 1)] for c in range(3)]
+        sums[0, 1], sums[1, 0] = pair(high, 4 * CHUNK, HALF), pair(high, 5 * CHUNK, HALF)
+        acts[1, 1] = d_high[3]
+        x1_high = {2: [x1_two[:], high[:, 0:HALF]], 3: [x1_three[:], high[:, HALF : 2 * HALF]]}
         out_tiles = out.rearrange("(c p) m -> p c m", p=P)
 
         def high_difference(c, t):
-            first = x1_two[:, CHUNK * c : CHUNK * (c + 1)] if t == 2 else x1_three[c]
+            first = x1_high[t][c // 2][:, CHUNK * (c % 2) : CHUNK * (c % 2 + 1)]
             gather_difference(d_high[c][0][t - 2], t, CHUNK * c, CHUNK, first)
 
         def round_high(c):
@@ -347,30 +348,27 @@ def tile_list_regression_bisect_features_kernel(
             queue = nc.scalar if (c, g) == (3, 1) else nc.sync
             queue.dma_start(out_tiles[:, 2 * g : 2 * g + 2, CHUNK * c : CHUNK * (c + 1)], sums[c, g][1])
 
-        gather(x1_two[:, 0:HALF], 2, idx3, 0, HALF)
-        gather(x1_three[0], 3, idx3, 0, CHUNK)
-        high_difference(0, 2)
-        high_difference(0, 3)
-        round_high(0)
-        gather(x1_two[:, HALF:M], 2, idx3, HALF, HALF)
-        quantise_d(0)
-        for g in range(2):
-            second_products(0, g)
-        gather(high[:, 0 : 3 * CHUNK], 3, idx3, CHUNK, M - CHUNK)
         for t in (2, 3):
-            high_difference(1, t)
-        round_high(1)
-        gather_difference(high[:, 5 * CHUNK : 7 * CHUNK], 2, HALF, HALF, x1_two[:, HALF:M])
-        high_difference(2, 3)
-        round_high(2)
-        quantise_d(1)
-        high_difference(3, 3)
-        round_high(3)
+            gather(x1_high[t][0], t, idx3, 0, HALF)
+        for c in range(2):
+            for t in (2, 3):
+                high_difference(c, t)
+            round_high(c)
+        for c in range(2):
+            gather(x1_high[2 + c][1], 2 + c, idx3, HALF, HALF)
+            quantise_d(c)
+            second_products(c, 0)
+        second_products(0, 1)
+        finish(0, 0)
+        for c in (2, 3):
+            for t in (2, 3):
+                high_difference(c, t)
+            round_high(c)
+        finish(0, 1)
+        for c in (2, 3):
+            quantise_d(c)
+        second_products(1, 1)
         for g in range(2):
-            second_products(1, g)
-        for g in range(2):
-            finish(0, g)
-            quantise_d(2 + g)
             second_products(2, g)
         for g in range(2):
             finish(1, g)

@@ -74,13 +74,13 @@ def tile_list_regression_bisect_features_kernel(
         v_w = [sb("v_w%d" % a, [P, S], U32) for a in range(2)]
         picked_s = sb("picked_s", [P, S], U8)
         v_planes = sb("v_planes", [P, 2 * S], U8)
-        w1_raw = at(W1, "w1_raw", [P, 2 * 2 * H], U8)
+        w1_raw = [at((W1, TABS + 64 + 2 * KB)[g], "w1_raw%d" % g, [P, 2 * H], U8) for g in range(2)]
         w1_w = sb("w1_w", [P, 2 * 2 * H], U8)
         w1_raw_s = sb("w1_raw_s", [P, 2 * H], U8)
         w1_s = sb("w1_s", [P, 2 * H], U8)
         w3_w = at(W3, "w3_w", [P, N], U32)
         w3_s = at(W1 + 64, "w3_s", [P, N], U8)
-        gain_sb = at(W1 + KB, "gain_sb", [P, TILES], F32)
+        gain_sb = at(W1 + 640, "gain_sb", [P, TILES], F32)
         w2_raw = [at((W2A, TAB0)[g], "w2_raw%d" % g, [P, 2 * 4 * 2 * P], F32) for g in range(2)]
         w4_raw = at(W4, "w4_raw", [P, 4, N], F32)
         stage = [[at(((STAGE00, STAGE01), (STAGE10, STAGE11))[t][a], "stage%d%d" % (t, a), [P, HALF], BF16)[:] for a in range(2)] for t in range(2)]
@@ -116,6 +116,9 @@ def tile_list_regression_bisect_features_kernel(
         def load_wgs_low(h):
             nc.sync.dma_start(wgs_low[h][:], wgs_even[:, :, HALF * h : HALF * (h + 1)].to_broadcast([64, 2, HALF]))
 
+        def load_w1(g):
+            nc.sync.dma_start(w1_raw[g][:].bitcast(I32).rearrange("p (a c) -> p a c", a=2), w1_words.bitcast(I32).rearrange("a p (g c) -> g p a c", g=2)[g])
+
         def load_w2(g, a):
             nc.sync.dma_start(w2_view[g][:, a], w2_rows[a, :, :, 2 * P * g : 2 * P * (g + 1)])
 
@@ -125,7 +128,7 @@ def tile_list_regression_bisect_features_kernel(
         nc.sync.dma_start(idx2[:], offs2)
         nc.sync.dma_start(idx3[:], offs3)
         nc.sync.dma_start(idx4[:], offs4)
-        nc.sync.dma_start(w1_raw[:].bitcast(I32).rearrange("p (a c) -> p a c", a=2), w1_words.bitcast(I32).rearrange("a p c -> p a c"))
+        load_w1(0)
         nc.sync.dma_start(tab_w[1][:].bitcast(I32), tab_rows[1])
         for q in range(4):
             nc.gpsimd.dma_start(
@@ -142,6 +145,7 @@ def tile_list_regression_bisect_features_kernel(
             load_w2(0, a)
         load_wgs_low(0)
         nc.sync.dma_start(page[0][:], page_low[0, 0])
+        load_w1(1)
         nc.vector.tensor_copy(v_w[0][:], tab_w[0][:].indirect(idx1[:]))
         load_wgs_low(1)
         for a in range(2):
@@ -155,8 +159,17 @@ def tile_list_regression_bisect_features_kernel(
             return (dst.rearrange("p (a t c) -> p a t c", a=2, t=4)[:, :, 2:4, :],
                     src.rearrange("p (a c u e) -> p e a u c", a=2, u=2, e=2)[:, 1])
 
+        def even_words(t):
+            return (w1_w[:].bitcast(U16).rearrange("p (a t q g) -> p t a q g", a=2, t=4, g=2)[:, t],
+                    w1_raw[t][:].bitcast(U16).rearrange("p (a g q e) -> p e a q g", a=2, g=2, e=2)[:, 0])
+
+        def odd_words(g):
+            return (w1_w[:].bitcast(U16).rearrange("p (a t g c) -> p g a t c", a=2, t=4, g=2)[:, g, :, 2:4],
+                    w1_raw[g][:].bitcast(U16).rearrange("p (a c u e) -> p e a u c", a=2, u=2, e=2)[:, 1])
+
+        for words in (even_words, odd_words):
+            nc.vector.tensor_copy(*words(0))
         for columns in (even_columns, odd_columns):
-            nc.vector.tensor_copy(*columns(w1_w[:].bitcast(U16), w1_raw[:].bitcast(U16)))
             nc.gpsimd.tensor_copy(*columns(w1_s[:], w1_raw_s[:]))
         nc.sync.dma_start(w3_w[:].bitcast(I32), w3_words[0].rearrange("p n i -> p (n i)").bitcast(I32))
         nc.gpsimd.memset(w3_s[:].bitcast(I32), 0)
@@ -229,11 +242,13 @@ def tile_list_regression_bisect_features_kernel(
         nc.vector.tensor_tensor(h_sb[0][:, 0:HALF], bank_b(0, 0)[:], bw[0][:, 0:HALF], MULT)
         nc.scalar.copy(b_sb[0][:, HALF:S], bank_b(0, 1)[:])
         nc.scalar.copy(a_sb[0][:], bank_a(0, 1)[:])
+        nc.scalar.copy(*even_words(1))
         cast_high(0)
         nc.sync.dma_start(page[3][:], page_high[3])
         for a in range(2):
             cast_low(1, a)
         cast_high(1)
+        nc.scalar.copy(*odd_words(1))
 
         def first_products(t):
             for h in range(2):

from contextlib import ExitStack

import concourse.mybir as mybir

K, H, N, T, S, T2, M = 1024, 512, 512, 4096, 1024, 2048, 1024
FLOPS = 2 * 2 * K * H * S + 2 * 2 * H * N * M

F32 = mybir.dt.float32
BF16 = mybir.dt.bfloat16
I32 = mybir.dt.int32
U32 = mybir.dt.uint32
U16 = mybir.dt.uint16
U8 = mybir.dt.uint8
FP8X4 = mybir.dt.float8_e4m3fn_x4
FP4X4 = mybir.dt.float4_e2m1fn_x4
MULT = mybir.AluOpType.mult
ADD = mybir.AluOpType.add
SUBTRACT = mybir.AluOpType.subtract
GELU = mybir.ActivationFunctionType.Gelu_apprx_tanh

P = 128
HALF = 512
CHUNK = 256
TILES = 4


def tile_list_regression_bisect_features_kernel(
    tc, tab_words, tab_scales, offs, w1_words, w1_scales, w2, wgs, page0,
    offs2, offs3, offs4, w3_words, w3_scales, w4, gain, out,
):
    nc = tc.nc
    with ExitStack() as ctx:
        keep = ctx.enter_context(tc.tile_pool(name="keep", bufs=1))
        laid = ctx.enter_context(tc.tile_pool(name="laid", bufs=1))
        psum = ctx.enter_context(tc.psum_pool(name="psum", bufs=1))

        def sb(name, shape, dtype):
            return keep.tile(shape, dtype, name=name, align_bytes=64)

        def at(offset, name, shape, dtype):
            return laid.tile(shape, dtype, name=name, align_bytes=64, offset=offset)

        KB = 1024
        TAB0, TAB1, W2A = 0, 16 * KB, 32 * KB
        TABS = W2A + 8 * KB - 64
        PAGE0 = TABS + 4 * KB - 64
        W4 = PAGE0 + 8 * KB + 64
        STAGE00 = W4 + 8 * KB - 64
        PAGE2 = STAGE00 + KB - 64
        STAGE01 = PAGE2 + 8 * KB
        A0 = STAGE01 + KB - 64
        W3 = A0 + 2 * KB
        W1 = W3 + 2 * KB - 64
        X1_FIRST = W1 + 2 * KB
        STAGE11 = X1_FIRST + 3 * KB
        STAGE10 = STAGE11 + KB
        A1 = STAGE10 + 2 * KB
        STAGE23 = A1 + 4 * KB
        A2 = STAGE23 + 4 * KB
        B1 = A2 + 4 * KB
        B2 = B1 + 4 * KB
        A3 = B2 + 4 * KB
        X1_HEAD = A3 + 4 * KB
        D_LOW = X1_HEAD + 2 * KB - 64

        banks = [psum.tile([P, HALF], F32, name="bank%d" % i) for i in range(8)]

        idx1 = keep.tile([P, S // 16], U16, name="idx1")
        idx2 = keep.tile([P, S // 16], U16, name="idx2")
        idx3 = keep.tile([P, M // 16], U16, name="idx3")
        idx4 = keep.tile([P, M // 16], U16, name="idx4")
        tab_w = [at((TAB0, TAB1)[a], "tab_w%d" % a, [P, T], U32) for a in range(2)]
        tab_s = at(TABS, "tab_s", [P, T], U8)
        v_w = [sb("v_w%d" % a, [P, S], U32) for a in range(2)]
        picked_s = sb("picked_s", [P, S], U8)
        v_planes = sb("v_planes", [P, 2 * S], U8)
        w1_raw = [at((W1, TABS + 64 + 2 * KB)[g], "w1_raw%d" % g, [P, 2 * H], U8) for g in range(2)]
        w1_w = sb("w1_w", [P, 2 * 2 * H], U8)
        w1_raw_s = sb("w1_raw_s", [P, 2 * H], U8)
        w1_s = sb("w1_s", [P, 2 * H], U8)
        w3_w = at(W3, "w3_w", [P, N], U32)
        w3_s = at(W1 + 64, "w3_s", [P, N], U8)
        gain_sb = at(W1 + 640, "gain_sb", [P, TILES], F32)
        w2_raw = [at((W2A, TAB0)[g], "w2_raw%d" % g, [P, 2 * 4 * 2 * P], F32) for g in range(2)]
        w4_raw = at(W4, "w4_raw", [P, 4, N], F32)
        stage = [[at(((STAGE00, STAGE01), (STAGE10, STAGE11))[t][a], "stage%d%d" % (t, a), [P, HALF], BF16)[:] for a in range(2)] for t in range(2)]
        stage_high = at(STAGE23, "stage_high", [P, 4 * HALF], BF16)
        stage4 = at(B1, "stage4", [P, 4 * N], BF16)
        low_w = sb("low_w", [P, 4 * P], U32)
        low_s = sb("low_s", [P, 4 * P], U8)
        high_w = sb("high_w", [P, 4 * P], U32)
        high_s = sb("high_s", [P, 4 * P], U8)
        w4_w = sb("w4_w", [P, N], U32)
        w4_s = sb("w4_s", [P, N], U8)
        wgs_low = [at((TABS + 64, TAB0 + 8 * KB)[h], "wgs_low%d" % h, [P, HALF], F32) for h in range(2)]
        wgs_high = at(TAB1 + 8 * KB, "wgs_high", [P, 2 * S], F32)
        page = [at((PAGE0, TAB1, PAGE2, W2A)[t], "page%d" % t, [P, T2], F32) for t in range(TILES)]

        nc.vector.memset(w1_raw_s[:].bitcast(I32), 0)
        nc.vector.memset(tab_s[0:96, :].bitcast(I32), 0)
        nc.vector.memset(v_planes[:].bitcast(I32), 0)

        warm = sb("warm", [P, 16], F32)
        nc.gpsimd.memset(warm[:, 0:8], 0.0)
        nc.scalar.activation(warm[:, 8:16], warm[:, 0:8], GELU)

        w2_rows = w2.rearrange("(a p j) c -> a p j c", a=2, j=4)
        tab_rows = [tab_words[a].rearrange("p t i -> p (t i)").bitcast(I32) for a in range(2)]
        wgs_even = wgs.rearrange("(q e) j -> q e j", e=2)[:, 0:1, :]
        wgs_odd = wgs.rearrange("(p u e) j -> p u e j", u=2, e=2)[:, :, 1, :]
        page_low = page0.rearrange("(t g q e) c -> t e q g c", t=2, g=2, e=2)
        page_high = page0.rearrange("(p i) t -> i p t", i=4)

        w2_view = [raw[:].rearrange("p (a j c) -> p a j c", a=2, j=4) for raw in w2_raw]

        def load_wgs_low(h):
            nc.sync.dma_start(wgs_low[h][:], wgs_even[:, :, HALF * h : HALF * (h + 1)].to_broadcast([64, 2, HALF]))

        def load_w1(g):
            nc.sync.dma_start(w1_raw[g][:].bitcast(I32).rearrange("p (a c) -> p a c", a=2), w1_words.bitcast(I32).rearrange("a p (g c) -> g p a c", g=2)[g])

        def load_w2(g, a):
            nc.sync.dma_start(w2_view[g][:, a], w2_rows[a, :, :, 2 * P * g : 2 * P * (g + 1)])

        nc.sync.dma_start(idx1[:], offs)
        nc.sync.dma_start(tab_s[96:P, :].bitcast(I32), tab_scales.bitcast(I32).rearrange("a q t -> q a t"))
        nc.sync.dma_start(tab_w[0][:].bitcast(I32), tab_rows[0])
        nc.sync.dma_start(idx2[:], offs2)
        nc.sync.dma_start(idx3[:], offs3)
        nc.sync.dma_start(idx4[:], offs4)
        load_w1(0)
        nc.sync.dma_start(tab_w[1][:].bitcast(I32), tab_rows[1])
        for q in range(4):
            nc.gpsimd.dma_start(
                w1_raw_s[32 * q : 32 * q + 4, :].bitcast(I32).rearrange("r (a c) -> r a c", a=2),
                w1_scales[:, 4 * q : 4 * q + 4, :].bitcast(I32).rearrange("a r c -> r a c"),
            )
        nc.vector.tensor_copy(picked_s[:], tab_s[:].indirect(idx1[:]))
        for q in range(4):
            nc.sync.dma_start(
                v_planes[32 * q : 32 * q + 4, :].bitcast(I32).rearrange("r (a c) -> r a c", a=2),
                picked_s[96 + 8 * q : 96 + 8 * (q + 1), :].bitcast(I32),
            )
        for a in range(2):
            load_w2(0, a)
        load_wgs_low(0)
        nc.sync.dma_start(page[0][:], page_low[0, 0])
        load_w1(1)
        nc.vector.tensor_copy(v_w[0][:], tab_w[0][:].indirect(idx1[:]))
        load_wgs_low(1)
        for a in range(2):
            load_w2(1, a)

        def even_columns(dst, src):
            return (dst.rearrange("p (a t q g) -> p a t q g", a=2, t=4, g=2)[:, :, 0:2],
                    src.rearrange("p (a t g q e) -> p e a t q g", a=2, t=2, g=2, e=2)[:, 0])

        def odd_columns(dst, src):
            return (dst.rearrange("p (a t c) -> p a t c", a=2, t=4)[:, :, 2:4, :],
                    src.rearrange("p (a c u e) -> p e a u c", a=2, u=2, e=2)[:, 1])

        def even_words(t):
            return (w1_w[:].bitcast(U16).rearrange("p (a t q g) -> p t a q g", a=2, t=4, g=2)[:, t],
                    w1_raw[t][:].bitcast(U16).rearrange("p (a g q e) -> p e a q g", a=2, g=2, e=2)[:, 0])

        def odd_words(g):
            return (w1_w[:].bitcast(U16).rearrange("p (a t g c) -> p g a t c", a=2, t=4, g=2)[:, g, :, 2:4],
                    w1_raw[g][:].bitcast(U16).rearrange("p (a c u e) -> p e a u c", a=2, u=2, e=2)[:, 1])

        for words in (even_words, odd_words):
            nc.vector.tensor_copy(*words(0))
        for columns in (even_columns, odd_columns):
            nc.gpsimd.tensor_copy(*columns(w1_s[:], w1_raw_s[:]))
        nc.sync.dma_start(w3_w[:].bitcast(I32), w3_words[0].rearrange("p n i -> p (n i)").bitcast(I32))
        nc.gpsimd.memset(w3_s[:].bitcast(I32), 0)
        for q in range(4):
            nc.sync.dma_start(w3_s[32 * q : 32 * q + 4, :].bitcast(I32), w3_scales[0, 4 * q : 4 * q + 4, :].bitcast(I32))
        with nc.allow_non_contiguous_dma(reason="one gain value to each partition"):
            nc.sync.dma_start(gain_sb[:], gain.rearrange("(c p) -> p c", p=P))
        for h in range(2):
            nc.vector.tensor_copy(v_w[1][:, HALF * h : HALF * (h + 1)], tab_w[1][:].indirect(idx1[:, 32 * h : 32 * (h + 1)]))
        nc.sync.dma_start(page[1][:], page_low[1, 0])
        for g in range(4):
            nc.sync.dma_start(wgs_high[32 * g : 32 * (g + 1), :].rearrange("p (i j) -> p i j", i=2), wgs_odd)

        def cast_low(t, a):
            nc.scalar.copy(
                stage[t][a].rearrange("p (c u g j) -> p c g u j", u=2, g=2, j=4),
                w2_view[t][:, a].rearrange("p j (g c u e) -> p e c g u j", g=2, u=2, e=2)[:, 0],
            )

        def cast_high(g):
            nc.scalar.copy(
                stage_high[:].rearrange("p (t a g c j) -> p g a c t j", t=2, a=2, g=2, j=4)[:, g],
                w2_view[g].rearrange("p a j (c u e) -> p e a c u j", u=2, e=2)[:, 1],
            )

        def quantise(codes, scales, c0, src):
            width = src.shape[1] // 4
            nc.vector.quantize_mx(out=codes[:, c0 : c0 + width].bitcast(FP8X4), scales=scales[:, c0 : c0 + width], in_=src)

        def mx(dst, w, w_scale, x, x_scale, start, stop):
            nc.tensor.matmul_mx(out=dst, lhsT=w, lhsT_scale=w_scale, rhs=x, rhs_scale=x_scale, start=start, stop=stop)

        def bank_a(t, h):
            return banks[((0, 2), (1, 3), (4, 5), (1, 3))[t][h]]

        def bank_b(t, h):
            return banks[((1, 3), (4, 5), (0, 2), (6, 7))[t][h]]

        def pass_b(t, h, a):
            codes, scales = (low_w, low_s) if t < 2 else (high_w, high_s)
            c0 = P * (2 * (t % 2) + a)
            mx(bank_b(t, h)[:], codes[:, c0 : c0 + P].bitcast(FP8X4), scales[:, c0 : c0 + P],
               v_w[a][:, HALF * h : HALF * (h + 1)].bitcast(FP8X4), v_planes[:, S * a + HALF * h : S * a + HALF * (h + 1)], a == 0, a == 1)

        def pass_a(t, h, a):
            c0 = H * a + P * t
            mx(bank_a(t, h)[:], w1_w[:, 2 * c0 : 2 * (c0 + P)].bitcast(FP4X4), w1_s[:, c0 : c0 + P],
               v_w[a][:, HALF * h : HALF * (h + 1)].bitcast(FP8X4), v_planes[:, S * a + HALF * h : S * a + HALF * (h + 1)], a == 0, a == 1)

        a_sb = [at(A0, "a_sb0", [P, HALF], F32)] + [at(A1, "a_sb1", [P, S], F32), at(A2, "a_sb2", [P, S], F32), at(A3, "a_sb3", [P, S], F32)]
        b_sb = [sb("b_sb0", [P, S], F32), at(B1, "b_sb1", [P, S], F32), at(B2, "b_sb2", [P, S], F32), sb("b_sb3", [P, S], F32)]
        bw_high = sb("bw_high", [P, S], F32)
        bw = [sb("bw0", [P, S], F32), None, bw_high, bw_high]
        h_sb = [sb("h_first", [P, S], F32), sb("h_sb1", [P, S], F32), at(B1, "h_sb2", [P, S], F32), sb("h_last", [P, S], F32)]
        x1 = [at(X1_FIRST, "x1_0", [P, M], F32), at(W4 - 64, "x1_1", [P, M], F32)]
        x2 = [at(STAGE23, "x2_0", [P, M], F32), at(W4 + 4 * KB - 64, "x2_1", [P, M], F32)]
        rounded = [at((B2, A3)[t], "rounded%d" % t, [P, M], BF16) for t in range(2)]

        for a in range(2):
            cast_low(0, a)
            quantise(low_w, low_s, P * a, stage[0][a])
        nc.sync.dma_start(w4_raw[:], w4.rearrange("(p j) n -> p j n", j=4))
        nc.sync.dma_start(page[2][:], page_high[1])
        for h in range(2):
            pass_a(0, h, 0)
            pass_b(0, h, 0)
            pass_a(0, h, 1)
            pass_b(0, h, 1)
        nc.vector.tensor_tensor(bw[0][:, 0:HALF], bank_a(0, 0)[:], wgs_low[0][:], MULT)
        nc.vector.tensor_tensor(h_sb[0][:, 0:HALF], bank_b(0, 0)[:], bw[0][:, 0:HALF], MULT)
        nc.scalar.copy(b_sb[0][:, HALF:S], bank_b(0, 1)[:])
        nc.scalar.copy(a_sb[0][:], bank_a(0, 1)[:])
        nc.scalar.copy(*even_words(1))
        cast_high(0)
        nc.sync.dma_start(page[3][:], page_high[3])
        for a in range(2):
            cast_low(1, a)
        cast_high(1)
        nc.scalar.copy(*odd_words(1))

        def first_products(t):
            for h in range(2):
                for a in range(2):
                    pass_b(t, h, a)
                nc.scalar.copy(b_sb[t][:, HALF * h : HALF * (h + 1)], bank_b(t, h)[:])
                for a in range(2):
                    pass_a(t, h, a)
                nc.scalar.copy(a_sb[t][:, HALF * h : HALF * (h + 1)], bank_a(t, h)[:])

        def weigh(t):
            nc.gpsimd.tensor_tensor(bw[t][:], b_sb[t][:], wgs_high[:, S * (t - 2) : S * (t - 1)], MULT)

        def join(t):
            nc.gpsimd.tensor_tensor(h_sb[t][:], a_sb[t][:], bw[t][:], MULT)

        def scatter_half(t, h):
            nc.vector.tensor_copy(page[t][:].indirect(idx2[:, 32 * h : 32 * (h + 1)]), h_sb[t][:, HALF * h : HALF * (h + 1)])

        def scatter(t):
            nc.vector.tensor_copy(page[t][:].indirect(idx2[:]), h_sb[t][:])

        def gather(dst, t, idx, m0, width):
            nc.vector.tensor_copy(dst, page[t][:].indirect(idx[:, m0 // 16 : (m0 + width) // 16]))

        def gather_difference(dst, t, m0, width, first):
            nc.vector.tensor_tensor(dst, page[t][:].indirect(idx4[:, m0 // 16 : (m0 + width) // 16]), first, SUBTRACT)

        d_low = at(D_LOW, "d_low", [P, 2, M], BF16)
        d_in = sb("d_in", [P, 4 * M], BF16)
        d_cols = d_in[:].rearrange("p (m i) -> p m i", i=4)

        def low_difference(t):
            nc.gpsimd.tensor_tensor(rounded[t][:], x2[t][:, 0:M], x1[t][:], SUBTRACT)
            for g in range(2):
                nc.sync.dma_start(d_low[64 * t + 32 * g : 64 * t + 32 * (g + 1), :, :], rounded[t][g:P:2, :])

        nc.gpsimd.tensor_tensor(bw[0][:, HALF:S], b_sb[0][:, HALF:S], wgs_low[1][:], MULT)
        nc.gpsimd.tensor_tensor(h_sb[0][:, HALF:S], a_sb[0][:], bw[0][:, HALF:S], MULT)
        for h in range(2):
            scatter_half(0, h)
            quantise(low_w, low_s, P * (2 + h), stage[1][h])
        quantise(high_w, high_s, 0, stage_high[:])
        for t in (1, 2, 3):
            first_products(t)
        aw = [at(STAGE10, "aw_first", [P, HALF], F32)[:], at(A0, "aw_second", [P, HALF], F32)[:]]
        for h in range(2):
            nc.gpsimd.tensor_tensor(aw[h], a_sb[1][:, HALF * h : HALF * (h + 1)], wgs_low[h][:], MULT)
        for h in range(2):
            cols = slice(HALF * h, HALF * (h + 1))
            nc.gpsimd.tensor_tensor(h_sb[1][:, cols], b_sb[1][:, cols], aw[h], MULT)
        nc.scalar.copy(stage4[:].rearrange("p (c j) -> p c j", j=4), w4_raw[:].rearrange("p j c -> p c j"))
        gather(x1[0][:], 0, idx3, 0, M)
        gather(x2[0][:], 0, idx4, 0, M)
        scatter(1)
        quantise(w4_w, w4_s, 0, stage4[:])
        gather(x1[1][:], 1, idx3, 0, M)
        gather(x2[1][:], 1, idx4, 0, M)
        weigh(2)
        low_difference(0)
        join(2)
        weigh(3)
        join(3)
        low_difference(1)
        nc.scalar.copy(d_cols[:, :, 0:4:2], d_low[:].rearrange("p i m -> p m i"))
        for t in (2, 3):
            scatter(t)

        act = at(TAB0, "act", [P, TILES * 4 * CHUNK], F32)
        res = sb("res", [P, TILES * 4 * CHUNK], F32)
        d_w = sb("d_w", [P, M], U32)
        d_s = sb("d_s", [P, M], U8)
        high = sb("high", [P, 12 * CHUNK], F32)
        x1_two = at(D_LOW + 64, "x1_two", [P, HALF], F32)
        x1_three = at(X1_HEAD, "x1_three", [P, HALF], F32)

        def pair(tile, c0, pitch=CHUNK):
            return [tile[:, c0 + pitch * i : c0 + pitch * i + CHUNK] for i in range(2)], tile[:, c0 : c0 + 2 * pitch].rearrange("p (i m) -> p i m", i=2)[:, :, 0:CHUNK]

        d_high = [pair(high, 0), pair(high, 2 * CHUNK), pair(high, 4 * CHUNK + P, HALF), pair(high, 9 * CHUNK)]
        acts = {(c, g): pair(act, CHUNK * (4 * c + 2 * g)) for c in range(4) for g in range(2)}
        sums = {(c, g): pair(res, CHUNK * (4 * c + 2 * g)) for c in range(4) for g in range(2)}
        sums[0, 1], sums[1, 0] = pair(high, 4 * CHUNK, HALF), pair(high, 5 * CHUNK, HALF)
        acts[1, 1] = d_high[3]
        x1_high = {2: [x1_two[:], high[:, 0:HALF]], 3: [x1_three[:], high[:, HALF : 2 * HALF]]}
        out_tiles = out.rearrange("(c p) m -> p c m", p=P)

        def high_difference(c, t):
            first = x1_high[t][c // 2][:, CHUNK * (c % 2) : CHUNK * (c % 2 + 1)]
            gather_difference(d_high[c][0][t - 2], t, CHUNK * c, CHUNK, first)

        def round_high(c):
            nc.scalar.copy(d_cols[:, CHUNK * c : CHUNK * (c + 1), 1:4:2], d_high[c][1].rearrange("p i m -> p m i"))

        def quantise_d(c):
            quantise(d_w, d_s, CHUNK * c, d_in[:, 4 * CHUNK * c : 4 * CHUNK * (c + 1)])

        def second_products(c, g):
            cols = slice(CHUNK * c, CHUNK * (c + 1))
            for codes, scales, bank in ((w3_w, w3_s, banks[4 * (c % 2) + g]), (w4_w, w4_s, banks[4 * (c % 2) + 2 + g])):
                for i in range(2):
                    n = 2 * g + i
                    mx(bank[:, CHUNK * i : CHUNK * (i + 1)], codes[:, P * n : P * (n + 1)].bitcast(FP8X4), scales[:, P * n : P * (n + 1)],
                       d_w[:, cols].bitcast(FP8X4), d_s[:, cols], True, True)
            nc.scalar.activation(acts[c, g][1], banks[4 * (c % 2) + g][:].rearrange("p (i m) -> p i m", i=2), GELU)

        def finish(c, g):
            for i in range(2):
                n = 2 * g + i
                nc.vector.scalar_tensor_tensor(sums[c, g][0][i], acts[c, g][0][i], gain_sb[:, n : n + 1],
                                               banks[4 * (c % 2) + 2 + g][:, CHUNK * i : CHUNK * (i + 1)], MULT, ADD)
            queue = nc.scalar if (c, g) == (3, 1) else nc.sync
            queue.dma_start(out_tiles[:, 2 * g : 2 * g + 2, CHUNK * c : CHUNK * (c + 1)], sums[c, g][1])

        for t in (2, 3):
            gather(x1_high[t][0], t, idx3, 0, HALF)
        for c in range(2):
            for t in (2, 3):
                high_difference(c, t)
            round_high(c)
        for c in range(2):
            gather(x1_high[2 + c][1], 2 + c, idx3, HALF, HALF)
            quantise_d(c)
            second_products(c, 0)
        second_products(0, 1)
        finish(0, 0)
        for c in (2, 3):
            for t in (2, 3):
                high_difference(c, t)
            round_high(c)
        finish(0, 1)
        for c in (2, 3):
            quantise_d(c)
        second_products(1, 1)
        for g in range(2):
            second_products(2, g)
        for g in range(2):
            finish(1, g)
            second_products(3, g)
        for c in (2, 3):
            for g in range(2):
                finish(c, g)
